import numpy as np
import ml_dtypes


def mxq(x, axis, fmt="e4m3"):
    dtype, down = {"e4m3": (ml_dtypes.float8_e4m3fn, 7), "e5m2": (ml_dtypes.float8_e5m2, 14)}[fmt]
    v = np.moveaxis(np.asarray(x, np.float32).astype(ml_dtypes.bfloat16).astype(np.float64), axis, -1)
    blocks = v.reshape(v.shape[:-1] + (-1, 32))
    amax = np.abs(blocks).max(-1, keepdims=True)
    byte = np.maximum(np.where(amax > 0, np.frexp(amax)[1] - 1 + 127, 0) - down, 1)
    scale = np.exp2(byte - 127.0)
    codes = (blocks / scale).astype(np.float32).astype(dtype).astype(np.float64)
    return np.moveaxis((codes * scale).reshape(v.shape), -1, axis)


WIDE = False


def mx_kscale(k):
    if not WIDE:
        return np.ones(k)
    levels = np.array([24, -24, 12, -12, 0])
    if k % 512:
        return np.exp2(np.random.permutation(np.resize(levels, k // 32))).repeat(32)
    a = np.empty((k // 512, 16))
    for p in range(k // 512):
        a[p, :8] = np.random.permutation(np.resize(levels, 8))
        for g in range(8):
            far = levels[np.abs(levels - a[p, g]) >= 10]
            a[p, g + 8] = far[np.random.randint(len(far))]
    return np.exp2(a.ravel()).repeat(32)


def f64(x):
    return np.asarray(x).astype(np.float64)


def striped(idx):
    return np.tile(idx.reshape(-1, 16).T, (8, 1)).astype(np.uint16)


def unstriped(offs):
    return offs[:16].T.reshape(-1).astype(np.int64)


E2M1 = np.array([0.0, 0.5, 1.0, 1.5, 2.0, 3.0, 4.0, 6.0, -0.0, -0.5, -1.0, -1.5, -2.0, -3.0, -4.0, -6.0])


def pack_weight(w, fmt):
    k, n = w.shape
    w = f64(np.asarray(w, np.float32).astype(ml_dtypes.bfloat16)).reshape(k // 32, 32, n)
    amax = np.abs(w).max(1)
    if fmt == "e4m3":
        byte = np.frexp(amax)[1] - 1 + 127 - 7
    else:
        mant, ex = np.frexp(amax / 6.0)
        byte = np.where(mant > 0.5, ex, ex - 1) + 127
    byte = np.clip(np.where(amax > 0, byte, 1), 1, 254)
    scaled = (w * np.exp2(127.0 - byte)[:, None, :]).reshape(k, n).astype(np.float32)
    by_word = np.ascontiguousarray(scaled.reshape(k // 512, 128, 4, n).transpose(0, 1, 3, 2))
    if fmt == "e4m3":
        words = by_word.astype(ml_dtypes.float8_e4m3fn).view(np.uint8)
    else:
        c = by_word.astype(ml_dtypes.float4_e2m1fn).view(np.uint8) & 0xF
        words = (c[..., 0::2] | (c[..., 1::2] << 4)).reshape(k // 512, 128, 2 * n)
    return np.ascontiguousarray(words), np.ascontiguousarray(byte.astype(np.uint8).reshape(k // 512, 16, n))


def unpack_weight(words, scales, fmt):
    g, _, n = scales.shape
    words = np.ascontiguousarray(words).reshape(g, 128, n, -1)
    if fmt == "e4m3":
        vals = words.view(ml_dtypes.float8_e4m3fn).astype(np.float64)
    else:
        nib = np.empty((g, 128, n, 4), np.uint8)
        nib[..., 0::2] = words & 0xF
        nib[..., 1::2] = words >> 4
        vals = E2M1[nib]
    vals = vals * np.repeat(np.exp2(scales.astype(np.float64) - 127.0), 8, axis=1)[..., None]
    return vals.transpose(0, 1, 3, 2).reshape(g * 512, n)


def pack_table4(v):
    words, scales = pack_weight(v, "e2m1")
    g, t = words.shape[0] // 2, v.shape[1]
    return np.ascontiguousarray(words.reshape(g, 2, 128, t, 2).transpose(0, 2, 3, 1, 4).reshape(g, 128, t, 4)), scales


def unpack_table4(words, scales):
    g, _, t, _ = words.shape
    return unpack_weight(words.reshape(g, 128, t, 2, 2).transpose(0, 3, 1, 2, 4).reshape(2 * g, 128, 2 * t), scales, "e2m1")


K, L, R, N, T, J = 512, 1024, 512, 512, 4096, 2048


def setup_inputs():
    n = np.random.standard_normal
    s = mx_kscale(K)[:, None]
    s2 = mx_kscale(L)[:, None]
    u = mx_kscale(R)[:, None]
    p_tab = pack_weight(n((K, T)) * s, "e4m3")
    p_tab2 = pack_table4(n((L, T)) * s2)
    p_wrr = pack_weight(n((L, R)) / np.sqrt(L) / s2, "e4m3")
    p_wri = pack_weight(n((L, R)) / np.sqrt(L) / s2, "e4m3")
    p_nr = pack_weight(n((R, N)) / np.sqrt(R) / u, "e2m1")
    p_ni = pack_weight(n((R, N)) / np.sqrt(R) / u, "e2m1")
    return {
        "tab_words": p_tab[0],
        "tab_scales": p_tab[1],
        "tab2_words": p_tab2[0],
        "tab2_scales": p_tab2[1],
        "wer": (n((K, R)) / np.sqrt(K) / s * u.T).astype(np.float32),
        "wei": (n((K, R)) / np.sqrt(K) / s * u.T).astype(np.float32),
        "wrr_words": p_wrr[0],
        "wrr_scales": p_wrr[1],
        "wri_words": p_wri[0],
        "wri_scales": p_wri[1],
        "nr_words": p_nr[0],
        "nr_scales": p_nr[1],
        "ni_words": p_ni[0],
        "ni_scales": p_ni[1],
        "b": (0.3 * n(N)).astype(np.float32),
        "offs": striped(np.random.permutation(T)[:J]),
        "offs2": striped(np.random.permutation(T)[:J]),
    }


def reference(tab_words, tab_scales, tab2_words, tab2_scales, wer, wei, wrr_words, wrr_scales, wri_words, wri_scales, nr_words, nr_scales, ni_words, ni_scales, b, offs, offs2):
    idx = unstriped(offs)
    idx2 = unstriped(offs2)
    tab_ = unpack_weight(tab_words, tab_scales, "e4m3")[:, idx]
    tab2_ = unpack_table4(tab2_words, tab2_scales)[:, idx2]
    wer_ = mxq(f64(wer), 0, "e4m3")
    aer = wer_.T @ tab_
    wei_ = mxq(f64(wei), 0, "e4m3")
    aei = wei_.T @ tab_
    wrr_ = unpack_weight(wrr_words, wrr_scales, "e4m3")
    arr = wrr_.T @ tab2_
    wri_ = unpack_weight(wri_words, wri_scales, "e4m3")
    ari = wri_.T @ tab2_
    hr = aer * arr - aei * ari
    hi = aer * ari + aei * arr
    hr_ = mxq(hr, 0, "e4m3")
    hi_ = mxq(hi, 0, "e4m3")
    nr_ = unpack_weight(nr_words, nr_scales, "e2m1")
    ni_ = unpack_weight(ni_words, ni_scales, "e2m1")
    y = nr_.T @ hr_ + ni_.T @ hi_
    return y + f64(b)[:, None]

@@ -1,0 +1,271 @@
+from contextlib import ExitStack
+
+import concourse.mybir as mybir
+
+K, L, R, N, T, J = 512, 1024, 512, 512, 4096, 2048
+FLOPS = 2 * J * (2 * K * R + 2 * L * R + 2 * R * N)
+
+F32 = mybir.dt.float32
+BF16 = mybir.dt.bfloat16
+I32 = mybir.dt.int32
+U32 = mybir.dt.uint32
+U16 = mybir.dt.uint16
+U8 = mybir.dt.uint8
+FP8X4 = mybir.dt.float8_e4m3fn_x4
+FP4X4 = mybir.dt.float4_e2m1fn_x4
+MULT = mybir.AluOpType.mult
+ADD = mybir.AluOpType.add
+IDENTITY = mybir.ActivationFunctionType.Identity
+
+P = 128
+PACK = 4
+TOK = 128
+CHUNK = 512
+N_CHUNKS = J // CHUNK
+N_TILES = J // TOK
+GROUPS = [4, 4, 4, 1, 1, 1, 1]
+
+
+def tile_list_ckg_bias_kernel(
+    tc, tab_words, tab_scales, tab2_words, tab2_scales, wer, wei, wrr_words, wrr_scales, wri_words, wri_scales,
+    nr_words, nr_scales, ni_words, ni_scales, b, offs, offs2, out,
+):
+    nc = tc.nc
+    with ExitStack() as ctx:
+        keep = ctx.enter_context(tc.tile_pool(name="keep", bufs=1))
+        ring = ctx.enter_context(tc.tile_pool(name="ring", bufs=3))
+        psum = ctx.enter_context(tc.psum_pool(name="psum", bufs=1))
+
+        list1 = keep.tile([P, J // 16], U16, name="list1")
+        list2 = keep.tile([P, J // 16], U16, name="list2")
+        v_words = keep.tile([P, T], I32, name="v_words", align_bytes=64)
+        v2_words = keep.tile([P, T], I32, name="v2_words", align_bytes=64)
+        v_plane = keep.tile([P, T // 4], I32, name="v_plane", align_bytes=64)
+        v2_planes = keep.tile([P, T // 4], I32, name="v2_planes", align_bytes=64)
+        wr_raw = keep.tile([P, 2, 2 * R], I32, name="wr_raw", align_bytes=64)
+        wr_raw_plane = keep.tile([P, 2, 2, R // 4], I32, name="wr_raw_plane", align_bytes=64)
+        n_words = keep.tile([P, 2, N // 2], I32, name="n_words", align_bytes=64)
+        n_plane = keep.tile([P, 2, N // 4], I32, name="n_plane", align_bytes=64)
+        g2_pass1 = keep.tile([P, J // 4], I32, name="g2_pass1", align_bytes=64)
+        we_raw = [keep.tile([P, PACK, R], F32, name=f"we_raw{w}") for w in range(2)]
+        bias = keep.tile([P, N // P], F32, name="bias")
+
+        for plane in (v2_planes, v_plane, wr_raw_plane, n_plane, g2_pass1):
+            nc.vector.memset(plane[:], 0)
+
+        nc.sync.dma_start(list2[:], offs2)
+        for q in range(4):
+            nc.sync.dma_start(v2_planes[32 * q : 32 * q + 8, :], tab2_scales[:, 4 * q : 4 * q + 4, :].bitcast(I32))
+        nc.sync.dma_start(list1[:], offs)
+        for q in range(4):
+            nc.sync.dma_start(v_plane[32 * q : 32 * q + 4, :], tab_scales[0, 4 * q : 4 * q + 4, :].bitcast(I32))
+        for w, src in enumerate((wer, wei)):
+            nc.sync.dma_start(we_raw[w][:], src.rearrange("(p i) r -> p i r", i=PACK))
+        for w, src in enumerate((wrr_words, wri_words)):
+            nc.sync.dma_start(
+                wr_raw[:, w, :].rearrange("p (a r) -> p a r", a=2), src.rearrange("a p r i -> p a (r i)").bitcast(I32)
+            )
+        nc.sync.dma_start(v2_words[:], tab2_words[0].rearrange("p t i -> p (t i)").bitcast(I32))
+        nc.sync.dma_start(v_words[:], tab_words[0].rearrange("p t i -> p (t i)").bitcast(I32))
+        for w, src in enumerate((nr_words, ni_words)):
+            nc.sync.dma_start(n_words[:, w, :], src[0].bitcast(I32))
+        with nc.allow_non_contiguous_dma(reason="one bias value to a partition"):
+            nc.sync.dma_start(bias[:], b.rearrange("(q p) -> p q", p=P))
+        for w, src in enumerate((wrr_scales, wri_scales)):
+            for q in range(4):
+                nc.gpsimd.dma_start(
+                    wr_raw_plane[32 * q : 32 * q + 4, w, :, :],
+                    src[:, 4 * q : 4 * q + 4, :].rearrange("a q r -> q a r").bitcast(I32),
+                )
+        for w, src in enumerate((nr_scales, ni_scales)):
+            for q in range(4):
+                nc.sync.dma_start(n_plane[32 * q : 32 * q + 4, w, :], src[0, 4 * q : 4 * q + 4, :].bitcast(I32))
+
+        def cols(lst, c):
+            return lst[:, c * (CHUNK // 16) : (c + 1) * (CHUNK // 16)]
+
+        g2_planes = keep.tile([P, J], U8, name="g2_planes", align_bytes=64)
+        nc.vector.tensor_copy(g2_planes[:], v2_planes[:].bitcast(U8).indirect(list2[:]))
+        for q in range(4):
+            nc.gpsimd.dma_start(g2_pass1[32 * q : 32 * q + 4, :], g2_planes[32 * q + 4 : 32 * q + 8, :].bitcast(I32))
+
+        g_plane = [keep.tile([P, CHUNK], U8, name=f"g_plane{c}", align_bytes=64) for c in range(N_CHUNKS)]
+        for c in range(N_CHUNKS):
+            nc.vector.tensor_copy(g_plane[c][:], v_plane[:].bitcast(U8).indirect(cols(list1, c)))
+
+        we_bf = [keep.tile([P, PACK * R], BF16, name=f"we_bf{w}", align_bytes=64) for w in range(2)]
+        for w in range(2):
+            nc.scalar.copy(
+                we_bf[w][:].rearrange("p (t m i) -> p m i t", t=PACK, i=PACK),
+                we_raw[w][:].rearrange("p i (m t) -> p m i t", t=PACK),
+            )
+
+        wr_words = keep.tile([P, 2, PACK, 2 * P], I32, name="wr_words", align_bytes=64)
+        for w in range(2):
+            nc.vector.tensor_copy(
+                wr_words[:, w, :, :].rearrange("p t (g m) -> p g t m", m=4),
+                wr_raw[:, w, :].rearrange("p (g m t) -> p g t m", m=4, t=PACK),
+            )
+        wr_plane = keep.tile([P, 2, PACK, 2 * P], U8, name="wr_plane", align_bytes=64)
+        for w in range(2):
+            nc.vector.tensor_copy(
+                wr_plane[:, w, :, :],
+                wr_raw_plane[:, w, :, :].rearrange("p a r -> p (a r)").bitcast(U8).rearrange("p (m t) -> p t m", t=PACK),
+            )
+
+        we_words = [keep.tile([P, R], U32, name=f"we_words{w}", align_bytes=64) for w in range(2)]
+        we_plane = [keep.tile([P, R], U8, name=f"we_plane{w}", align_bytes=64) for w in range(2)]
+        for w in range(2):
+            nc.vector.quantize_mx(out=we_words[w][:].bitcast(FP8X4), scales=we_plane[w][:], in_=we_bf[w][:])
+
+        g_words = [keep.tile([P, CHUNK], U32, name=f"g_words{c}", align_bytes=64) for c in range(N_CHUNKS)]
+        g2_pairs = [keep.tile([P, CHUNK], U32, name=f"g2_pairs{c}", align_bytes=64) for c in range(N_CHUNKS)]
+        g2_words = [keep.tile([P, 2, 2 * CHUNK], U8, name=f"g2_words{c}", align_bytes=64) for c in range(N_CHUNKS)]
+
+        def gather_v(c):
+            nc.vector.tensor_copy(g_words[c][:], v_words[:].bitcast(U32).indirect(cols(list1, c)))
+
+        def gather_v2(c):
+            nc.vector.tensor_copy(g2_pairs[c][:], v2_words[:].bitcast(U32).indirect(cols(list2, c)))
+
+        def part_v2(c):
+            nc.vector.tensor_copy(
+                g2_words[c][:].bitcast(U16), g2_pairs[c][:].bitcast(U16).rearrange("p (n d) -> p d n", d=2)
+            )
+
+        def products(i):
+            c, u = divmod(i, CHUNK // TOK)
+            tok = slice(u * TOK, (u + 1) * TOK)
+            cd = ring.tile([P, 2, TOK, PACK], F32, name="cd")
+            for w in range(2):
+                bank = psum.tile([P, PACK, TOK], F32, name=f"rel{w}")
+                for t in range(PACK):
+                    for a in range(2):
+                        plane = g2_planes[:] if a == 0 else g2_pass1[:].bitcast(U8)
+                        nc.tensor.matmul_mx(
+                            out=bank[:, t, :],
+                            lhsT=wr_words[:, w, t, a * P : (a + 1) * P].bitcast(FP8X4),
+                            lhsT_scale=wr_plane[:, w, t, a * P : (a + 1) * P],
+                            rhs=g2_words[c][:, a, 2 * u * TOK : 2 * (u + 1) * TOK].bitcast(FP4X4),
+                            rhs_scale=plane[:, i * TOK : (i + 1) * TOK],
+                            start=(a == 0),
+                            stop=(a == 1),
+                        )
+                nc.scalar.copy(cd[:, w, :, :], bank[:].rearrange("p t n -> p n t"))
+            ent = []
+            for w in range(2):
+                bank = psum.tile([P, PACK, TOK], F32, name=f"ent{w}", bufs=2)
+                for t in range(PACK):
+                    nc.tensor.matmul_mx(
+                        out=bank[:, t, :],
+                        lhsT=we_words[w][:, t * P : (t + 1) * P].bitcast(FP8X4),
+                        lhsT_scale=we_plane[w][:, t * P : (t + 1) * P],
+                        rhs=g_words[c][:, tok].bitcast(FP8X4),
+                        rhs_scale=g_plane[c][:, tok],
+                        start=True,
+                        stop=True,
+                    )
+                ent.append(bank[:].rearrange("p t n -> p n t"))
+            first = ring.tile([P, 2, TOK, PACK], F32, name="first")
+            second = ring.tile([P, 2, TOK, PACK], F32, name="second")
+            nc.vector.tensor_tensor(first[:, 0, :, :], ent[0], cd[:, 0, :, :], MULT)
+            nc.vector.tensor_tensor(first[:, 1, :, :], ent[0], cd[:, 1, :, :], MULT)
+            nc.vector.scalar_tensor_tensor(second[:, 0, :, :], ent[1], -1.0, cd[:, 1, :, :], MULT, MULT)
+            nc.vector.tensor_tensor(second[:, 1, :, :], ent[1], cd[:, 0, :, :], MULT)
+            return first, second
+
+        starts = [sum(GROUPS[:g]) for g in range(len(GROUPS))]
+        group_of = [g for g, n in enumerate(GROUPS) for u in range(n)]
+        h_bf = {}
+        h_mx = {}
+
+        def add_up(i, first, second):
+            g = group_of[i]
+            u = i - starts[g]
+            if u == 0:
+                h_bf[g] = ring.tile([P, 2, GROUPS[g] * TOK * PACK], BF16, name="h_bf", align_bytes=64)
+            engine = nc.vector if i == N_TILES - 1 else nc.gpsimd
+            engine.tensor_tensor(
+                h_bf[g][:, :, u * TOK * PACK : (u + 1) * TOK * PACK],
+                first[:].rearrange("p w n t -> p w (n t)"),
+                second[:].rearrange("p w n t -> p w (n t)"),
+                ADD,
+            )
+
+        def quantise(g):
+            width = GROUPS[g] * TOK
+            words = ring.tile([P, 2 * width], U32, name="h_words", align_bytes=64)
+            plane = ring.tile([P, 2 * width], U8, name="h_plane", align_bytes=64)
+            nc.vector.quantize_mx(
+                out=words[:].bitcast(FP8X4), scales=plane[:], in_=h_bf[g][:].rearrange("p w x -> p (w x)")
+            )
+            h_mx[g] = (words, plane)
+
+        def score(g, q, bank, staged):
+            width = GROUPS[g] * TOK
+            words, plane = h_mx[g]
+            for w in range(2):
+                nc.tensor.matmul_mx(
+                    out=bank,
+                    lhsT=n_words[:, w, q * 64 : (q + 1) * 64].bitcast(FP4X4),
+                    lhsT_scale=n_plane[:, w, :].bitcast(U8)[:, q * P : (q + 1) * P],
+                    rhs=words[:, w * width : (w + 1) * width].bitcast(FP8X4),
+                    rhs_scale=plane[:, w * width : (w + 1) * width],
+                    start=(w == 0),
+                    stop=(w == 1),
+                )
+
+        def score_wide(g, q):
+            bank = psum.tile([P, CHUNK], F32, name="score", bufs=2)
+            staged = ring.tile([P, CHUNK], F32, name="staged")
+            score(g, q, bank[:], staged)
+            nc.scalar.activation(staged[:], bank[:], IDENTITY, bias=bias[:, q : q + 1])
+            nc.sync.dma_start(out[q * P : (q + 1) * P, starts[g] * TOK : starts[g] * TOK + CHUNK], staged[:])
+
+        def score_narrow(g):
+            bank = psum.tile([P, CHUNK], F32, name="score", bufs=2)
+            staged = ring.tile([P, CHUNK], F32, name="staged")
+            for q in range(4):
+                score(g, q, bank[:, q * TOK : (q + 1) * TOK], staged)
+            for q in range(4):
+                nc.scalar.activation(
+                    staged[:, q * TOK : (q + 1) * TOK], bank[:, q * TOK : (q + 1) * TOK], IDENTITY, bias=bias[:, q : q + 1]
+                )
+            nc.sync.dma_start(
+                out[:, starts[g] * TOK : (starts[g] + 1) * TOK].rearrange("(q p) j -> p q j", p=P),
+                staged[:].rearrange("p (q j) -> p q j", q=4),
+            )
+
+        gather_v2(0)
+        gather_v2(1)
+        part_v2(0)
+        gather_v2(2)
+        part_v2(1)
+        gather_v(0)
+        part_v2(2)
+        gather_v2(3)
+        part_v2(3)
+
+        pending = []
+        for i in range(N_TILES + 2):
+            if i < N_TILES:
+                first, second = products(i)
+            done = i - 2
+            if done >= 0 and done + 1 - starts[group_of[done]] == GROUPS[group_of[done]]:
+                g = group_of[done]
+                quantise(g)
+                if GROUPS[g] == 1:
+                    pending.append((g, None))
+                else:
+                    pending.extend((g, q) for q in range(4))
+            if i < N_TILES:
+                add_up(i, first, second)
+            if i % 4 == 0 and i // 4 + 1 < N_CHUNKS:
+                gather_v(i // 4 + 1)
+            take = len(pending) if i >= N_TILES - 3 else min(1, len(pending))
+            for g, q in pending[:take]:
+                if q is None:
+                    score_narrow(g)
+                else:
+                    score_wide(g, q)
+            pending = pending[take:]

@@ -36,94 +36,44 @@ def tile_list_ckg_bias_kernel(
         ring = ctx.enter_context(tc.tile_pool(name="ring", bufs=3))
         psum = ctx.enter_context(tc.psum_pool(name="psum", bufs=1))
 
-        list1 = keep.tile([P, J // 16], U16, name="list1")
-        list2 = keep.tile([P, J // 16], U16, name="list2")
-        v_words = keep.tile([P, T], I32, name="v_words", align_bytes=64)
-        v2_words = keep.tile([P, T], I32, name="v2_words", align_bytes=64)
-        v_plane = keep.tile([P, T // 4], I32, name="v_plane", align_bytes=64)
-        v2_planes = keep.tile([P, T // 4], I32, name="v2_planes", align_bytes=64)
-        wr_raw = keep.tile([P, 2, 2 * R], I32, name="wr_raw", align_bytes=64)
-        wr_raw_plane = keep.tile([P, 2, 2, R // 4], I32, name="wr_raw_plane", align_bytes=64)
-        n_words = keep.tile([P, 2, N // 2], I32, name="n_words", align_bytes=64)
-        n_plane = keep.tile([P, 2, N // 4], I32, name="n_plane", align_bytes=64)
-        g2_pass1 = keep.tile([P, J // 4], I32, name="g2_pass1", align_bytes=64)
-        we_raw = [keep.tile([P, PACK, R], F32, name=f"we_raw{w}") for w in range(2)]
-        bias = keep.tile([P, N // P], F32, name="bias")
-
-        for plane in (v2_planes, v_plane, wr_raw_plane, n_plane, g2_pass1):
-            nc.vector.memset(plane[:], 0)
-
-        nc.sync.dma_start(list2[:], offs2)
-        for q in range(4):
-            nc.sync.dma_start(v2_planes[32 * q : 32 * q + 8, :], tab2_scales[:, 4 * q : 4 * q + 4, :].bitcast(I32))
-        nc.sync.dma_start(list1[:], offs)
-        for q in range(4):
-            nc.sync.dma_start(v_plane[32 * q : 32 * q + 4, :], tab_scales[0, 4 * q : 4 * q + 4, :].bitcast(I32))
-        for w, src in enumerate((wer, wei)):
-            nc.sync.dma_start(we_raw[w][:], src.rearrange("(p i) r -> p i r", i=PACK))
-        for w, src in enumerate((wrr_words, wri_words)):
-            nc.sync.dma_start(
-                wr_raw[:, w, :].rearrange("p (a r) -> p a r", a=2), src.rearrange("a p r i -> p a (r i)").bitcast(I32)
-            )
-        nc.sync.dma_start(v2_words[:], tab2_words[0].rearrange("p t i -> p (t i)").bitcast(I32))
-        nc.sync.dma_start(v_words[:], tab_words[0].rearrange("p t i -> p (t i)").bitcast(I32))
-        for w, src in enumerate((nr_words, ni_words)):
-            nc.sync.dma_start(n_words[:, w, :], src[0].bitcast(I32))
-        with nc.allow_non_contiguous_dma(reason="one bias value to a partition"):
-            nc.sync.dma_start(bias[:], b.rearrange("(q p) -> p q", p=P))
-        for w, src in enumerate((wrr_scales, wri_scales)):
-            for q in range(4):
-                nc.gpsimd.dma_start(
-                    wr_raw_plane[32 * q : 32 * q + 4, w, :, :],
-                    src[:, 4 * q : 4 * q + 4, :].rearrange("a q r -> q a r").bitcast(I32),
-                )
-        for w, src in enumerate((nr_scales, ni_scales)):
-            for q in range(4):
-                nc.sync.dma_start(n_plane[32 * q : 32 * q + 4, w, :], src[0, 4 * q : 4 * q + 4, :].bitcast(I32))
+        def held(shape, dtype, name, tag=None):
+            return keep.tile(shape, dtype, name=name, tag=tag or name, align_bytes=64)
 
         def cols(lst, c):
             return lst[:, c * (CHUNK // 16) : (c + 1) * (CHUNK // 16)]
 
-        g2_planes = keep.tile([P, J], U8, name="g2_planes", align_bytes=64)
-        nc.vector.tensor_copy(g2_planes[:], v2_planes[:].bitcast(U8).indirect(list2[:]))
-        for q in range(4):
-            nc.gpsimd.dma_start(g2_pass1[32 * q : 32 * q + 4, :], g2_planes[32 * q + 4 : 32 * q + 8, :].bitcast(I32))
+        list1 = keep.tile([P, J // 16], U16, name="list1")
+        list2 = keep.tile([P, J // 16], U16, name="list2")
+        v_rows = held([P, T // 4], I32, "v_rows", "slot_a")
+        v2_planes = held([P, T // 4], I32, "v2_planes", "slot_b")
+        wr_raw = held([P, 2, 2 * R], I32, "wr_raw")
+        wr_raw_plane = held([P, 2, 2, R // 4], I32, "wr_raw_plane")
+        g_plane = held([P, J // 4], I32, "g_plane")
+        g2_pass1 = held([P, J // 4], I32, "g2_pass1")
+        for plane in (v2_planes, wr_raw_plane, g_plane, g2_pass1):
+            nc.vector.memset(plane[:], 0)
 
-        g_plane = [keep.tile([P, CHUNK], U8, name=f"g_plane{c}", align_bytes=64) for c in range(N_CHUNKS)]
-        for c in range(N_CHUNKS):
-            nc.vector.tensor_copy(g_plane[c][:], v_plane[:].bitcast(U8).indirect(cols(list1, c)))
-
-        we_bf = [keep.tile([P, PACK * R], BF16, name=f"we_bf{w}", align_bytes=64) for w in range(2)]
-        for w in range(2):
-            nc.scalar.copy(
-                we_bf[w][:].rearrange("p (t m i) -> p m i t", t=PACK, i=PACK),
-                we_raw[w][:].rearrange("p i (m t) -> p m i t", t=PACK),
+        nc.sync.dma_start(list1[:], offs)
+        nc.sync.dma_start(v_rows[:], tab_scales[0].bitcast(I32).unsqueeze(1).to_broadcast([16, 8, T // 4]))
+        nc.sync.dma_start(list2[:], offs2)
+        for w, src in enumerate((wrr_words, wri_words)):
+            nc.sync.dma_start(
+                wr_raw[:, w, :].rearrange("p (a r) -> p a r", a=2), src.rearrange("a p r i -> p a (r i)").bitcast(I32)
             )
-
-        wr_words = keep.tile([P, 2, PACK, 2 * P], I32, name="wr_words", align_bytes=64)
-        for w in range(2):
-            nc.vector.tensor_copy(
-                wr_words[:, w, :, :].rearrange("p t (g m) -> p g t m", m=4),
-                wr_raw[:, w, :].rearrange("p (g m t) -> p g t m", m=4, t=PACK),
+        for r in range(4):
+            nc.sync.dma_start(
+                v2_planes[r:P:16, :], tab2_scales.rearrange("a (q r) t -> r q a t", r=4)[r].bitcast(I32)
             )
-        wr_plane = keep.tile([P, 2, PACK, 2 * P], U8, name="wr_plane", align_bytes=64)
-        for w in range(2):
-            nc.vector.tensor_copy(
-                wr_plane[:, w, :, :],
-                wr_raw_plane[:, w, :, :].rearrange("p a r -> p (a r)").bitcast(U8).rearrange("p (m t) -> p t m", t=PACK),
-            )
+        for w, src in enumerate((wrr_scales, wri_scales)):
+            for q in range(4):
+                nc.sync.dma_start(
+                    wr_raw_plane[32 * q : 32 * q + 4, w, :, :],
+                    src[:, 4 * q : 4 * q + 4, :].rearrange("a q r -> q a r").bitcast(I32),
+                )
 
-        we_words = [keep.tile([P, R], U32, name=f"we_words{w}", align_bytes=64) for w in range(2)]
-        we_plane = [keep.tile([P, R], U8, name=f"we_plane{w}", align_bytes=64) for w in range(2)]
-        for w in range(2):
-            nc.vector.quantize_mx(out=we_words[w][:].bitcast(FP8X4), scales=we_plane[w][:], in_=we_bf[w][:])
-
-        g_words = [keep.tile([P, CHUNK], U32, name=f"g_words{c}", align_bytes=64) for c in range(N_CHUNKS)]
-        g2_pairs = [keep.tile([P, CHUNK], U32, name=f"g2_pairs{c}", align_bytes=64) for c in range(N_CHUNKS)]
-        g2_words = [keep.tile([P, 2, 2 * CHUNK], U8, name=f"g2_words{c}", align_bytes=64) for c in range(N_CHUNKS)]
-
-        def gather_v(c):
-            nc.vector.tensor_copy(g_words[c][:], v_words[:].bitcast(U32).indirect(cols(list1, c)))
+        g_words = [held([P, CHUNK], U32, f"g_words{c}") for c in range(N_CHUNKS)]
+        g2_pairs = [held([P, CHUNK], U32, f"g2_pairs{c}") for c in range(N_CHUNKS)]
+        g2_words = [held([P, 2, 2 * CHUNK], U8, f"g2_words{c}") for c in range(N_CHUNKS)]
 
         def gather_v2(c):
             nc.vector.tensor_copy(g2_pairs[c][:], v2_words[:].bitcast(U32).indirect(cols(list2, c)))
@@ -133,10 +83,54 @@ def tile_list_ckg_bias_kernel(
                 g2_words[c][:].bitcast(U16), g2_pairs[c][:].bitcast(U16).rearrange("p (n d) -> p d n", d=2)
             )
 
+        g_rows = held([P, J], U8, "g_rows", "slot_c")
+        nc.vector.tensor_copy(g_rows[:], v_rows[:].bitcast(U8).indirect(list1[:]))
+        v2_words = held([P, T], I32, "v2_words", "slot_a")
+        for q in range(4):
+            nc.sync.dma_start(g_plane[32 * q : 32 * q + 4, :], g_rows[32 * q : 32 * q + 32 : 8, :].bitcast(I32))
+        nc.sync.dma_start(v2_words[:], tab2_words[0].rearrange("p t i -> p (t i)").bitcast(I32))
+        we_raw = held([P, 2, PACK, R], F32, "we_raw", "slot_c")
+        for w, src in enumerate((wer, wei)):
+            nc.sync.dma_start(we_raw[:, w, :, :], src.rearrange("(p i) r -> p i r", i=PACK))
+
+        g2_planes = held([P, J], U8, "g2_planes")
+        nc.vector.tensor_copy(g2_planes[:], v2_planes[:].bitcast(U8).indirect(list2[:]))
+        for q in range(4):
+            nc.sync.dma_start(g2_pass1[32 * q : 32 * q + 4, :], g2_planes[32 * q + 16 : 32 * q + 20, :].bitcast(I32))
+        v_words = held([P, T], I32, "v_words", "slot_b")
+        nc.sync.dma_start(v_words[:], tab_words[0].rearrange("p t i -> p (t i)").bitcast(I32))
+
+        def gather_v(c):
+            nc.vector.tensor_copy(g_words[c][:], v_words[:].bitcast(U32).indirect(cols(list1, c)))
+
+        wr_plane = held([P, 2, PACK, 2 * P], U8, "wr_plane")
+        wr_words = held([P, 2, PACK, 2 * P], I32, "wr_words")
+        for w in range(2):
+            nc.vector.tensor_copy(
+                wr_plane[:, w, :, :],
+                wr_raw_plane[:, w, :, :].rearrange("p a r -> p (a r)").bitcast(U8).rearrange("p (m t) -> p t m", t=PACK),
+            )
+            nc.vector.tensor_copy(
+                wr_words[:, w, :, :].rearrange("p t (g m) -> p g t m", m=4),
+                wr_raw[:, w, :].rearrange("p (g m t) -> p g t m", m=4, t=PACK),
+            )
+
+        we_bf = [held([P, PACK * R], BF16, f"we_bf{w}") for w in range(2)]
+        for w in range(2):
+            nc.scalar.copy(
+                we_bf[w][:].rearrange("p (t m i) -> p m i t", t=PACK, i=PACK),
+                we_raw[:, w, :, :].rearrange("p i (m t) -> p m i t", t=PACK),
+            )
+        we_words = [held([P, R], U32, f"we_words{w}") for w in range(2)]
+        we_plane = [held([P, R], U8, f"we_plane{w}") for w in range(2)]
+
+        def quantise_we(w):
+            nc.vector.quantize_mx(out=we_words[w][:].bitcast(FP8X4), scales=we_plane[w][:], in_=we_bf[w][:])
+
         def products(i):
             c, u = divmod(i, CHUNK // TOK)
             tok = slice(u * TOK, (u + 1) * TOK)
-            cd = ring.tile([P, 2, TOK, PACK], F32, name="cd")
+            cd = ring.tile([P, 2, TOK, PACK], F32, name="cd", bufs=6)
             for w in range(2):
                 bank = psum.tile([P, PACK, TOK], F32, name=f"rel{w}")
                 for t in range(PACK):
@@ -161,7 +155,7 @@ def tile_list_ckg_bias_kernel(
                         lhsT=we_words[w][:, t * P : (t + 1) * P].bitcast(FP8X4),
                         lhsT_scale=we_plane[w][:, t * P : (t + 1) * P],
                         rhs=g_words[c][:, tok].bitcast(FP8X4),
-                        rhs_scale=g_plane[c][:, tok],
+                        rhs_scale=g_plane[:].bitcast(U8)[:, i * TOK : (i + 1) * TOK],
                         start=True,
                         stop=True,
                     )
@@ -217,14 +211,14 @@ def tile_list_ckg_bias_kernel(
 
         def score_wide(g, q):
             bank = psum.tile([P, CHUNK], F32, name="score", bufs=2)
-            staged = ring.tile([P, CHUNK], F32, name="staged")
+            staged = ring.tile([P, CHUNK], F32, name="staged", bufs=4)
             score(g, q, bank[:], staged)
             nc.scalar.activation(staged[:], bank[:], IDENTITY, bias=bias[:, q : q + 1])
             nc.sync.dma_start(out[q * P : (q + 1) * P, starts[g] * TOK : starts[g] * TOK + CHUNK], staged[:])
 
         def score_narrow(g):
             bank = psum.tile([P, CHUNK], F32, name="score", bufs=2)
-            staged = ring.tile([P, CHUNK], F32, name="staged")
+            staged = ring.tile([P, CHUNK], F32, name="staged", bufs=4)
             for q in range(4):
                 score(g, q, bank[:, q * TOK : (q + 1) * TOK], staged)
             for q in range(4):
@@ -236,32 +230,59 @@ def tile_list_ckg_bias_kernel(
                 staged[:].rearrange("p (q j) -> p q j", q=4),
             )
 
-        gather_v2(0)
-        gather_v2(1)
-        part_v2(0)
-        gather_v2(2)
-        part_v2(1)
+        for c in range(N_CHUNKS):
+            gather_v2(c)
+            if c > 0:
+                part_v2(c - 1)
+        quantise_we(0)
+        part_v2(N_CHUNKS - 1)
+        quantise_we(1)
         gather_v(0)
-        part_v2(2)
-        gather_v2(3)
-        part_v2(3)
+        gather_v(1)
+
+        n_words = held([P, 2, N // 2], I32, "n_words", "slot_c")
+        for w, src in enumerate((nr_words, ni_words)):
+            nc.sync.dma_start(n_words[:, w, :], src[0].bitcast(I32))
+        n_plane = held([P, 2, N // 4], I32, "n_plane", "we_bf0")
+        nc.gpsimd.memset(n_plane[:], 0)
+        for w, src in enumerate((nr_scales, ni_scales)):
+            for q in range(4):
+                nc.sync.dma_start(n_plane[32 * q : 32 * q + 4, w, :], src[0, 4 * q : 4 * q + 4, :].bitcast(I32))
+        bias = held([P, N // P], F32, "bias", "we_bf1")
+        with nc.allow_non_contiguous_dma(reason="one bias value to a partition"):
+            nc.sync.dma_start(bias[:], b.rearrange("(q p) -> p q", p=P))
+
+        def score_last(g):
+            for half in range(2):
+                bank = psum.tile([P, CHUNK], F32, name=f"rel{half}")
+                staged = ring.tile([P, CHUNK], F32, name="staged", bufs=4)
+                for u in range(2):
+                    score(g, 2 * half + u, bank[:, u * TOK : (u + 1) * TOK], staged)
+                for u in range(2):
+                    q = 2 * half + u
+                    span = slice(u * TOK, (u + 1) * TOK)
+                    if half == 0:
+                        nc.scalar.activation(staged[:, span], bank[:, span], IDENTITY, bias=bias[:, q : q + 1])
+                    else:
+                        nc.vector.tensor_scalar(staged[:, span], bank[:, span], bias[:, q : q + 1], None, ADD)
+                nc.sync.dma_start(
+                    out[2 * half * P : 2 * (half + 1) * P, starts[g] * TOK : (starts[g] + 1) * TOK].rearrange(
+                        "(q p) j -> p q j", p=P
+                    ),
+                    staged[:, 0 : 2 * TOK].rearrange("p (q j) -> p q j", q=2),
+                )
 
         pending = []
-        for i in range(N_TILES + 2):
-            if i < N_TILES:
-                first, second = products(i)
-            done = i - 2
-            if done >= 0 and done + 1 - starts[group_of[done]] == GROUPS[group_of[done]]:
+        for i in range(N_TILES):
+            first, second = products(i)
+            for done in range(max(i - 2, 0), i - 1 if i < N_TILES - 1 else i):
                 g = group_of[done]
-                quantise(g)
-                if GROUPS[g] == 1:
-                    pending.append((g, None))
-                else:
-                    pending.extend((g, q) for q in range(4))
-            if i < N_TILES:
-                add_up(i, first, second)
-            if i % 4 == 0 and i // 4 + 1 < N_CHUNKS:
-                gather_v(i // 4 + 1)
+                if done + 1 - starts[g] == GROUPS[g]:
+                    quantise(g)
+                    pending.extend([(g, None)] if GROUPS[g] == 1 else [(g, q) for q in range(4)])
+            add_up(i, first, second)
+            if i in (2, 6):
+                gather_v(i // 4 + 2)
             take = len(pending) if i >= N_TILES - 3 else min(1, len(pending))
             for g, q in pending[:take]:
                 if q is None:
@@ -269,3 +290,5 @@ def tile_list_ckg_bias_kernel(
                 else:
                     score_wide(g, q)
             pending = pending[take:]
+        quantise(len(GROUPS) - 1)
+        score_last(len(GROUPS) - 1)

@@ -44,32 +44,64 @@ def tile_list_ckg_bias_kernel(
 
         list1 = keep.tile([P, J // 16], U16, name="list1")
         list2 = keep.tile([P, J // 16], U16, name="list2")
-        v_rows = held([P, T // 4], I32, "v_rows", "slot_a")
-        v2_planes = held([P, T // 4], I32, "v2_planes", "slot_b")
-        wr_raw = held([P, 2, 2 * R], I32, "wr_raw")
-        wr_raw_plane = held([P, 2, 2, R // 4], I32, "wr_raw_plane")
-        g_plane = held([P, J // 4], I32, "g_plane")
+        v_plane = held([P, T // 4], I32, "v_plane", "slot_a")
+        wr_raw_plane = held([P, 2, 2, R // 4], I32, "wr_raw_plane", "slot_b")
+        v2_planes = held([P, T // 4], I32, "v2_planes", "slot_c")
         g2_pass1 = held([P, J // 4], I32, "g2_pass1")
-        for plane in (v2_planes, wr_raw_plane, g_plane, g2_pass1):
+        for plane in (v_plane, wr_raw_plane, v2_planes, g2_pass1):
             nc.vector.memset(plane[:], 0)
 
         nc.sync.dma_start(list1[:], offs)
-        nc.sync.dma_start(v_rows[:], tab_scales[0].bitcast(I32).unsqueeze(1).to_broadcast([16, 8, T // 4]))
         nc.sync.dma_start(list2[:], offs2)
-        for w, src in enumerate((wrr_words, wri_words)):
-            nc.sync.dma_start(
-                wr_raw[:, w, :].rearrange("p (a r) -> p a r", a=2), src.rearrange("a p r i -> p a (r i)").bitcast(I32)
-            )
-        for r in range(4):
-            nc.sync.dma_start(
-                v2_planes[r:P:16, :], tab2_scales.rearrange("a (q r) t -> r q a t", r=4)[r].bitcast(I32)
-            )
+
+        def load_wr(src, name, tag):
+            raw = held([P, 2 * R], I32, name, tag)
+            nc.sync.dma_start(raw[:].rearrange("p (a r) -> p a r", a=2), src.rearrange("a p r i -> p a (r i)").bitcast(I32))
+            return raw
+
+        wrr_raw = load_wr(wrr_words, "wrr_raw", None)
+        for q in range(4):
+            nc.sync.dma_start(v_plane[32 * q : 32 * q + 4, :], tab_scales[0, 4 * q : 4 * q + 4, :].bitcast(I32))
         for w, src in enumerate((wrr_scales, wri_scales)):
             for q in range(4):
                 nc.sync.dma_start(
                     wr_raw_plane[32 * q : 32 * q + 4, w, :, :],
                     src[:, 4 * q : 4 * q + 4, :].rearrange("a q r -> q a r").bitcast(I32),
                 )
+        for r in range(4):
+            nc.sync.dma_start(
+                v2_planes[r:P:16, :], tab2_scales.rearrange("a (q r) t -> r q a t", r=4)[r].bitcast(I32)
+            )
+
+        g_plane = held([P, J], U8, "g_plane")
+        nc.vector.tensor_copy(g_plane[:], v_plane[:].bitcast(U8).indirect(list1[:]))
+        v2_words = held([P, T], I32, "v2_words", "slot_a")
+        nc.sync.dma_start(v2_words[:], tab2_words[0].rearrange("p t i -> p (t i)").bitcast(I32))
+
+        wr_plane = held([P, 2, PACK, 2 * P], U8, "wr_plane")
+        for w in range(2):
+            nc.vector.tensor_copy(
+                wr_plane[:, w, :, :],
+                wr_raw_plane[:, w, :, :].rearrange("p a r -> p (a r)").bitcast(U8).rearrange("p (m t) -> p t m", t=PACK),
+            )
+        we_raw = held([P, 2, PACK, R], F32, "we_raw", "slot_b")
+        for w, src in enumerate((wer, wei)):
+            nc.sync.dma_start(we_raw[:, w, :, :], src.rearrange("(p i) r -> p i r", i=PACK))
+
+        g2_planes = held([P, J], U8, "g2_planes")
+        nc.vector.tensor_copy(g2_planes[:], v2_planes[:].bitcast(U8).indirect(list2[:]))
+        for q in range(4):
+            nc.sync.dma_start(g2_pass1[32 * q : 32 * q + 4, :], g2_planes[32 * q + 16 : 32 * q + 20, :].bitcast(I32))
+        wri_raw = load_wr(wri_words, "wri_raw", "slot_c")
+        wr_words = held([P, 2, PACK, 2 * P], I32, "wr_words")
+
+        def permute_words(w, raw):
+            nc.vector.tensor_copy(
+                wr_words[:, w, :, :].rearrange("p t (g m) -> p g t m", m=4),
+                raw[:].rearrange("p (g m t) -> p g t m", m=4, t=PACK),
+            )
+
+        permute_words(0, wrr_raw)
 
         g_words = [held([P, CHUNK], U32, f"g_words{c}") for c in range(N_CHUNKS)]
         g2_pairs = [held([P, CHUNK], U32, f"g2_pairs{c}") for c in range(N_CHUNKS)]
@@ -83,43 +115,24 @@ def tile_list_ckg_bias_kernel(
                 g2_words[c][:].bitcast(U16), g2_pairs[c][:].bitcast(U16).rearrange("p (n d) -> p d n", d=2)
             )
 
-        g_rows = held([P, J], U8, "g_rows", "slot_c")
-        nc.vector.tensor_copy(g_rows[:], v_rows[:].bitcast(U8).indirect(list1[:]))
-        v2_words = held([P, T], I32, "v2_words", "slot_a")
-        for q in range(4):
-            nc.sync.dma_start(g_plane[32 * q : 32 * q + 4, :], g_rows[32 * q : 32 * q + 32 : 8, :].bitcast(I32))
-        nc.sync.dma_start(v2_words[:], tab2_words[0].rearrange("p t i -> p (t i)").bitcast(I32))
-        we_raw = held([P, 2, PACK, R], F32, "we_raw", "slot_c")
-        for w, src in enumerate((wer, wei)):
-            nc.sync.dma_start(we_raw[:, w, :, :], src.rearrange("(p i) r -> p i r", i=PACK))
-
-        g2_planes = held([P, J], U8, "g2_planes")
-        nc.vector.tensor_copy(g2_planes[:], v2_planes[:].bitcast(U8).indirect(list2[:]))
-        for q in range(4):
-            nc.sync.dma_start(g2_pass1[32 * q : 32 * q + 4, :], g2_planes[32 * q + 16 : 32 * q + 20, :].bitcast(I32))
-        v_words = held([P, T], I32, "v_words", "slot_b")
+        for c in range(N_CHUNKS + 1):
+            if c < N_CHUNKS:
+                gather_v2(c)
+            if c > 0:
+                part_v2(c - 1)
+        v_words = held([P, T], I32, "v_words", "g2_pairs0")
         nc.sync.dma_start(v_words[:], tab_words[0].rearrange("p t i -> p (t i)").bitcast(I32))
 
         def gather_v(c):
             nc.vector.tensor_copy(g_words[c][:], v_words[:].bitcast(U32).indirect(cols(list1, c)))
 
-        wr_plane = held([P, 2, PACK, 2 * P], U8, "wr_plane")
-        wr_words = held([P, 2, PACK, 2 * P], I32, "wr_words")
-        for w in range(2):
-            nc.vector.tensor_copy(
-                wr_plane[:, w, :, :],
-                wr_raw_plane[:, w, :, :].rearrange("p a r -> p (a r)").bitcast(U8).rearrange("p (m t) -> p t m", t=PACK),
-            )
-            nc.vector.tensor_copy(
-                wr_words[:, w, :, :].rearrange("p t (g m) -> p g t m", m=4),
-                wr_raw[:, w, :].rearrange("p (g m t) -> p g t m", m=4, t=PACK),
-            )
+        permute_words(1, wri_raw)
 
         we_bf = [held([P, PACK * R], BF16, f"we_bf{w}") for w in range(2)]
         for w in range(2):
             nc.scalar.copy(
-                we_bf[w][:].rearrange("p (t m i) -> p m i t", t=PACK, i=PACK),
-                we_raw[:, w, :, :].rearrange("p i (m t) -> p m i t", t=PACK),
+                we_bf[w][:].rearrange("p (t m i) -> p m t i", t=PACK, i=PACK),
+                we_raw[:, w, :, :].rearrange("p i (m t) -> p m t i", t=PACK),
             )
         we_words = [held([P, R], U32, f"we_words{w}") for w in range(2)]
         we_plane = [held([P, R], U8, f"we_plane{w}") for w in range(2)]
@@ -155,7 +168,7 @@ def tile_list_ckg_bias_kernel(
                         lhsT=we_words[w][:, t * P : (t + 1) * P].bitcast(FP8X4),
                         lhsT_scale=we_plane[w][:, t * P : (t + 1) * P],
                         rhs=g_words[c][:, tok].bitcast(FP8X4),
-                        rhs_scale=g_plane[:].bitcast(U8)[:, i * TOK : (i + 1) * TOK],
+                        rhs_scale=g_plane[:, i * TOK : (i + 1) * TOK],
                         start=True,
                         stop=True,
                     )
@@ -230,17 +243,12 @@ def tile_list_ckg_bias_kernel(
                 staged[:].rearrange("p (q j) -> p q j", q=4),
             )
 
-        for c in range(N_CHUNKS):
-            gather_v2(c)
-            if c > 0:
-                part_v2(c - 1)
         quantise_we(0)
-        part_v2(N_CHUNKS - 1)
         quantise_we(1)
         gather_v(0)
         gather_v(1)
 
-        n_words = held([P, 2, N // 2], I32, "n_words", "slot_c")
+        n_words = held([P, 2, N // 2], I32, "n_words", "slot_b")
         for w, src in enumerate((nr_words, ni_words)):
             nc.sync.dma_start(n_words[:, w, :], src[0].bitcast(I32))
         n_plane = held([P, 2, N // 4], I32, "n_plane", "we_bf0")

@@ -24,6 +24,10 @@ CHUNK = 512
 N_CHUNKS = J // CHUNK
 N_TILES = J // TOK
 GROUPS = [4, 4, 4, 1, 1, 1, 1]
+REL_AHEAD = 2
+WORDS_AFTER = {2: 4, 3: 8}
+PAIRS_AFTER = {3: 5}
+PLANE_AFTER = {3: 7}
 
 
 def tile_list_ckg_bias_kernel(
@@ -44,121 +48,134 @@ def tile_list_ckg_bias_kernel(
 
         list1 = keep.tile([P, J // 16], U16, name="list1")
         list2 = keep.tile([P, J // 16], U16, name="list2")
-        v_plane = held([P, T // 4], I32, "v_plane", "slot_a")
-        wr_raw_plane = held([P, 2, 2, R // 4], I32, "wr_raw_plane", "slot_b")
-        v2_planes = held([P, T // 4], I32, "v2_planes", "slot_c")
-        g2_pass1 = held([P, J // 4], I32, "g2_pass1")
-        for plane in (v_plane, wr_raw_plane, v2_planes, g2_pass1):
-            nc.vector.memset(plane[:], 0)
-
-        nc.sync.dma_start(list1[:], offs)
-        nc.sync.dma_start(list2[:], offs2)
-
-        def load_wr(src, name, tag):
-            raw = held([P, 2 * R], I32, name, tag)
-            nc.sync.dma_start(raw[:].rearrange("p (a r) -> p a r", a=2), src.rearrange("a p r i -> p a (r i)").bitcast(I32))
-            return raw
-
-        wrr_raw = load_wr(wrr_words, "wrr_raw", None)
-        for q in range(4):
-            nc.sync.dma_start(v_plane[32 * q : 32 * q + 4, :], tab_scales[0, 4 * q : 4 * q + 4, :].bitcast(I32))
+        v2_rows = held([P, T // 4], I32, "v2_rows", "slot_a")
+        v_plane = held([P, T // 4], I32, "v_plane")
+        g2_planes = held([P, 2 * J // 4], I32, "g2_planes")
+        wr_raw_plane = held([P, 2, 2, R // 4], I32, "wr_raw_plane")
+        nc.gpsimd.memset(v_plane[:], 0)
+        nc.vector.memset(v2_rows[0:96, :], 0)
+        nc.gpsimd.memset(wr_raw_plane[:], 0)
         for w, src in enumerate((wrr_scales, wri_scales)):
-            for q in range(4):
-                nc.sync.dma_start(
-                    wr_raw_plane[32 * q : 32 * q + 4, w, :, :],
-                    src[:, 4 * q : 4 * q + 4, :].rearrange("a q r -> q a r").bitcast(I32),
+            for r in range(4):
+                nc.gpsimd.dma_start(
+                    wr_raw_plane[r:P:32, w, :, :], src.rearrange("a (q r) c -> r q a c", r=4)[r].bitcast(I32)
                 )
-        for r in range(4):
-            nc.sync.dma_start(
-                v2_planes[r:P:16, :], tab2_scales.rearrange("a (q r) t -> r q a t", r=4)[r].bitcast(I32)
-            )
+        nc.vector.memset(g2_planes[:], 0)
 
-        g_plane = held([P, J], U8, "g_plane")
-        nc.vector.tensor_copy(g_plane[:], v_plane[:].bitcast(U8).indirect(list1[:]))
-        v2_words = held([P, T], I32, "v2_words", "slot_a")
+        nc.sync.dma_start(list2[:], offs2)
+        nc.sync.dma_start(v2_rows[96:P, :], tab2_scales.rearrange("a g t -> g a t").bitcast(I32))
+        v2_words = held([P, T], I32, "v2_words")
         nc.sync.dma_start(v2_words[:], tab2_words[0].rearrange("p t i -> p (t i)").bitcast(I32))
-
-        wr_plane = held([P, 2, PACK, 2 * P], U8, "wr_plane")
-        for w in range(2):
-            nc.vector.tensor_copy(
-                wr_plane[:, w, :, :],
-                wr_raw_plane[:, w, :, :].rearrange("p a r -> p (a r)").bitcast(U8).rearrange("p (m t) -> p t m", t=PACK),
+        wr_raw = held([P, 2, 2 * R], I32, "wr_raw")
+        for w, src in enumerate((wrr_words, wri_words)):
+            nc.sync.dma_start(
+                wr_raw[:, w, :].rearrange("p (a r) -> p a r", a=2), src.rearrange("a p r i -> p a (r i)").bitcast(I32)
             )
-        we_raw = held([P, 2, PACK, R], F32, "we_raw", "slot_b")
+        nc.sync.dma_start(list1[:], offs)
+        for r in range(4):
+            nc.scalar.dma_start(v_plane[r:P:32, :], tab_scales[0].rearrange("(q r) t -> r q t", r=4)[r].bitcast(I32))
+
+        g2_rows = held([P, J], U8, "g2_rows")
+        nc.vector.tensor_copy(g2_rows[:], v2_rows[:].bitcast(U8).indirect(list2[:]))
+        we_raw = held([P, 2, PACK, R], F32, "we_raw", "slot_a")
         for w, src in enumerate((wer, wei)):
             nc.sync.dma_start(we_raw[:, w, :, :], src.rearrange("(p i) r -> p i r", i=PACK))
-
-        g2_planes = held([P, J], U8, "g2_planes")
-        nc.vector.tensor_copy(g2_planes[:], v2_planes[:].bitcast(U8).indirect(list2[:]))
         for q in range(4):
-            nc.sync.dma_start(g2_pass1[32 * q : 32 * q + 4, :], g2_planes[32 * q + 16 : 32 * q + 20, :].bitcast(I32))
-        wri_raw = load_wr(wri_words, "wri_raw", "slot_c")
-        wr_words = held([P, 2, PACK, 2 * P], I32, "wr_words")
+            nc.sync.dma_start(g2_planes[32 * q : 32 * q + 4, :], g2_rows[96 + 8 * q : 96 + 8 * q + 8, :].bitcast(I32))
 
-        def permute_words(w, raw):
-            nc.vector.tensor_copy(
-                wr_words[:, w, :, :].rearrange("p t (g m) -> p g t m", m=4),
-                raw[:].rearrange("p (g m t) -> p g t m", m=4, t=PACK),
-            )
+        g_plane = {}
+        g_words = {}
+        g2_pairs = {}
+        g2_words = {}
 
-        permute_words(0, wrr_raw)
+        def gather_plane(c):
+            g_plane[c] = held([P, CHUNK], U8, f"g_plane{c}", f"second{PLANE_AFTER[c]}" if c in PLANE_AFTER else None)
+            nc.vector.tensor_copy(g_plane[c][:], v_plane[:].bitcast(U8).indirect(cols(list1, c)))
 
-        g_words = [held([P, CHUNK], U32, f"g_words{c}") for c in range(N_CHUNKS)]
-        g2_pairs = [held([P, CHUNK], U32, f"g2_pairs{c}") for c in range(N_CHUNKS)]
-        g2_words = [held([P, 2, 2 * CHUNK], U8, f"g2_words{c}") for c in range(N_CHUNKS)]
+        def gather_v(c):
+            g_words[c] = held([P, CHUNK], U32, f"g_words{c}", f"first{WORDS_AFTER[c]}" if c in WORDS_AFTER else None)
+            nc.vector.tensor_copy(g_words[c][:], v_words[:].bitcast(U32).indirect(cols(list1, c)))
 
         def gather_v2(c):
+            g2_pairs[c] = held([P, CHUNK], U32, f"g2_pairs{c}", {2: "wr_raw_plane", 3: f"first{PAIRS_AFTER[3]}"}.get(c))
             nc.vector.tensor_copy(g2_pairs[c][:], v2_words[:].bitcast(U32).indirect(cols(list2, c)))
 
         def part_v2(c):
+            g2_words[c] = held([P, 2, 2 * CHUNK], U8, f"g2_words{c}")
             nc.vector.tensor_copy(
                 g2_words[c][:].bitcast(U16), g2_pairs[c][:].bitcast(U16).rearrange("p (n d) -> p d n", d=2)
             )
 
-        for c in range(N_CHUNKS + 1):
-            if c < N_CHUNKS:
-                gather_v2(c)
-            if c > 0:
-                part_v2(c - 1)
+        gather_v2(0)
+        gather_v2(1)
+        part_v2(0)
+        part_v2(1)
+        wr_words = held([P, 2, PACK, 2 * P], I32, "wr_words")
+        for w in range(2):
+            nc.vector.tensor_copy(
+                wr_words[:, w, :, :].rearrange("p t (g m) -> p g t m", m=4),
+                wr_raw[:, w, :].rearrange("p (g m t) -> p g t m", m=4, t=PACK),
+            )
         v_words = held([P, T], I32, "v_words", "g2_pairs0")
         nc.sync.dma_start(v_words[:], tab_words[0].rearrange("p t i -> p (t i)").bitcast(I32))
-
-        def gather_v(c):
-            nc.vector.tensor_copy(g_words[c][:], v_words[:].bitcast(U32).indirect(cols(list1, c)))
-
-        permute_words(1, wri_raw)
+        gather_plane(0)
+        gather_plane(1)
+        gather_plane(2)
 
         we_bf = [held([P, PACK * R], BF16, f"we_bf{w}") for w in range(2)]
+        we_words = [held([P, R], U32, f"we_words{w}") for w in range(2)]
+        we_plane = [held([P, R], U8, f"we_plane{w}") for w in range(2)]
         for w in range(2):
             nc.scalar.copy(
                 we_bf[w][:].rearrange("p (t m i) -> p m t i", t=PACK, i=PACK),
                 we_raw[:, w, :, :].rearrange("p i (m t) -> p m t i", t=PACK),
             )
-        we_words = [held([P, R], U32, f"we_words{w}") for w in range(2)]
-        we_plane = [held([P, R], U8, f"we_plane{w}") for w in range(2)]
 
         def quantise_we(w):
             nc.vector.quantize_mx(out=we_words[w][:].bitcast(FP8X4), scales=we_plane[w][:], in_=we_bf[w][:])
 
-        def products(i):
+        quantise_we(0)
+        wr_plane = held([P, 2, PACK, 2 * P], U8, "wr_plane", "we_bf0")
+        for w in range(2):
+            nc.vector.tensor_copy(
+                wr_plane[:, w, :, :],
+                wr_raw_plane[:, w, :, :].rearrange("p a r -> p (a r)").bitcast(U8).rearrange("p (m t) -> p t m", t=PACK),
+            )
+        quantise_we(1)
+        gather_v2(2)
+        part_v2(2)
+        gather_v(0)
+        gather_v(1)
+
+        relation = {}
+
+        def project_relation(i):
             c, u = divmod(i, CHUNK // TOK)
-            tok = slice(u * TOK, (u + 1) * TOK)
-            cd = ring.tile([P, 2, TOK, PACK], F32, name="cd", bufs=6)
+            relation[i] = ring.tile([P, 2, TOK, PACK], F32, name="cd", bufs=REL_AHEAD)
             for w in range(2):
                 bank = psum.tile([P, PACK, TOK], F32, name=f"rel{w}")
                 for t in range(PACK):
                     for a in range(2):
-                        plane = g2_planes[:] if a == 0 else g2_pass1[:].bitcast(U8)
                         nc.tensor.matmul_mx(
                             out=bank[:, t, :],
                             lhsT=wr_words[:, w, t, a * P : (a + 1) * P].bitcast(FP8X4),
                             lhsT_scale=wr_plane[:, w, t, a * P : (a + 1) * P],
                             rhs=g2_words[c][:, a, 2 * u * TOK : 2 * (u + 1) * TOK].bitcast(FP4X4),
-                            rhs_scale=plane[:, i * TOK : (i + 1) * TOK],
+                            rhs_scale=g2_planes[:].bitcast(U8)[:, a * J + i * TOK : a * J + (i + 1) * TOK],
                             start=(a == 0),
                             stop=(a == 1),
                         )
-                nc.scalar.copy(cd[:, w, :, :], bank[:].rearrange("p t n -> p n t"))
+                nc.scalar.copy(relation[i][:, w, :, :], bank[:].rearrange("p t n -> p n t"))
+
+        def term(i, name, after):
+            if i in after:
+                return held([P, 2, TOK, PACK], F32, f"{name}{i}")
+            return ring.tile([P, 2, TOK, PACK], F32, name=name)
+
+        def products(i):
+            c, u = divmod(i, CHUNK // TOK)
+            tok = slice(u * TOK, (u + 1) * TOK)
+            cd = relation[i]
             ent = []
             for w in range(2):
                 bank = psum.tile([P, PACK, TOK], F32, name=f"ent{w}", bufs=2)
@@ -168,13 +185,13 @@ def tile_list_ckg_bias_kernel(
                         lhsT=we_words[w][:, t * P : (t + 1) * P].bitcast(FP8X4),
                         lhsT_scale=we_plane[w][:, t * P : (t + 1) * P],
                         rhs=g_words[c][:, tok].bitcast(FP8X4),
-                        rhs_scale=g_plane[:, i * TOK : (i + 1) * TOK],
+                        rhs_scale=g_plane[c][:, tok],
                         start=True,
                         stop=True,
                     )
                 ent.append(bank[:].rearrange("p t n -> p n t"))
-            first = ring.tile([P, 2, TOK, PACK], F32, name="first")
-            second = ring.tile([P, 2, TOK, PACK], F32, name="second")
+            first = term(i, "first", list(WORDS_AFTER.values()) + list(PAIRS_AFTER.values()))
+            second = term(i, "second", list(PLANE_AFTER.values()))
             nc.vector.tensor_tensor(first[:, 0, :, :], ent[0], cd[:, 0, :, :], MULT)
             nc.vector.tensor_tensor(first[:, 1, :, :], ent[0], cd[:, 1, :, :], MULT)
             nc.vector.scalar_tensor_tensor(second[:, 0, :, :], ent[1], -1.0, cd[:, 1, :, :], MULT, MULT)
@@ -243,20 +260,15 @@ def tile_list_ckg_bias_kernel(
                 staged[:].rearrange("p (q j) -> p q j", q=4),
             )
 
-        quantise_we(0)
-        quantise_we(1)
-        gather_v(0)
-        gather_v(1)
-
-        n_words = held([P, 2, N // 2], I32, "n_words", "slot_b")
+        n_words = held([P, 2, N // 2], I32, "n_words", "slot_a")
         for w, src in enumerate((nr_words, ni_words)):
             nc.sync.dma_start(n_words[:, w, :], src[0].bitcast(I32))
-        n_plane = held([P, 2, N // 4], I32, "n_plane", "we_bf0")
+        n_plane = held([P, 2, N // 4], I32, "n_plane", "we_bf1")
         nc.gpsimd.memset(n_plane[:], 0)
         for w, src in enumerate((nr_scales, ni_scales)):
             for q in range(4):
                 nc.sync.dma_start(n_plane[32 * q : 32 * q + 4, w, :], src[0, 4 * q : 4 * q + 4, :].bitcast(I32))
-        bias = held([P, N // P], F32, "bias", "we_bf1")
+        bias = held([P, N // P], F32, "bias", "g2_rows")
         with nc.allow_non_contiguous_dma(reason="one bias value to a partition"):
             nc.sync.dma_start(bias[:], b.rearrange("(q p) -> p q", p=P))
 
@@ -280,6 +292,8 @@ def tile_list_ckg_bias_kernel(
                     staged[:, 0 : 2 * TOK].rearrange("p (q j) -> p q j", q=2),
                 )
 
+        for i in range(REL_AHEAD):
+            project_relation(i)
         pending = []
         for i in range(N_TILES):
             first, second = products(i)
@@ -289,8 +303,17 @@ def tile_list_ckg_bias_kernel(
                     quantise(g)
                     pending.extend([(g, None)] if GROUPS[g] == 1 else [(g, q) for q in range(4)])
             add_up(i, first, second)
-            if i in (2, 6):
-                gather_v(i // 4 + 2)
+            for c in range(1, N_CHUNKS):
+                if WORDS_AFTER.get(c) == i - 1:
+                    gather_v(c)
+                if PAIRS_AFTER.get(c) == i - 1:
+                    gather_v2(c)
+                if PAIRS_AFTER.get(c) == i - 2:
+                    part_v2(c)
+                if PLANE_AFTER.get(c) == i - 1:
+                    gather_plane(c)
+            if i + REL_AHEAD < N_TILES:
+                project_relation(i + REL_AHEAD)
             take = len(pending) if i >= N_TILES - 3 else min(1, len(pending))
             for g, q in pending[:take]:
                 if q is None:

@@ -72,14 +72,15 @@ def tile_list_ckg_bias_kernel(
                 wr_raw[:, w, :].rearrange("p (a r) -> p a r", a=2), src.rearrange("a p r i -> p a (r i)").bitcast(I32)
             )
         nc.sync.dma_start(list1[:], offs)
+        we_raw = [held([P, PACK, R], F32, "wer_raw")]
+        nc.sync.dma_start(we_raw[0][:], wer.rearrange("(p i) r -> p i r", i=PACK))
         for r in range(4):
             nc.scalar.dma_start(v_plane[r:P:32, :], tab_scales[0].rearrange("(q r) t -> r q t", r=4)[r].bitcast(I32))
 
         g2_rows = held([P, J], U8, "g2_rows")
         nc.vector.tensor_copy(g2_rows[:], v2_rows[:].bitcast(U8).indirect(list2[:]))
-        we_raw = held([P, 2, PACK, R], F32, "we_raw", "slot_a")
-        for w, src in enumerate((wer, wei)):
-            nc.sync.dma_start(we_raw[:, w, :, :], src.rearrange("(p i) r -> p i r", i=PACK))
+        we_raw.append(held([P, PACK, R], F32, "wei_raw", "slot_a"))
+        nc.sync.dma_start(we_raw[1][:], wei.rearrange("(p i) r -> p i r", i=PACK))
         for q in range(4):
             nc.sync.dma_start(g2_planes[32 * q : 32 * q + 4, :], g2_rows[96 + 8 * q : 96 + 8 * q + 8, :].bitcast(I32))
 
@@ -88,16 +89,16 @@ def tile_list_ckg_bias_kernel(
         g2_pairs = {}
         g2_words = {}
 
-        def gather_plane(c):
-            g_plane[c] = held([P, CHUNK], U8, f"g_plane{c}", f"second{PLANE_AFTER[c]}" if c in PLANE_AFTER else None)
+        def gather_plane(c, tag=None):
+            g_plane[c] = held([P, CHUNK], U8, f"g_plane{c}", tag)
             nc.vector.tensor_copy(g_plane[c][:], v_plane[:].bitcast(U8).indirect(cols(list1, c)))
 
-        def gather_v(c):
-            g_words[c] = held([P, CHUNK], U32, f"g_words{c}", f"first{WORDS_AFTER[c]}" if c in WORDS_AFTER else None)
+        def gather_v(c, tag=None):
+            g_words[c] = held([P, CHUNK], U32, f"g_words{c}", tag)
             nc.vector.tensor_copy(g_words[c][:], v_words[:].bitcast(U32).indirect(cols(list1, c)))
 
-        def gather_v2(c):
-            g2_pairs[c] = held([P, CHUNK], U32, f"g2_pairs{c}", {2: "wr_raw_plane", 3: f"first{PAIRS_AFTER[3]}"}.get(c))
+        def gather_v2(c, tag=None):
+            g2_pairs[c] = held([P, CHUNK], U32, f"g2_pairs{c}", tag)
             nc.vector.tensor_copy(g2_pairs[c][:], v2_words[:].bitcast(U32).indirect(cols(list2, c)))
 
         def part_v2(c):
@@ -128,7 +129,7 @@ def tile_list_ckg_bias_kernel(
         for w in range(2):
             nc.scalar.copy(
                 we_bf[w][:].rearrange("p (t m i) -> p m t i", t=PACK, i=PACK),
-                we_raw[:, w, :, :].rearrange("p i (m t) -> p m t i", t=PACK),
+                we_raw[w][:].rearrange("p i (m t) -> p m t i", t=PACK),
             )
 
         def quantise_we(w):
@@ -142,16 +143,16 @@ def tile_list_ckg_bias_kernel(
                 wr_raw_plane[:, w, :, :].rearrange("p a r -> p (a r)").bitcast(U8).rearrange("p (m t) -> p t m", t=PACK),
             )
         quantise_we(1)
-        gather_v2(2)
+        gather_v2(2, "wr_raw_plane")
         part_v2(2)
-        gather_v(0)
+        gather_v(0, "wr_raw_plane")
         gather_v(1)
 
         relation = {}
 
         def project_relation(i):
             c, u = divmod(i, CHUNK // TOK)
-            relation[i] = ring.tile([P, 2, TOK, PACK], F32, name="cd", bufs=REL_AHEAD)
+            relation[i] = ring.tile([P, 2, TOK, PACK], F32, name="relation", bufs=REL_AHEAD)
             for w in range(2):
                 bank = psum.tile([P, PACK, TOK], F32, name=f"rel{w}")
                 for t in range(PACK):
@@ -167,15 +168,15 @@ def tile_list_ckg_bias_kernel(
                         )
                 nc.scalar.copy(relation[i][:, w, :, :], bank[:].rearrange("p t n -> p n t"))
 
-        def term(i, name, after):
-            if i in after:
+        def term(i, name, taken_over):
+            if i in taken_over:
                 return held([P, 2, TOK, PACK], F32, f"{name}{i}")
             return ring.tile([P, 2, TOK, PACK], F32, name=name)
 
         def products(i):
             c, u = divmod(i, CHUNK // TOK)
             tok = slice(u * TOK, (u + 1) * TOK)
-            cd = relation[i]
+            arr, ari = relation[i][:, 0, :, :], relation[i][:, 1, :, :]
             ent = []
             for w in range(2):
                 bank = psum.tile([P, PACK, TOK], F32, name=f"ent{w}", bufs=2)
@@ -192,10 +193,10 @@ def tile_list_ckg_bias_kernel(
                 ent.append(bank[:].rearrange("p t n -> p n t"))
             first = term(i, "first", list(WORDS_AFTER.values()) + list(PAIRS_AFTER.values()))
             second = term(i, "second", list(PLANE_AFTER.values()))
-            nc.vector.tensor_tensor(first[:, 0, :, :], ent[0], cd[:, 0, :, :], MULT)
-            nc.vector.tensor_tensor(first[:, 1, :, :], ent[0], cd[:, 1, :, :], MULT)
-            nc.vector.scalar_tensor_tensor(second[:, 0, :, :], ent[1], -1.0, cd[:, 1, :, :], MULT, MULT)
-            nc.vector.tensor_tensor(second[:, 1, :, :], ent[1], cd[:, 0, :, :], MULT)
+            nc.vector.tensor_tensor(first[:, 0, :, :], ent[0], arr, MULT)
+            nc.vector.tensor_tensor(first[:, 1, :, :], ent[0], ari, MULT)
+            nc.vector.scalar_tensor_tensor(second[:, 0, :, :], ent[1], -1.0, ari, MULT, MULT)
+            nc.vector.tensor_tensor(second[:, 1, :, :], ent[1], arr, MULT)
             return first, second
 
         starts = [sum(GROUPS[:g]) for g in range(len(GROUPS))]
@@ -225,13 +226,13 @@ def tile_list_ckg_bias_kernel(
             )
             h_mx[g] = (words, plane)
 
-        def score(g, q, bank, staged):
+        def score(g, q, bank):
             width = GROUPS[g] * TOK
             words, plane = h_mx[g]
             for w in range(2):
                 nc.tensor.matmul_mx(
                     out=bank,
-                    lhsT=n_words[:, w, q * 64 : (q + 1) * 64].bitcast(FP4X4),
+                    lhsT=n_words[:, w, q * P // 2 : (q + 1) * P // 2].bitcast(FP4X4),
                     lhsT_scale=n_plane[:, w, :].bitcast(U8)[:, q * P : (q + 1) * P],
                     rhs=words[:, w * width : (w + 1) * width].bitcast(FP8X4),
                     rhs_scale=plane[:, w * width : (w + 1) * width],
@@ -242,7 +243,7 @@ def tile_list_ckg_bias_kernel(
         def score_wide(g, q):
             bank = psum.tile([P, CHUNK], F32, name="score", bufs=2)
             staged = ring.tile([P, CHUNK], F32, name="staged", bufs=4)
-            score(g, q, bank[:], staged)
+            score(g, q, bank[:])
             nc.scalar.activation(staged[:], bank[:], IDENTITY, bias=bias[:, q : q + 1])
             nc.sync.dma_start(out[q * P : (q + 1) * P, starts[g] * TOK : starts[g] * TOK + CHUNK], staged[:])
 
@@ -250,7 +251,7 @@ def tile_list_ckg_bias_kernel(
             bank = psum.tile([P, CHUNK], F32, name="score", bufs=2)
             staged = ring.tile([P, CHUNK], F32, name="staged", bufs=4)
             for q in range(4):
-                score(g, q, bank[:, q * TOK : (q + 1) * TOK], staged)
+                score(g, q, bank[:, q * TOK : (q + 1) * TOK])
             for q in range(4):
                 nc.scalar.activation(
                     staged[:, q * TOK : (q + 1) * TOK], bank[:, q * TOK : (q + 1) * TOK], IDENTITY, bias=bias[:, q : q + 1]
@@ -277,7 +278,7 @@ def tile_list_ckg_bias_kernel(
                 bank = psum.tile([P, CHUNK], F32, name=f"rel{half}")
                 staged = ring.tile([P, CHUNK], F32, name="staged", bufs=4)
                 for u in range(2):
-                    score(g, 2 * half + u, bank[:, u * TOK : (u + 1) * TOK], staged)
+                    score(g, 2 * half + u, bank[:, u * TOK : (u + 1) * TOK])
                 for u in range(2):
                     q = 2 * half + u
                     span = slice(u * TOK, (u + 1) * TOK)
@@ -303,15 +304,15 @@ def tile_list_ckg_bias_kernel(
                     quantise(g)
                     pending.extend([(g, None)] if GROUPS[g] == 1 else [(g, q) for q in range(4)])
             add_up(i, first, second)
-            for c in range(1, N_CHUNKS):
+            for c in range(N_CHUNKS):
                 if WORDS_AFTER.get(c) == i - 1:
-                    gather_v(c)
+                    gather_v(c, f"first{i - 1}")
                 if PAIRS_AFTER.get(c) == i - 1:
-                    gather_v2(c)
+                    gather_v2(c, f"first{i - 1}")
                 if PAIRS_AFTER.get(c) == i - 2:
                     part_v2(c)
                 if PLANE_AFTER.get(c) == i - 1:
-                    gather_plane(c)
+                    gather_plane(c, f"second{i - 1}")
             if i + REL_AHEAD < N_TILES:
                 project_relation(i + REL_AHEAD)
             take = len(pending) if i >= N_TILES - 3 else min(1, len(pending))

@@ -26,8 +26,7 @@ N_TILES = J // TOK
 GROUPS = [4, 4, 4, 1, 1, 1, 1]
 REL_AHEAD = 2
 WORDS_AFTER = {2: 4, 3: 8}
-PAIRS_AFTER = {3: 5}
-PLANE_AFTER = {3: 7}
+PAIRS_AFTER = {3: 6}
 
 
 def tile_list_ckg_bias_kernel(
@@ -37,61 +36,76 @@ def tile_list_ckg_bias_kernel(
     nc = tc.nc
     with ExitStack() as ctx:
         keep = ctx.enter_context(tc.tile_pool(name="keep", bufs=1))
+        shared = ctx.enter_context(tc.tile_pool(name="shared", bufs=1))
         ring = ctx.enter_context(tc.tile_pool(name="ring", bufs=3))
         psum = ctx.enter_context(tc.psum_pool(name="psum", bufs=1))
 
         def held(shape, dtype, name, tag=None):
             return keep.tile(shape, dtype, name=name, tag=tag or name, align_bytes=64)
 
+        def placed(shape, dtype, name, offset):
+            return shared.tile(shape, dtype, name=name, align_bytes=64, offset=offset)
+
         def cols(lst, c):
             return lst[:, c * (CHUNK // 16) : (c + 1) * (CHUNK // 16)]
 
         list1 = keep.tile([P, J // 16], U16, name="list1")
         list2 = keep.tile([P, J // 16], U16, name="list2")
-        v2_rows = held([P, T // 4], I32, "v2_rows", "slot_a")
-        v_plane = held([P, T // 4], I32, "v_plane")
-        g2_planes = held([P, 2 * J // 4], I32, "g2_planes")
-        wr_raw_plane = held([P, 2, 2, R // 4], I32, "wr_raw_plane")
-        nc.gpsimd.memset(v_plane[:], 0)
+        v2_rows = placed([P, T // 4], I32, "v2_rows", 6144)
+        v_rows = held([P, T // 4], I32, "v_rows")
+        wr_rows = placed([P, 2, R // 4], I32, "wr_rows", 24576 + 8192 - 512)
+        wr_plane = held([P, 4 * R // 4], I32, "wr_plane")
+        nc.gpsimd.memset(v_rows[:], 0)
         nc.vector.memset(v2_rows[0:96, :], 0)
-        nc.gpsimd.memset(wr_raw_plane[:], 0)
-        for w, src in enumerate((wrr_scales, wri_scales)):
-            for r in range(4):
-                nc.gpsimd.dma_start(
-                    wr_raw_plane[r:P:32, w, :, :], src.rearrange("a (q r) c -> r q a c", r=4)[r].bitcast(I32)
-                )
-        nc.vector.memset(g2_planes[:], 0)
+        nc.vector.memset(wr_rows[0:96, :, :], 0)
+        nc.vector.memset(wr_plane[:], 0)
 
         nc.sync.dma_start(list2[:], offs2)
         nc.sync.dma_start(v2_rows[96:P, :], tab2_scales.rearrange("a g t -> g a t").bitcast(I32))
+        for w, src in enumerate((wrr_scales, wri_scales)):
+            nc.scalar.dma_start(wr_rows[96:P, w, :], src.rearrange("a g c -> g a c").bitcast(I32))
+        nc.sync.dma_start(list1[:], offs)
+        wr_raw = [held([P, 2, R], I32, f"wr_raw{w}") for w in range(2)]
+        for w, src in enumerate((wrr_words, wri_words)):
+            nc.sync.dma_start(wr_raw[w][:], src.rearrange("a p r i -> p a (r i)").bitcast(I32))
         v2_words = held([P, T], I32, "v2_words")
         nc.sync.dma_start(v2_words[:], tab2_words[0].rearrange("p t i -> p (t i)").bitcast(I32))
-        wr_raw = held([P, 2, 2 * R], I32, "wr_raw")
-        for w, src in enumerate((wrr_words, wri_words)):
+        nc.scalar.dma_start(v_rows[112:P, :], tab_scales[0].bitcast(I32))
+
+        wr_rows_t = held([P, 2, PACK, P], U8, "wr_rows_t")
+        nc.gpsimd.tensor_copy(
+            wr_rows_t[:],
+            wr_rows[:].rearrange("p w c -> p (w c)").bitcast(U8).rearrange("p (w m t) -> p w t m", w=2, t=PACK),
+        )
+        for q in range(4):
             nc.sync.dma_start(
-                wr_raw[:, w, :].rearrange("p (a r) -> p a r", a=2), src.rearrange("a p r i -> p a (r i)").bitcast(I32)
+                wr_plane[32 * q : 32 * q + 4, :],
+                wr_rows_t[96 + 8 * q : 96 + 8 * q + 8, :, :, :].rearrange("p w t m -> p (w t m)").bitcast(I32),
             )
-        nc.sync.dma_start(list1[:], offs)
-        we_raw = [held([P, PACK, R], F32, "wer_raw")]
+        g2_planes = placed([P, 2 * J // 4], I32, "g2_planes", 24576 + 8192)
+        nc.gpsimd.memset(g2_planes[:], 0)
+        wr_words = held([P, 2, 2, PACK, P], I32, "wr_words")
+        for w in range(2):
+            for a in range(2):
+                nc.gpsimd.tensor_copy(wr_words[:, w, a, :, :], wr_raw[w][:, a, :].rearrange("p (m t) -> p t m", t=PACK))
+        wr_scale = wr_plane[:].bitcast(U8).rearrange("p (a w t m) -> p a w t m", a=2, w=2, t=PACK)
+        we_raw = [placed([P, PACK, R], F32, "wer_raw", 24576)]
         nc.sync.dma_start(we_raw[0][:], wer.rearrange("(p i) r -> p i r", i=PACK))
-        for r in range(4):
-            nc.scalar.dma_start(v_plane[r:P:32, :], tab_scales[0].rearrange("(q r) t -> r q t", r=4)[r].bitcast(I32))
 
         g2_rows = held([P, J], U8, "g2_rows")
         nc.vector.tensor_copy(g2_rows[:], v2_rows[:].bitcast(U8).indirect(list2[:]))
-        we_raw.append(held([P, PACK, R], F32, "wei_raw", "slot_a"))
-        nc.sync.dma_start(we_raw[1][:], wei.rearrange("(p i) r -> p i r", i=PACK))
         for q in range(4):
             nc.sync.dma_start(g2_planes[32 * q : 32 * q + 4, :], g2_rows[96 + 8 * q : 96 + 8 * q + 8, :].bitcast(I32))
+        we_raw.append(placed([P, PACK, R], F32, "wei_raw", 0))
+        nc.sync.dma_start(we_raw[1][:], wei.rearrange("(p i) r -> p i r", i=PACK))
+        v_words = placed([P, T], I32, "v_words", 8192)
+        nc.sync.dma_start(v_words[:], tab_words[0].rearrange("p t i -> p (t i)").bitcast(I32))
+        g_rows = held([P, J], U8, "g_rows")
+        nc.vector.tensor_copy(g_rows[:], v_rows[:].bitcast(U8).indirect(list1[:]))
 
-        g_plane = {}
         g_words = {}
         g2_pairs = {}
         g2_words = {}
-
-        def gather_plane(c, tag=None):
-            g_plane[c] = held([P, CHUNK], U8, f"g_plane{c}", tag)
-            nc.vector.tensor_copy(g_plane[c][:], v_plane[:].bitcast(U8).indirect(cols(list1, c)))
 
         def gather_v(c, tag=None):
             g_words[c] = held([P, CHUNK], U32, f"g_words{c}", tag)
@@ -107,21 +121,13 @@ def tile_list_ckg_bias_kernel(
                 g2_words[c][:].bitcast(U16), g2_pairs[c][:].bitcast(U16).rearrange("p (n d) -> p d n", d=2)
             )
 
-        gather_v2(0)
-        gather_v2(1)
-        part_v2(0)
-        part_v2(1)
-        wr_words = held([P, 2, PACK, 2 * P], I32, "wr_words")
-        for w in range(2):
-            nc.vector.tensor_copy(
-                wr_words[:, w, :, :].rearrange("p t (g m) -> p g t m", m=4),
-                wr_raw[:, w, :].rearrange("p (g m t) -> p g t m", m=4, t=PACK),
-            )
-        v_words = held([P, T], I32, "v_words", "g2_pairs0")
-        nc.sync.dma_start(v_words[:], tab_words[0].rearrange("p t i -> p (t i)").bitcast(I32))
-        gather_plane(0)
-        gather_plane(1)
-        gather_plane(2)
+        for c in range(3):
+            gather_v2(c)
+            part_v2(c)
+        g_planes = held([P, J // 4], I32, "g_planes", "g2_pairs0")
+        nc.gpsimd.memset(g_planes[:], 0)
+        for q in range(4):
+            nc.sync.dma_start(g_planes[32 * q : 32 * q + 4, :], g_rows[112 + 4 * q : 112 + 4 * q + 4, :].bitcast(I32))
 
         we_bf = [held([P, PACK * R], BF16, f"we_bf{w}") for w in range(2)]
         we_words = [held([P, R], U32, f"we_words{w}") for w in range(2)]
@@ -131,36 +137,26 @@ def tile_list_ckg_bias_kernel(
                 we_bf[w][:].rearrange("p (t m i) -> p m t i", t=PACK, i=PACK),
                 we_raw[w][:].rearrange("p i (m t) -> p m t i", t=PACK),
             )
-
-        def quantise_we(w):
             nc.vector.quantize_mx(out=we_words[w][:].bitcast(FP8X4), scales=we_plane[w][:], in_=we_bf[w][:])
-
-        quantise_we(0)
-        wr_plane = held([P, 2, PACK, 2 * P], U8, "wr_plane", "we_bf0")
-        for w in range(2):
-            nc.vector.tensor_copy(
-                wr_plane[:, w, :, :],
-                wr_raw_plane[:, w, :, :].rearrange("p a r -> p (a r)").bitcast(U8).rearrange("p (m t) -> p t m", t=PACK),
-            )
-        quantise_we(1)
-        gather_v2(2, "wr_raw_plane")
-        part_v2(2)
-        gather_v(0, "wr_raw_plane")
+        gather_v(0)
         gather_v(1)
 
         relation = {}
 
         def project_relation(i):
             c, u = divmod(i, CHUNK // TOK)
-            relation[i] = ring.tile([P, 2, TOK, PACK], F32, name="relation", bufs=REL_AHEAD)
+            if i < REL_AHEAD:
+                relation[i] = placed([P, 2, TOK, PACK], F32, f"relation{i}", 4096 * i)
+            else:
+                relation[i] = ring.tile([P, 2, TOK, PACK], F32, name="relation", bufs=REL_AHEAD)
             for w in range(2):
                 bank = psum.tile([P, PACK, TOK], F32, name=f"rel{w}")
                 for t in range(PACK):
                     for a in range(2):
                         nc.tensor.matmul_mx(
                             out=bank[:, t, :],
-                            lhsT=wr_words[:, w, t, a * P : (a + 1) * P].bitcast(FP8X4),
-                            lhsT_scale=wr_plane[:, w, t, a * P : (a + 1) * P],
+                            lhsT=wr_words[:, w, a, t, :].bitcast(FP8X4),
+                            lhsT_scale=wr_scale[:, a, w, t, :],
                             rhs=g2_words[c][:, a, 2 * u * TOK : 2 * (u + 1) * TOK].bitcast(FP4X4),
                             rhs_scale=g2_planes[:].bitcast(U8)[:, a * J + i * TOK : a * J + (i + 1) * TOK],
                             start=(a == 0),
@@ -186,13 +182,13 @@ def tile_list_ckg_bias_kernel(
                         lhsT=we_words[w][:, t * P : (t + 1) * P].bitcast(FP8X4),
                         lhsT_scale=we_plane[w][:, t * P : (t + 1) * P],
                         rhs=g_words[c][:, tok].bitcast(FP8X4),
-                        rhs_scale=g_plane[c][:, tok],
+                        rhs_scale=g_planes[:].bitcast(U8)[:, i * TOK : (i + 1) * TOK],
                         start=True,
                         stop=True,
                     )
                 ent.append(bank[:].rearrange("p t n -> p n t"))
             first = term(i, "first", list(WORDS_AFTER.values()) + list(PAIRS_AFTER.values()))
-            second = term(i, "second", list(PLANE_AFTER.values()))
+            second = term(i, "second", [])
             nc.vector.tensor_tensor(first[:, 0, :, :], ent[0], arr, MULT)
             nc.vector.tensor_tensor(first[:, 1, :, :], ent[0], ari, MULT)
             nc.vector.scalar_tensor_tensor(second[:, 0, :, :], ent[1], -1.0, ari, MULT, MULT)
@@ -261,7 +257,7 @@ def tile_list_ckg_bias_kernel(
                 staged[:].rearrange("p (q j) -> p q j", q=4),
             )
 
-        n_words = held([P, 2, N // 2], I32, "n_words", "slot_a")
+        n_words = placed([P, 2, N // 2], I32, "n_words", 24576)
         for w, src in enumerate((nr_words, ni_words)):
             nc.sync.dma_start(n_words[:, w, :], src[0].bitcast(I32))
         n_plane = held([P, 2, N // 4], I32, "n_plane", "we_bf1")
@@ -311,8 +307,6 @@ def tile_list_ckg_bias_kernel(
                     gather_v2(c, f"first{i - 1}")
                 if PAIRS_AFTER.get(c) == i - 2:
                     part_v2(c)
-                if PLANE_AFTER.get(c) == i - 1:
-                    gather_plane(c, f"second{i - 1}")
             if i + REL_AHEAD < N_TILES:
                 project_relation(i + REL_AHEAD)
             take = len(pending) if i >= N_TILES - 3 else min(1, len(pending))

@@ -51,9 +51,9 @@ def tile_list_ckg_bias_kernel(
 
         list1 = keep.tile([P, J // 16], U16, name="list1")
         list2 = keep.tile([P, J // 16], U16, name="list2")
-        v2_rows = placed([P, T // 4], I32, "v2_rows", 6144)
+        v2_rows = placed([P, T // 4], I32, "v2_rows", 4096 + 8192 + 14336)
         v_rows = held([P, T // 4], I32, "v_rows")
-        wr_rows = placed([P, 2, R // 4], I32, "wr_rows", 24576 + 8192 - 512)
+        wr_rows = placed([P, 2, R // 4], I32, "wr_rows", 4096 - 512)
         wr_plane = held([P, 4 * R // 4], I32, "wr_plane")
         nc.gpsimd.memset(v_rows[:], 0)
         nc.vector.memset(v2_rows[0:96, :], 0)
@@ -65,11 +65,11 @@ def tile_list_ckg_bias_kernel(
         for w, src in enumerate((wrr_scales, wri_scales)):
             nc.scalar.dma_start(wr_rows[96:P, w, :], src.rearrange("a g c -> g a c").bitcast(I32))
         nc.sync.dma_start(list1[:], offs)
+        v2_words = held([P, T], I32, "v2_words")
+        nc.sync.dma_start(v2_words[:], tab2_words[0].rearrange("p t i -> p (t i)").bitcast(I32))
         wr_raw = [held([P, 2, R], I32, f"wr_raw{w}") for w in range(2)]
         for w, src in enumerate((wrr_words, wri_words)):
             nc.sync.dma_start(wr_raw[w][:], src.rearrange("a p r i -> p a (r i)").bitcast(I32))
-        v2_words = held([P, T], I32, "v2_words")
-        nc.sync.dma_start(v2_words[:], tab2_words[0].rearrange("p t i -> p (t i)").bitcast(I32))
         nc.scalar.dma_start(v_rows[112:P, :], tab_scales[0].bitcast(I32))
 
         wr_rows_t = held([P, 2, PACK, P], U8, "wr_rows_t")
@@ -82,26 +82,24 @@ def tile_list_ckg_bias_kernel(
                 wr_plane[32 * q : 32 * q + 4, :],
                 wr_rows_t[96 + 8 * q : 96 + 8 * q + 8, :, :, :].rearrange("p w t m -> p (w t m)").bitcast(I32),
             )
-        g2_planes = placed([P, 2 * J // 4], I32, "g2_planes", 24576 + 8192)
+        g2_planes = placed([P, 2 * J // 4], I32, "g2_planes", 0)
         nc.gpsimd.memset(g2_planes[:], 0)
         wr_words = held([P, 2, 2, PACK, P], I32, "wr_words")
         for w in range(2):
             for a in range(2):
                 nc.gpsimd.tensor_copy(wr_words[:, w, a, :, :], wr_raw[w][:, a, :].rearrange("p (m t) -> p t m", t=PACK))
         wr_scale = wr_plane[:].bitcast(U8).rearrange("p (a w t m) -> p a w t m", a=2, w=2, t=PACK)
-        we_raw = [placed([P, PACK, R], F32, "wer_raw", 24576)]
+        we_raw = [placed([P, PACK, R], F32, "wer_raw", 4096)]
         nc.sync.dma_start(we_raw[0][:], wer.rearrange("(p i) r -> p i r", i=PACK))
 
         g2_rows = held([P, J], U8, "g2_rows")
         nc.vector.tensor_copy(g2_rows[:], v2_rows[:].bitcast(U8).indirect(list2[:]))
         for q in range(4):
             nc.sync.dma_start(g2_planes[32 * q : 32 * q + 4, :], g2_rows[96 + 8 * q : 96 + 8 * q + 8, :].bitcast(I32))
-        we_raw.append(placed([P, PACK, R], F32, "wei_raw", 0))
+        we_raw.append(placed([P, PACK, R], F32, "wei_raw", 4096 + 8192 + 16384))
         nc.sync.dma_start(we_raw[1][:], wei.rearrange("(p i) r -> p i r", i=PACK))
-        v_words = placed([P, T], I32, "v_words", 8192)
+        v_words = placed([P, T], I32, "v_words", 4096 + 8192)
         nc.sync.dma_start(v_words[:], tab_words[0].rearrange("p t i -> p (t i)").bitcast(I32))
-        g_rows = held([P, J], U8, "g_rows")
-        nc.vector.tensor_copy(g_rows[:], v_rows[:].bitcast(U8).indirect(list1[:]))
 
         g_words = {}
         g2_pairs = {}
@@ -121,10 +119,14 @@ def tile_list_ckg_bias_kernel(
                 g2_words[c][:].bitcast(U16), g2_pairs[c][:].bitcast(U16).rearrange("p (n d) -> p d n", d=2)
             )
 
-        for c in range(3):
+        gather_v2(0)
+        part_v2(0)
+        g_rows = held([P, J], U8, "g_rows", "g2_pairs0")
+        nc.vector.tensor_copy(g_rows[:], v_rows[:].bitcast(U8).indirect(list1[:]))
+        for c in range(1, 3):
             gather_v2(c)
             part_v2(c)
-        g_planes = held([P, J // 4], I32, "g_planes", "g2_pairs0")
+        g_planes = held([P, J // 4], I32, "g_planes", "g2_pairs1")
         nc.gpsimd.memset(g_planes[:], 0)
         for q in range(4):
             nc.sync.dma_start(g_planes[32 * q : 32 * q + 4, :], g_rows[112 + 4 * q : 112 + 4 * q + 4, :].bitcast(I32))
@@ -145,12 +147,14 @@ def tile_list_ckg_bias_kernel(
 
         def project_relation(i):
             c, u = divmod(i, CHUNK // TOK)
-            if i < REL_AHEAD:
-                relation[i] = placed([P, 2, TOK, PACK], F32, f"relation{i}", 4096 * i)
-            else:
-                relation[i] = ring.tile([P, 2, TOK, PACK], F32, name="relation", bufs=REL_AHEAD)
+            relation[i] = shared.tile(
+                [P, 3, TOK, PACK], F32, name="relation", bufs=REL_AHEAD, align_bytes=64, offset=4096 + 8192 + 16384
+            )
             for w in range(2):
-                bank = psum.tile([P, PACK, TOK], F32, name=f"rel{w}")
+                if i == 1:
+                    bank = psum.tile([P, PACK, TOK], F32, name="score", bufs=2)
+                else:
+                    bank = psum.tile([P, PACK, TOK], F32, name=f"rel{w}")
                 for t in range(PACK):
                     for a in range(2):
                         nc.tensor.matmul_mx(
@@ -162,7 +166,8 @@ def tile_list_ckg_bias_kernel(
                             start=(a == 0),
                             stop=(a == 1),
                         )
-                nc.scalar.copy(relation[i][:, w, :, :], bank[:].rearrange("p t n -> p n t"))
+                nc.scalar.copy(relation[i][:, 1 + w, :, :], bank[:].rearrange("p t n -> p n t"))
+            nc.scalar.mul(relation[i][:, 0, :, :], bank[:].rearrange("p t n -> p n t"), -1.0)
 
         def term(i, name, taken_over):
             if i in taken_over:
@@ -172,10 +177,12 @@ def tile_list_ckg_bias_kernel(
         def products(i):
             c, u = divmod(i, CHUNK // TOK)
             tok = slice(u * TOK, (u + 1) * TOK)
-            arr, ari = relation[i][:, 0, :, :], relation[i][:, 1, :, :]
             ent = []
             for w in range(2):
-                bank = psum.tile([P, PACK, TOK], F32, name=f"ent{w}", bufs=2)
+                if i == 0:
+                    bank = psum.tile([P, PACK, TOK], F32, name=f"rel{w}")
+                else:
+                    bank = psum.tile([P, PACK, TOK], F32, name=f"ent{w}", bufs=2)
                 for t in range(PACK):
                     nc.tensor.matmul_mx(
                         out=bank[:, t, :],
@@ -186,13 +193,11 @@ def tile_list_ckg_bias_kernel(
                         start=True,
                         stop=True,
                     )
-                ent.append(bank[:].rearrange("p t n -> p n t"))
+                ent.append(bank[:].rearrange("p t n -> p n t").unsqueeze(1).to_broadcast([P, 2, TOK, PACK]))
             first = term(i, "first", list(WORDS_AFTER.values()) + list(PAIRS_AFTER.values()))
             second = term(i, "second", [])
-            nc.vector.tensor_tensor(first[:, 0, :, :], ent[0], arr, MULT)
-            nc.vector.tensor_tensor(first[:, 1, :, :], ent[0], ari, MULT)
-            nc.vector.scalar_tensor_tensor(second[:, 0, :, :], ent[1], -1.0, ari, MULT, MULT)
-            nc.vector.tensor_tensor(second[:, 1, :, :], ent[1], arr, MULT)
+            nc.vector.tensor_tensor(first[:], ent[0], relation[i][:, 1:3, :, :], MULT)
+            nc.vector.tensor_tensor(second[:], ent[1], relation[i][:, 0:2, :, :], MULT)
             return first, second
 
         starts = [sum(GROUPS[:g]) for g in range(len(GROUPS))]
@@ -257,7 +262,7 @@ def tile_list_ckg_bias_kernel(
                 staged[:].rearrange("p (q j) -> p q j", q=4),
             )
 
-        n_words = placed([P, 2, N // 2], I32, "n_words", 24576)
+        n_words = placed([P, 2, N // 2], I32, "n_words", 4096)
         for w, src in enumerate((nr_words, ni_words)):
             nc.sync.dma_start(n_words[:, w, :], src[0].bitcast(I32))
         n_plane = held([P, 2, N // 4], I32, "n_plane", "we_bf1")

@@ -25,7 +25,7 @@ N_CHUNKS = J // CHUNK
 N_TILES = J // TOK
 GROUPS = [4, 4, 4, 1, 1, 1, 1]
 REL_AHEAD = 2
-WORDS_AFTER = {2: 4, 3: 8}
+WORDS_AFTER = {2: 2, 3: 8}
 PAIRS_AFTER = {3: 6}
 
 
@@ -131,7 +131,7 @@ def tile_list_ckg_bias_kernel(
         for q in range(4):
             nc.sync.dma_start(g_planes[32 * q : 32 * q + 4, :], g_rows[112 + 4 * q : 112 + 4 * q + 4, :].bitcast(I32))
 
-        we_bf = [held([P, PACK * R], BF16, f"we_bf{w}") for w in range(2)]
+        we_bf = [held([P, PACK * R], BF16, "we_bf0"), placed([P, PACK * R], BF16, "we_bf1", 4096 + 8192 + 16384 + 18432 - 3072)]
         we_words = [held([P, R], U32, f"we_words{w}") for w in range(2)]
         we_plane = [held([P, R], U8, f"we_plane{w}") for w in range(2)]
         for w in range(2):
@@ -148,7 +148,7 @@ def tile_list_ckg_bias_kernel(
         def project_relation(i):
             c, u = divmod(i, CHUNK // TOK)
             relation[i] = shared.tile(
-                [P, 3, TOK, PACK], F32, name="relation", bufs=REL_AHEAD, align_bytes=64, offset=4096 + 8192 + 16384
+                [P, 3, TOK, PACK], F32, name="relation", bufs=REL_AHEAD + 1, align_bytes=64, offset=4096 + 8192 + 16384
             )
             for w in range(2):
                 if i == 1:
@@ -172,17 +172,17 @@ def tile_list_ckg_bias_kernel(
         def term(i, name, taken_over):
             if i in taken_over:
                 return held([P, 2, TOK, PACK], F32, f"{name}{i}")
-            return ring.tile([P, 2, TOK, PACK], F32, name=name)
+            return ring.tile([P, 2, TOK, PACK], F32, name=name, bufs=6)
 
         def products(i):
             c, u = divmod(i, CHUNK // TOK)
             tok = slice(u * TOK, (u + 1) * TOK)
-            ent = []
-            for w in range(2):
+            ent = {}
+            for w in (0, 1) if i == 0 else (1, 0):
                 if i == 0:
                     bank = psum.tile([P, PACK, TOK], F32, name=f"rel{w}")
                 else:
-                    bank = psum.tile([P, PACK, TOK], F32, name=f"ent{w}", bufs=2)
+                    bank = psum.tile([P, PACK, TOK], F32, name=f"ent{i % 2}{(w + i // 2) % 2}")
                 for t in range(PACK):
                     nc.tensor.matmul_mx(
                         out=bank[:, t, :],
@@ -193,7 +193,7 @@ def tile_list_ckg_bias_kernel(
                         start=True,
                         stop=True,
                     )
-                ent.append(bank[:].rearrange("p t n -> p n t").unsqueeze(1).to_broadcast([P, 2, TOK, PACK]))
+                ent[w] = bank[:].rearrange("p t n -> p n t").unsqueeze(1).to_broadcast([P, 2, TOK, PACK])
             first = term(i, "first", list(WORDS_AFTER.values()) + list(PAIRS_AFTER.values()))
             second = term(i, "second", [])
             nc.vector.tensor_tensor(first[:], ent[0], relation[i][:, 1:3, :, :], MULT)
@@ -265,7 +265,7 @@ def tile_list_ckg_bias_kernel(
         n_words = placed([P, 2, N // 2], I32, "n_words", 4096)
         for w, src in enumerate((nr_words, ni_words)):
             nc.sync.dma_start(n_words[:, w, :], src[0].bitcast(I32))
-        n_plane = held([P, 2, N // 4], I32, "n_plane", "we_bf1")
+        n_plane = placed([P, 2, N // 4], I32, "n_plane", 4096 + 8192 + 16384 + 18432)
         nc.gpsimd.memset(n_plane[:], 0)
         for w, src in enumerate((nr_scales, ni_scales)):
             for q in range(4):
@@ -306,11 +306,11 @@ def tile_list_ckg_bias_kernel(
                     pending.extend([(g, None)] if GROUPS[g] == 1 else [(g, q) for q in range(4)])
             add_up(i, first, second)
             for c in range(N_CHUNKS):
-                if WORDS_AFTER.get(c) == i - 1:
-                    gather_v(c, f"first{i - 1}")
-                if PAIRS_AFTER.get(c) == i - 1:
-                    gather_v2(c, f"first{i - 1}")
+                if WORDS_AFTER.get(c) == i - 2:
+                    gather_v(c, f"first{i - 2}")
                 if PAIRS_AFTER.get(c) == i - 2:
+                    gather_v2(c, f"first{i - 2}")
+                if PAIRS_AFTER.get(c) == i - 3:
                     part_v2(c)
             if i + REL_AHEAD < N_TILES:
                 project_relation(i + REL_AHEAD)

@@ -25,8 +25,11 @@ N_CHUNKS = J // CHUNK
 N_TILES = J // TOK
 GROUPS = [4, 4, 4, 1, 1, 1, 1]
 REL_AHEAD = 2
-WORDS_AFTER = {2: 2, 3: 8}
-PAIRS_AFTER = {3: 6}
+HALVED = [2, 10]
+SHORT = [11, 14]
+SPLIT = 384
+WORDS_AFTER = {2: 2, 3: 6}
+PAIRS_AFTER = {3: 4}
 
 
 def tile_list_ckg_bias_kernel(
@@ -196,25 +199,41 @@ def tile_list_ckg_bias_kernel(
                 ent[w] = bank[:].rearrange("p t n -> p n t").unsqueeze(1).to_broadcast([P, 2, TOK, PACK])
             first = term(i, "first", list(WORDS_AFTER.values()) + list(PAIRS_AFTER.values()))
             second = term(i, "second", [])
-            nc.vector.tensor_tensor(first[:], ent[0], relation[i][:, 1:3, :, :], MULT)
-            nc.vector.tensor_tensor(second[:], ent[1], relation[i][:, 0:2, :, :], MULT)
+            for parts in [(0, 1), (1, 2)] if i == 0 else [(0, 2)]:
+                lo, hi = parts
+                nc.vector.tensor_tensor(first[:, lo:hi], ent[0][:, lo:hi], relation[i][:, 1 + lo : 1 + hi, :, :], MULT)
+                nc.vector.tensor_tensor(second[:, lo:hi], ent[1][:, lo:hi], relation[i][:, lo:hi, :, :], MULT)
             return first, second
 
         starts = [sum(GROUPS[:g]) for g in range(len(GROUPS))]
         group_of = [g for g, n in enumerate(GROUPS) for u in range(n)]
         h_bf = {}
         h_mx = {}
+        terms = {}
 
         def add_up(i, first, second):
+            whole = slice(0, TOK * PACK)
+            if i == 0:
+                add_part(nc.gpsimd, i, slice(0, 1), whole)
+                add_part(nc.gpsimd, i, slice(1, 2), whole)
+            elif i in HALVED:
+                add_part(nc.gpsimd, i, slice(0, 1), whole)
+            elif i in SHORT:
+                add_part(nc.gpsimd, i, slice(0, 2), slice(0, SPLIT))
+            elif i == N_TILES - 1:
+                add_part(nc.vector, i, slice(0, 2), whole)
+            else:
+                add_part(nc.gpsimd, i, slice(0, 2), whole)
+
+        def add_part(engine, i, parts, span):
             g = group_of[i]
-            u = i - starts[g]
-            if u == 0:
-                h_bf[g] = ring.tile([P, 2, GROUPS[g] * TOK * PACK], BF16, name="h_bf", align_bytes=64)
-            engine = nc.vector if i == N_TILES - 1 else nc.gpsimd
+            first, second = terms[i]
+            if g not in h_bf:
+                h_bf[g] = ring.tile([P, 2, GROUPS[g], TOK * PACK], BF16, name="h_bf", align_bytes=64)
             engine.tensor_tensor(
-                h_bf[g][:, :, u * TOK * PACK : (u + 1) * TOK * PACK],
-                first[:].rearrange("p w n t -> p w (n t)"),
-                second[:].rearrange("p w n t -> p w (n t)"),
+                h_bf[g][:, parts, i - starts[g], span],
+                first[:].rearrange("p w n t -> p w (n t)")[:, parts, span],
+                second[:].rearrange("p w n t -> p w (n t)")[:, parts, span],
                 ADD,
             )
 
@@ -223,7 +242,7 @@ def tile_list_ckg_bias_kernel(
             words = ring.tile([P, 2 * width], U32, name="h_words", align_bytes=64)
             plane = ring.tile([P, 2 * width], U8, name="h_plane", align_bytes=64)
             nc.vector.quantize_mx(
-                out=words[:].bitcast(FP8X4), scales=plane[:], in_=h_bf[g][:].rearrange("p w x -> p (w x)")
+                out=words[:].bitcast(FP8X4), scales=plane[:], in_=h_bf[g][:].rearrange("p w u x -> p (w u x)")
             )
             h_mx[g] = (words, plane)
 
@@ -299,6 +318,11 @@ def tile_list_ckg_bias_kernel(
         pending = []
         for i in range(N_TILES):
             first, second = products(i)
+            terms[i] = (first, second)
+            if i - 1 in HALVED:
+                add_part(nc.vector, i - 1, slice(1, 2), slice(0, TOK * PACK))
+            if i - 1 in SHORT:
+                add_part(nc.vector, i - 1, slice(0, 2), slice(SPLIT, TOK * PACK))
             for done in range(max(i - 2, 0), i - 1 if i < N_TILES - 1 else i):
                 g = group_of[done]
                 if done + 1 - starts[g] == GROUPS[g]:

@@ -25,11 +25,9 @@ N_CHUNKS = J // CHUNK
 N_TILES = J // TOK
 GROUPS = [4, 4, 4, 1, 1, 1, 1]
 REL_AHEAD = 2
-HALVED = [2, 10]
-SHORT = [11, 14]
-SPLIT = 384
+SPLIT = {2: 352, 6: 352, 10: 352, 11: 416, 14: 416}
 WORDS_AFTER = {2: 2, 3: 6}
-PAIRS_AFTER = {3: 4}
+PAIRS_AFTER = {}
 
 
 def tile_list_ckg_bias_kernel(
@@ -105,34 +103,27 @@ def tile_list_ckg_bias_kernel(
         nc.sync.dma_start(v_words[:], tab_words[0].rearrange("p t i -> p (t i)").bitcast(I32))
 
         g_words = {}
-        g2_pairs = {}
-        g2_words = {}
 
         def gather_v(c, tag=None):
             g_words[c] = held([P, CHUNK], U32, f"g_words{c}", tag)
             nc.vector.tensor_copy(g_words[c][:], v_words[:].bitcast(U32).indirect(cols(list1, c)))
 
-        def gather_v2(c, tag=None):
-            g2_pairs[c] = held([P, CHUNK], U32, f"g2_pairs{c}", tag)
-            nc.vector.tensor_copy(g2_pairs[c][:], v2_words[:].bitcast(U32).indirect(cols(list2, c)))
+        half = J // 2
+        g2_pairs = [held([P, half], U32, f"g2_pairs{h}") for h in range(2)]
+        g2_words = [held([P, 2, 2 * half], U8, f"g2_words{h}") for h in range(2)]
 
-        def part_v2(c):
-            g2_words[c] = held([P, 2, 2 * CHUNK], U8, f"g2_words{c}")
+        def part_v2(h):
             nc.vector.tensor_copy(
-                g2_words[c][:].bitcast(U16), g2_pairs[c][:].bitcast(U16).rearrange("p (n d) -> p d n", d=2)
+                g2_words[h][:].bitcast(U16), g2_pairs[h][:].bitcast(U16).rearrange("p (n d) -> p d n", d=2)
             )
 
-        gather_v2(0)
+        for h in range(2):
+            offsets = list2[:, h * (half // 16) : (h + 1) * (half // 16)]
+            nc.vector.tensor_copy(g2_pairs[h][:], v2_words[:].bitcast(U32).indirect(offsets))
         part_v2(0)
         g_rows = held([P, J], U8, "g_rows", "g2_pairs0")
         nc.vector.tensor_copy(g_rows[:], v_rows[:].bitcast(U8).indirect(list1[:]))
-        for c in range(1, 3):
-            gather_v2(c)
-            part_v2(c)
-        g_planes = held([P, J // 4], I32, "g_planes", "g2_pairs1")
-        nc.gpsimd.memset(g_planes[:], 0)
-        for q in range(4):
-            nc.sync.dma_start(g_planes[32 * q : 32 * q + 4, :], g_rows[112 + 4 * q : 112 + 4 * q + 4, :].bitcast(I32))
+        part_v2(1)
 
         we_bf = [held([P, PACK * R], BF16, "we_bf0"), placed([P, PACK * R], BF16, "we_bf1", 4096 + 8192 + 16384 + 18432 - 3072)]
         we_words = [held([P, R], U32, f"we_words{w}") for w in range(2)]
@@ -143,13 +134,17 @@ def tile_list_ckg_bias_kernel(
                 we_raw[w][:].rearrange("p i (m t) -> p m t i", t=PACK),
             )
             nc.vector.quantize_mx(out=we_words[w][:].bitcast(FP8X4), scales=we_plane[w][:], in_=we_bf[w][:])
+        g_planes = placed([P, J // 4], I32, "g_planes", 4096 + 2048)
+        nc.gpsimd.memset(g_planes[:], 0)
+        for q in range(4):
+            nc.sync.dma_start(g_planes[32 * q : 32 * q + 4, :], g_rows[112 + 4 * q : 112 + 4 * q + 4, :].bitcast(I32))
         gather_v(0)
         gather_v(1)
 
         relation = {}
 
         def project_relation(i):
-            c, u = divmod(i, CHUNK // TOK)
+            c, u = divmod(i, half // TOK)
             relation[i] = shared.tile(
                 [P, 3, TOK, PACK], F32, name="relation", bufs=REL_AHEAD + 1, align_bytes=64, offset=4096 + 8192 + 16384
             )
@@ -197,7 +192,7 @@ def tile_list_ckg_bias_kernel(
                         stop=True,
                     )
                 ent[w] = bank[:].rearrange("p t n -> p n t").unsqueeze(1).to_broadcast([P, 2, TOK, PACK])
-            first = term(i, "first", list(WORDS_AFTER.values()) + list(PAIRS_AFTER.values()))
+            first = term(i, "first", list(WORDS_AFTER.values()))
             second = term(i, "second", [])
             for parts in [(0, 1), (1, 2)] if i == 0 else [(0, 2)]:
                 lo, hi = parts
@@ -216,12 +211,8 @@ def tile_list_ckg_bias_kernel(
             if i == 0:
                 add_part(nc.gpsimd, i, slice(0, 1), whole)
                 add_part(nc.gpsimd, i, slice(1, 2), whole)
-            elif i in HALVED:
-                add_part(nc.gpsimd, i, slice(0, 1), whole)
-            elif i in SHORT:
-                add_part(nc.gpsimd, i, slice(0, 2), slice(0, SPLIT))
-            elif i == N_TILES - 1:
-                add_part(nc.vector, i, slice(0, 2), whole)
+            elif i in SPLIT:
+                add_part(nc.gpsimd, i, slice(0, 2), slice(0, SPLIT[i]))
             else:
                 add_part(nc.gpsimd, i, slice(0, 2), whole)
 
@@ -241,24 +232,32 @@ def tile_list_ckg_bias_kernel(
             width = GROUPS[g] * TOK
             words = ring.tile([P, 2 * width], U32, name="h_words", align_bytes=64)
             plane = ring.tile([P, 2 * width], U8, name="h_plane", align_bytes=64)
-            nc.vector.quantize_mx(
-                out=words[:].bitcast(FP8X4), scales=plane[:], in_=h_bf[g][:].rearrange("p w u x -> p (w u x)")
-            )
+            if g < len(GROUPS) - 1:
+                nc.vector.quantize_mx(
+                    out=words[:].bitcast(FP8X4), scales=plane[:], in_=h_bf[g][:].rearrange("p w u x -> p (w u x)")
+                )
+            else:
+                for w in range(2):
+                    span = slice(w * width, (w + 1) * width)
+                    nc.vector.quantize_mx(out=words[:, span].bitcast(FP8X4), scales=plane[:, span], in_=h_bf[g][:, w, 0, :])
             h_mx[g] = (words, plane)
 
         def score(g, q, bank):
+            for w in range(2):
+                one_pass(g, q, w, bank, w == 0, w == 1)
+
+        def one_pass(g, q, w, bank, start, stop):
             width = GROUPS[g] * TOK
             words, plane = h_mx[g]
-            for w in range(2):
-                nc.tensor.matmul_mx(
-                    out=bank,
-                    lhsT=n_words[:, w, q * P // 2 : (q + 1) * P // 2].bitcast(FP4X4),
-                    lhsT_scale=n_plane[:, w, :].bitcast(U8)[:, q * P : (q + 1) * P],
-                    rhs=words[:, w * width : (w + 1) * width].bitcast(FP8X4),
-                    rhs_scale=plane[:, w * width : (w + 1) * width],
-                    start=(w == 0),
-                    stop=(w == 1),
-                )
+            nc.tensor.matmul_mx(
+                out=bank,
+                lhsT=n_words[:, w, q * P // 2 : (q + 1) * P // 2].bitcast(FP4X4),
+                lhsT_scale=n_plane[:, w, :].bitcast(U8)[:, q * P : (q + 1) * P],
+                rhs=words[:, w * width : (w + 1) * width].bitcast(FP8X4),
+                rhs_scale=plane[:, w * width : (w + 1) * width],
+                start=start,
+                stop=stop,
+            )
 
         def score_wide(g, q):
             bank = psum.tile([P, CHUNK], F32, name="score", bufs=2)
@@ -294,18 +293,20 @@ def tile_list_ckg_bias_kernel(
             nc.sync.dma_start(bias[:], b.rearrange("(q p) -> p q", p=P))
 
         def score_last(g):
-            for half in range(2):
-                bank = psum.tile([P, CHUNK], F32, name=f"rel{half}")
+            banks = [psum.tile([P, CHUNK], F32, name=f"rel{half}") for half in range(2)]
+            for half, bank in enumerate(banks):
+                for u in range(2):
+                    one_pass(g, 2 * half + u, 0, bank[:, u * TOK : (u + 1) * TOK], u == 0, False)
+            for half, bank in enumerate(banks):
                 staged = ring.tile([P, CHUNK], F32, name="staged", bufs=4)
                 for u in range(2):
-                    score(g, 2 * half + u, bank[:, u * TOK : (u + 1) * TOK])
-                for u in range(2):
-                    q = 2 * half + u
-                    span = slice(u * TOK, (u + 1) * TOK)
-                    if half == 0:
-                        nc.scalar.activation(staged[:, span], bank[:, span], IDENTITY, bias=bias[:, q : q + 1])
-                    else:
-                        nc.vector.tensor_scalar(staged[:, span], bank[:, span], bias[:, q : q + 1], None, ADD)
+                    one_pass(g, 2 * half + u, 1, bank[:, u * TOK : (u + 1) * TOK], False, u == 1)
+                nc.vector.tensor_tensor(
+                    staged[:, 0 : 2 * TOK].rearrange("p (q j) -> p q j", q=2),
+                    bank[:, 0 : 2 * TOK].rearrange("p (q j) -> p q j", q=2),
+                    bias[:, 2 * half : 2 * half + 2].unsqueeze(2).to_broadcast([P, 2, TOK]),
+                    ADD,
+                )
                 nc.sync.dma_start(
                     out[2 * half * P : 2 * (half + 1) * P, starts[g] * TOK : (starts[g] + 1) * TOK].rearrange(
                         "(q p) j -> p q j", p=P
@@ -319,23 +320,21 @@ def tile_list_ckg_bias_kernel(
         for i in range(N_TILES):
             first, second = products(i)
             terms[i] = (first, second)
-            if i - 1 in HALVED:
-                add_part(nc.vector, i - 1, slice(1, 2), slice(0, TOK * PACK))
-            if i - 1 in SHORT:
-                add_part(nc.vector, i - 1, slice(0, 2), slice(SPLIT, TOK * PACK))
+            if i - 1 in SPLIT:
+                add_part(nc.vector, i - 1, slice(0, 2), slice(SPLIT[i - 1], TOK * PACK))
             for done in range(max(i - 2, 0), i - 1 if i < N_TILES - 1 else i):
                 g = group_of[done]
                 if done + 1 - starts[g] == GROUPS[g]:
                     quantise(g)
                     pending.extend([(g, None)] if GROUPS[g] == 1 else [(g, q) for q in range(4)])
-            add_up(i, first, second)
+            if i < N_TILES - 1:
+                add_up(i, first, second)
+            else:
+                for w in range(2):
+                    add_part(nc.vector, i, slice(w, w + 1), slice(0, TOK * PACK))
             for c in range(N_CHUNKS):
                 if WORDS_AFTER.get(c) == i - 2:
                     gather_v(c, f"first{i - 2}")
-                if PAIRS_AFTER.get(c) == i - 2:
-                    gather_v2(c, f"first{i - 2}")
-                if PAIRS_AFTER.get(c) == i - 3:
-                    part_v2(c)
             if i + REL_AHEAD < N_TILES:
                 project_relation(i + REL_AHEAD)
             take = len(pending) if i >= N_TILES - 3 else min(1, len(pending))

@@ -20,14 +20,29 @@ IDENTITY = mybir.ActivationFunctionType.Identity
 P = 128
 PACK = 4
 TOK = 128
+WIDTH = TOK * PACK
 CHUNK = 512
-N_CHUNKS = J // CHUNK
+HALF = J // 2
 N_TILES = J // TOK
+LAST = N_TILES - 1
 GROUPS = [4, 4, 4, 1, 1, 1, 1]
-REL_AHEAD = 2
-SPLIT = {2: 352, 6: 352, 10: 352, 11: 416, 14: 416}
+REL_AHEAD = 3
+TERM_BUFS = 6
 WORDS_AFTER = {2: 2, 3: 6}
-PAIRS_AFTER = {}
+SPLIT = {2: 352, 6: 352, 10: 352, 11: 416, 14: 416}
+
+RAW = PACK * R * 4
+SLOT = 3 * WIDTH * 4
+G2_PLANES_AT = 0
+WER_AT = 2 * J
+WR_ROWS_AT = WER_AT - R
+V_WORDS_AT = WER_AT + RAW
+WEI_AT = V_WORDS_AT + 4 * T
+V2_ROWS_AT = WEI_AT - T // 2
+RELATION_AT = WEI_AT
+WEI_BF_AT = RELATION_AT + 3 * SLOT - RAW // 4
+N_WORDS_AT = WER_AT
+G_PLANES_AT = WER_AT + 4 * N
 
 
 def tile_list_ckg_bias_kernel(
@@ -47,14 +62,14 @@ def tile_list_ckg_bias_kernel(
         def placed(shape, dtype, name, offset):
             return shared.tile(shape, dtype, name=name, align_bytes=64, offset=offset)
 
-        def cols(lst, c):
-            return lst[:, c * (CHUNK // 16) : (c + 1) * (CHUNK // 16)]
+        def entries(lst, c, n):
+            return lst[:, c * (n // 16) : (c + 1) * (n // 16)]
 
         list1 = keep.tile([P, J // 16], U16, name="list1")
         list2 = keep.tile([P, J // 16], U16, name="list2")
-        v2_rows = placed([P, T // 4], I32, "v2_rows", 4096 + 8192 + 14336)
+        v2_rows = placed([P, T // 4], I32, "v2_rows", V2_ROWS_AT)
         v_rows = held([P, T // 4], I32, "v_rows")
-        wr_rows = placed([P, 2, R // 4], I32, "wr_rows", 4096 - 512)
+        wr_rows = placed([P, 2, R // 4], I32, "wr_rows", WR_ROWS_AT)
         wr_plane = held([P, 4 * R // 4], I32, "wr_plane")
         nc.gpsimd.memset(v_rows[:], 0)
         nc.vector.memset(v2_rows[0:96, :], 0)
@@ -83,34 +98,33 @@ def tile_list_ckg_bias_kernel(
                 wr_plane[32 * q : 32 * q + 4, :],
                 wr_rows_t[96 + 8 * q : 96 + 8 * q + 8, :, :, :].rearrange("p w t m -> p (w t m)").bitcast(I32),
             )
-        g2_planes = placed([P, 2 * J // 4], I32, "g2_planes", 0)
+        g2_planes = placed([P, 2 * J // 4], I32, "g2_planes", G2_PLANES_AT)
         nc.gpsimd.memset(g2_planes[:], 0)
         wr_words = held([P, 2, 2, PACK, P], I32, "wr_words")
         for w in range(2):
             for a in range(2):
                 nc.gpsimd.tensor_copy(wr_words[:, w, a, :, :], wr_raw[w][:, a, :].rearrange("p (m t) -> p t m", t=PACK))
         wr_scale = wr_plane[:].bitcast(U8).rearrange("p (a w t m) -> p a w t m", a=2, w=2, t=PACK)
-        we_raw = [placed([P, PACK, R], F32, "wer_raw", 4096)]
+        we_raw = [placed([P, PACK, R], F32, "wer_raw", WER_AT)]
         nc.sync.dma_start(we_raw[0][:], wer.rearrange("(p i) r -> p i r", i=PACK))
 
         g2_rows = held([P, J], U8, "g2_rows")
         nc.vector.tensor_copy(g2_rows[:], v2_rows[:].bitcast(U8).indirect(list2[:]))
         for q in range(4):
             nc.sync.dma_start(g2_planes[32 * q : 32 * q + 4, :], g2_rows[96 + 8 * q : 96 + 8 * q + 8, :].bitcast(I32))
-        we_raw.append(placed([P, PACK, R], F32, "wei_raw", 4096 + 8192 + 16384))
+        we_raw.append(placed([P, PACK, R], F32, "wei_raw", WEI_AT))
         nc.sync.dma_start(we_raw[1][:], wei.rearrange("(p i) r -> p i r", i=PACK))
-        v_words = placed([P, T], I32, "v_words", 4096 + 8192)
+        v_words = placed([P, T], I32, "v_words", V_WORDS_AT)
         nc.sync.dma_start(v_words[:], tab_words[0].rearrange("p t i -> p (t i)").bitcast(I32))
 
         g_words = {}
 
         def gather_v(c, tag=None):
             g_words[c] = held([P, CHUNK], U32, f"g_words{c}", tag)
-            nc.vector.tensor_copy(g_words[c][:], v_words[:].bitcast(U32).indirect(cols(list1, c)))
+            nc.vector.tensor_copy(g_words[c][:], v_words[:].bitcast(U32).indirect(entries(list1, c, CHUNK)))
 
-        half = J // 2
-        g2_pairs = [held([P, half], U32, f"g2_pairs{h}") for h in range(2)]
-        g2_words = [held([P, 2, 2 * half], U8, f"g2_words{h}") for h in range(2)]
+        g2_pairs = [held([P, HALF], U32, f"g2_pairs{h}") for h in range(2)]
+        g2_words = [held([P, 2, 2 * HALF], U8, f"g2_words{h}") for h in range(2)]
 
         def part_v2(h):
             nc.vector.tensor_copy(
@@ -118,14 +132,13 @@ def tile_list_ckg_bias_kernel(
             )
 
         for h in range(2):
-            offsets = list2[:, h * (half // 16) : (h + 1) * (half // 16)]
-            nc.vector.tensor_copy(g2_pairs[h][:], v2_words[:].bitcast(U32).indirect(offsets))
+            nc.vector.tensor_copy(g2_pairs[h][:], v2_words[:].bitcast(U32).indirect(entries(list2, h, HALF)))
         part_v2(0)
         g_rows = held([P, J], U8, "g_rows", "g2_pairs0")
         nc.vector.tensor_copy(g_rows[:], v_rows[:].bitcast(U8).indirect(list1[:]))
         part_v2(1)
 
-        we_bf = [held([P, PACK * R], BF16, "we_bf0"), placed([P, PACK * R], BF16, "we_bf1", 4096 + 8192 + 16384 + 18432 - 3072)]
+        we_bf = [held([P, PACK * R], BF16, "we_bf0"), placed([P, PACK * R], BF16, "we_bf1", WEI_BF_AT)]
         we_words = [held([P, R], U32, f"we_words{w}") for w in range(2)]
         we_plane = [held([P, R], U8, f"we_plane{w}") for w in range(2)]
         for w in range(2):
@@ -134,7 +147,7 @@ def tile_list_ckg_bias_kernel(
                 we_raw[w][:].rearrange("p i (m t) -> p m t i", t=PACK),
             )
             nc.vector.quantize_mx(out=we_words[w][:].bitcast(FP8X4), scales=we_plane[w][:], in_=we_bf[w][:])
-        g_planes = placed([P, J // 4], I32, "g_planes", 4096 + 2048)
+        g_planes = placed([P, J // 4], I32, "g_planes", G_PLANES_AT)
         nc.gpsimd.memset(g_planes[:], 0)
         for q in range(4):
             nc.sync.dma_start(g_planes[32 * q : 32 * q + 4, :], g_rows[112 + 4 * q : 112 + 4 * q + 4, :].bitcast(I32))
@@ -144,13 +157,15 @@ def tile_list_ckg_bias_kernel(
         relation = {}
 
         def project_relation(i):
-            c, u = divmod(i, half // TOK)
+            h, u = divmod(i, HALF // TOK)
             relation[i] = shared.tile(
-                [P, 3, TOK, PACK], F32, name="relation", bufs=REL_AHEAD + 1, align_bytes=64, offset=4096 + 8192 + 16384
+                [P, 3, TOK, PACK], F32, name="relation", bufs=REL_AHEAD + 1, align_bytes=64, offset=RELATION_AT
             )
             for w in range(2):
                 if i == 1:
                     bank = psum.tile([P, PACK, TOK], F32, name="score", bufs=2)
+                elif i == 2:
+                    bank = psum.tile([P, PACK, TOK], F32, name=f"ent0{w}")
                 else:
                     bank = psum.tile([P, PACK, TOK], F32, name=f"rel{w}")
                 for t in range(PACK):
@@ -159,7 +174,7 @@ def tile_list_ckg_bias_kernel(
                             out=bank[:, t, :],
                             lhsT=wr_words[:, w, a, t, :].bitcast(FP8X4),
                             lhsT_scale=wr_scale[:, a, w, t, :],
-                            rhs=g2_words[c][:, a, 2 * u * TOK : 2 * (u + 1) * TOK].bitcast(FP4X4),
+                            rhs=g2_words[h][:, a, 2 * u * TOK : 2 * (u + 1) * TOK].bitcast(FP4X4),
                             rhs_scale=g2_planes[:].bitcast(U8)[:, a * J + i * TOK : a * J + (i + 1) * TOK],
                             start=(a == 0),
                             stop=(a == 1),
@@ -167,10 +182,7 @@ def tile_list_ckg_bias_kernel(
                 nc.scalar.copy(relation[i][:, 1 + w, :, :], bank[:].rearrange("p t n -> p n t"))
             nc.scalar.mul(relation[i][:, 0, :, :], bank[:].rearrange("p t n -> p n t"), -1.0)
 
-        def term(i, name, taken_over):
-            if i in taken_over:
-                return held([P, 2, TOK, PACK], F32, f"{name}{i}")
-            return ring.tile([P, 2, TOK, PACK], F32, name=name, bufs=6)
+        terms = {}
 
         def products(i):
             c, u = divmod(i, CHUNK // TOK)
@@ -192,35 +204,26 @@ def tile_list_ckg_bias_kernel(
                         stop=True,
                     )
                 ent[w] = bank[:].rearrange("p t n -> p n t").unsqueeze(1).to_broadcast([P, 2, TOK, PACK])
-            first = term(i, "first", list(WORDS_AFTER.values()))
-            second = term(i, "second", [])
-            for parts in [(0, 1), (1, 2)] if i == 0 else [(0, 2)]:
-                lo, hi = parts
+            if i in WORDS_AFTER.values():
+                first = held([P, 2, TOK, PACK], F32, f"first{i}")
+            else:
+                first = ring.tile([P, 2, TOK, PACK], F32, name="first", bufs=TERM_BUFS)
+            second = ring.tile([P, 2, TOK, PACK], F32, name="second", bufs=TERM_BUFS)
+            for lo, hi in [(0, 1), (1, 2)] if i == 0 else [(0, 2)]:
                 nc.vector.tensor_tensor(first[:, lo:hi], ent[0][:, lo:hi], relation[i][:, 1 + lo : 1 + hi, :, :], MULT)
                 nc.vector.tensor_tensor(second[:, lo:hi], ent[1][:, lo:hi], relation[i][:, lo:hi, :, :], MULT)
-            return first, second
+            terms[i] = (first, second)
 
         starts = [sum(GROUPS[:g]) for g in range(len(GROUPS))]
         group_of = [g for g, n in enumerate(GROUPS) for u in range(n)]
         h_bf = {}
         h_mx = {}
-        terms = {}
 
-        def add_up(i, first, second):
-            whole = slice(0, TOK * PACK)
-            if i == 0:
-                add_part(nc.gpsimd, i, slice(0, 1), whole)
-                add_part(nc.gpsimd, i, slice(1, 2), whole)
-            elif i in SPLIT:
-                add_part(nc.gpsimd, i, slice(0, 2), slice(0, SPLIT[i]))
-            else:
-                add_part(nc.gpsimd, i, slice(0, 2), whole)
-
-        def add_part(engine, i, parts, span):
+        def add(engine, i, parts, span):
             g = group_of[i]
             first, second = terms[i]
             if g not in h_bf:
-                h_bf[g] = ring.tile([P, 2, GROUPS[g], TOK * PACK], BF16, name="h_bf", align_bytes=64)
+                h_bf[g] = ring.tile([P, 2, GROUPS[g], WIDTH], BF16, name="h_bf", align_bytes=64)
             engine.tensor_tensor(
                 h_bf[g][:, parts, i - starts[g], span],
                 first[:].rearrange("p w n t -> p w (n t)")[:, parts, span],
@@ -232,14 +235,16 @@ def tile_list_ckg_bias_kernel(
             width = GROUPS[g] * TOK
             words = ring.tile([P, 2 * width], U32, name="h_words", align_bytes=64)
             plane = ring.tile([P, 2 * width], U8, name="h_plane", align_bytes=64)
-            if g < len(GROUPS) - 1:
+            if starts[g] < LAST:
                 nc.vector.quantize_mx(
                     out=words[:].bitcast(FP8X4), scales=plane[:], in_=h_bf[g][:].rearrange("p w u x -> p (w u x)")
                 )
             else:
                 for w in range(2):
                     span = slice(w * width, (w + 1) * width)
-                    nc.vector.quantize_mx(out=words[:, span].bitcast(FP8X4), scales=plane[:, span], in_=h_bf[g][:, w, 0, :])
+                    nc.vector.quantize_mx(
+                        out=words[:, span].bitcast(FP8X4), scales=plane[:, span], in_=h_bf[g][:, w, 0, :]
+                    )
             h_mx[g] = (words, plane)
 
         def score(g, q, bank):
@@ -280,10 +285,10 @@ def tile_list_ckg_bias_kernel(
                 staged[:].rearrange("p (q j) -> p q j", q=4),
             )
 
-        n_words = placed([P, 2, N // 2], I32, "n_words", 4096)
+        n_words = placed([P, 2, N // 2], I32, "n_words", N_WORDS_AT)
         for w, src in enumerate((nr_words, ni_words)):
             nc.sync.dma_start(n_words[:, w, :], src[0].bitcast(I32))
-        n_plane = placed([P, 2, N // 4], I32, "n_plane", 4096 + 8192 + 16384 + 18432)
+        n_plane = held([P, 2, N // 4], I32, "n_plane", "we_bf0")
         nc.gpsimd.memset(n_plane[:], 0)
         for w, src in enumerate((nr_scales, ni_scales)):
             for q in range(4):
@@ -293,47 +298,45 @@ def tile_list_ckg_bias_kernel(
             nc.sync.dma_start(bias[:], b.rearrange("(q p) -> p q", p=P))
 
         def score_last(g):
-            banks = [psum.tile([P, CHUNK], F32, name=f"rel{half}") for half in range(2)]
-            for half, bank in enumerate(banks):
+            banks = [psum.tile([P, CHUNK], F32, name=f"rel{pair}") for pair in range(2)]
+            for pair, bank in enumerate(banks):
                 for u in range(2):
-                    one_pass(g, 2 * half + u, 0, bank[:, u * TOK : (u + 1) * TOK], u == 0, False)
-            for half, bank in enumerate(banks):
+                    one_pass(g, 2 * pair + u, 0, bank[:, u * TOK : (u + 1) * TOK], u == 0, False)
+            for pair, bank in enumerate(banks):
                 staged = ring.tile([P, CHUNK], F32, name="staged", bufs=4)
                 for u in range(2):
-                    one_pass(g, 2 * half + u, 1, bank[:, u * TOK : (u + 1) * TOK], False, u == 1)
+                    one_pass(g, 2 * pair + u, 1, bank[:, u * TOK : (u + 1) * TOK], False, u == 1)
                 nc.vector.tensor_tensor(
                     staged[:, 0 : 2 * TOK].rearrange("p (q j) -> p q j", q=2),
                     bank[:, 0 : 2 * TOK].rearrange("p (q j) -> p q j", q=2),
-                    bias[:, 2 * half : 2 * half + 2].unsqueeze(2).to_broadcast([P, 2, TOK]),
+                    bias[:, 2 * pair : 2 * pair + 2].unsqueeze(2).to_broadcast([P, 2, TOK]),
                     ADD,
                 )
                 nc.sync.dma_start(
-                    out[2 * half * P : 2 * (half + 1) * P, starts[g] * TOK : (starts[g] + 1) * TOK].rearrange(
-                        "(q p) j -> p q j", p=P
-                    ),
+                    out[2 * pair * P : 2 * (pair + 1) * P, LAST * TOK : J].rearrange("(q p) j -> p q j", p=P),
                     staged[:, 0 : 2 * TOK].rearrange("p (q j) -> p q j", q=2),
                 )
 
         for i in range(REL_AHEAD):
             project_relation(i)
+        both = slice(0, 2)
         pending = []
         for i in range(N_TILES):
-            first, second = products(i)
-            terms[i] = (first, second)
+            products(i)
             if i - 1 in SPLIT:
-                add_part(nc.vector, i - 1, slice(0, 2), slice(SPLIT[i - 1], TOK * PACK))
-            for done in range(max(i - 2, 0), i - 1 if i < N_TILES - 1 else i):
+                add(nc.vector, i - 1, both, slice(SPLIT[i - 1], WIDTH))
+            for done in range(max(i - 2, 0), i - 1 if i < LAST else i):
                 g = group_of[done]
                 if done + 1 - starts[g] == GROUPS[g]:
                     quantise(g)
                     pending.extend([(g, None)] if GROUPS[g] == 1 else [(g, q) for q in range(4)])
-            if i < N_TILES - 1:
-                add_up(i, first, second)
-            else:
+            if i in (0, LAST):
                 for w in range(2):
-                    add_part(nc.vector, i, slice(w, w + 1), slice(0, TOK * PACK))
-            for c in range(N_CHUNKS):
-                if WORDS_AFTER.get(c) == i - 2:
+                    add(nc.gpsimd if i == 0 else nc.vector, i, slice(w, w + 1), slice(0, WIDTH))
+            else:
+                add(nc.gpsimd, i, both, slice(0, SPLIT.get(i, WIDTH)))
+            for c in WORDS_AFTER:
+                if WORDS_AFTER[c] == i - 2:
                     gather_v(c, f"first{i - 2}")
             if i + REL_AHEAD < N_TILES:
                 project_relation(i + REL_AHEAD)

@@ -33,16 +33,17 @@ SPLIT = {2: 352, 6: 352, 10: 352, 11: 416, 14: 416}
 
 RAW = PACK * R * 4
 SLOT = 3 * WIDTH * 4
-G2_PLANES_AT = 0
-WER_AT = 2 * J
-WR_ROWS_AT = WER_AT - R
-V_WORDS_AT = WER_AT + RAW
-WEI_AT = V_WORDS_AT + 4 * T
-V2_ROWS_AT = WEI_AT - T // 2
+EARLY = 512
+G2_EARLY_AT = 0
+WEI_AT = 2 * EARLY
+WR_ROWS_AT = WEI_AT - R
 RELATION_AT = WEI_AT
 WEI_BF_AT = RELATION_AT + 3 * SLOT - RAW // 4
+WER_AT = RELATION_AT + (REL_AHEAD + 1) * SLOT
 N_WORDS_AT = WER_AT
 G_PLANES_AT = WER_AT + 4 * N
+G2_LATE_AT = G_PLANES_AT + J
+V_WORDS_AT = WER_AT + RAW
 
 
 def tile_list_ckg_bias_kernel(
@@ -67,7 +68,7 @@ def tile_list_ckg_bias_kernel(
 
         list1 = keep.tile([P, J // 16], U16, name="list1")
         list2 = keep.tile([P, J // 16], U16, name="list2")
-        v2_rows = placed([P, T // 4], I32, "v2_rows", V2_ROWS_AT)
+        v2_rows = held([P, T // 4], I32, "v2_rows")
         v_rows = held([P, T // 4], I32, "v_rows")
         wr_rows = placed([P, 2, R // 4], I32, "wr_rows", WR_ROWS_AT)
         wr_plane = held([P, 4 * R // 4], I32, "wr_plane")
@@ -79,41 +80,46 @@ def tile_list_ckg_bias_kernel(
         nc.sync.dma_start(list2[:], offs2)
         nc.sync.dma_start(v2_rows[96:P, :], tab2_scales.rearrange("a g t -> g a t").bitcast(I32))
         for w, src in enumerate((wrr_scales, wri_scales)):
-            nc.scalar.dma_start(wr_rows[96:P, w, :], src.rearrange("a g c -> g a c").bitcast(I32))
-        nc.sync.dma_start(list1[:], offs)
+            for a in range(2):
+                nc.scalar.dma_start(
+                    wr_rows[96 + a : P : 2, w, :], src[a].rearrange("(q s) c -> s q c", s=4).bitcast(I32)
+                )
         v2_words = held([P, T], I32, "v2_words")
         nc.sync.dma_start(v2_words[:], tab2_words[0].rearrange("p t i -> p (t i)").bitcast(I32))
-        wr_raw = [held([P, 2, R], I32, f"wr_raw{w}") for w in range(2)]
+        wr_raw = [placed([P, 2, R], I32, "wrr_raw", V_WORDS_AT), held([P, 2, R], I32, "wri_raw")]
         for w, src in enumerate((wrr_words, wri_words)):
             nc.sync.dma_start(wr_raw[w][:], src.rearrange("a p r i -> p a (r i)").bitcast(I32))
-        nc.scalar.dma_start(v_rows[112:P, :], tab_scales[0].bitcast(I32))
+        we_raw = [placed([P, PACK, R], F32, "wer_raw", WER_AT)]
+        nc.sync.dma_start(we_raw[0][:], wer.rearrange("(p i) r -> p i r", i=PACK))
+        nc.sync.dma_start(list1[:], offs)
+        nc.gpsimd.dma_start(v_rows[112:P, :], tab_scales[0].bitcast(I32))
 
         wr_rows_t = held([P, 2, PACK, P], U8, "wr_rows_t")
         nc.gpsimd.tensor_copy(
             wr_rows_t[:],
             wr_rows[:].rearrange("p w c -> p (w c)").bitcast(U8).rearrange("p (w m t) -> p w t m", w=2, t=PACK),
         )
-        for q in range(4):
+        for s in range(4):
             nc.sync.dma_start(
-                wr_plane[32 * q : 32 * q + 4, :],
-                wr_rows_t[96 + 8 * q : 96 + 8 * q + 8, :, :, :].rearrange("p w t m -> p (w t m)").bitcast(I32),
+                wr_plane[s:P:32, :],
+                wr_rows_t[96 + 8 * s : 96 + 8 * s + 8, :, :, :].rearrange("p w t m -> p (w t m)").bitcast(I32),
             )
-        g2_planes = placed([P, 2 * J // 4], I32, "g2_planes", G2_PLANES_AT)
-        nc.gpsimd.memset(g2_planes[:], 0)
+        we_raw.append(placed([P, PACK, R], F32, "wei_raw", WEI_AT))
+        nc.sync.dma_start(we_raw[1][:], wei.rearrange("(p i) r -> p i r", i=PACK))
+        g2_early = placed([P, 2 * EARLY // 4], I32, "g2_early", G2_EARLY_AT)
+        nc.gpsimd.memset(g2_early[:], 0)
         wr_words = held([P, 2, 2, PACK, P], I32, "wr_words")
         for w in range(2):
             for a in range(2):
                 nc.gpsimd.tensor_copy(wr_words[:, w, a, :, :], wr_raw[w][:, a, :].rearrange("p (m t) -> p t m", t=PACK))
         wr_scale = wr_plane[:].bitcast(U8).rearrange("p (a w t m) -> p a w t m", a=2, w=2, t=PACK)
-        we_raw = [placed([P, PACK, R], F32, "wer_raw", WER_AT)]
-        nc.sync.dma_start(we_raw[0][:], wer.rearrange("(p i) r -> p i r", i=PACK))
 
         g2_rows = held([P, J], U8, "g2_rows")
         nc.vector.tensor_copy(g2_rows[:], v2_rows[:].bitcast(U8).indirect(list2[:]))
         for q in range(4):
-            nc.sync.dma_start(g2_planes[32 * q : 32 * q + 4, :], g2_rows[96 + 8 * q : 96 + 8 * q + 8, :].bitcast(I32))
-        we_raw.append(placed([P, PACK, R], F32, "wei_raw", WEI_AT))
-        nc.sync.dma_start(we_raw[1][:], wei.rearrange("(p i) r -> p i r", i=PACK))
+            nc.sync.dma_start(
+                g2_early[32 * q : 32 * q + 4, :], g2_rows[96 + 8 * q : 96 + 8 * q + 8, 0:EARLY].bitcast(I32)
+            )
         v_words = placed([P, T], I32, "v_words", V_WORDS_AT)
         nc.sync.dma_start(v_words[:], tab_words[0].rearrange("p t i -> p (t i)").bitcast(I32))
 
@@ -149,8 +155,19 @@ def tile_list_ckg_bias_kernel(
             nc.vector.quantize_mx(out=we_words[w][:].bitcast(FP8X4), scales=we_plane[w][:], in_=we_bf[w][:])
         g_planes = placed([P, J // 4], I32, "g_planes", G_PLANES_AT)
         nc.gpsimd.memset(g_planes[:], 0)
+        for s in range(4):
+            nc.sync.dma_start(g_planes[s:P:32, :], g_rows[112 + s : P : 4, :].bitcast(I32))
+        g2_late = placed([P, 2 * (J - EARLY) // 4], I32, "g2_late", G2_LATE_AT)
+        nc.gpsimd.memset(g2_late[:], 0)
         for q in range(4):
-            nc.sync.dma_start(g_planes[32 * q : 32 * q + 4, :], g_rows[112 + 4 * q : 112 + 4 * q + 4, :].bitcast(I32))
+            nc.sync.dma_start(
+                g2_late[32 * q : 32 * q + 4, :], g2_rows[96 + 8 * q : 96 + 8 * q + 8, EARLY:J].bitcast(I32)
+            )
+
+        def g2_scale(a, i):
+            plane, width, at = (g2_early, EARLY, i * TOK) if i * TOK < EARLY else (g2_late, J - EARLY, i * TOK - EARLY)
+            return plane[:].bitcast(U8)[:, a * width + at : a * width + at + TOK]
+
         gather_v(0)
         gather_v(1)
 
@@ -175,7 +192,7 @@ def tile_list_ckg_bias_kernel(
                             lhsT=wr_words[:, w, a, t, :].bitcast(FP8X4),
                             lhsT_scale=wr_scale[:, a, w, t, :],
                             rhs=g2_words[h][:, a, 2 * u * TOK : 2 * (u + 1) * TOK].bitcast(FP4X4),
-                            rhs_scale=g2_planes[:].bitcast(U8)[:, a * J + i * TOK : a * J + (i + 1) * TOK],
+                            rhs_scale=g2_scale(a, i),
                             start=(a == 0),
                             stop=(a == 1),
                         )

@@ -34,16 +34,14 @@ SPLIT = {2: 352, 6: 352, 10: 352, 11: 416, 14: 416}
 RAW = PACK * R * 4
 SLOT = 3 * WIDTH * 4
 EARLY = 512
-G2_EARLY_AT = 0
-WEI_AT = 2 * EARLY
-WR_ROWS_AT = WEI_AT - R
+WEI_AT = 0
+WR_ROWS_AT = WEI_AT
 RELATION_AT = WEI_AT
 WEI_BF_AT = RELATION_AT + 3 * SLOT - RAW // 4
 WER_AT = RELATION_AT + (REL_AHEAD + 1) * SLOT
 N_WORDS_AT = WER_AT
 G_PLANES_AT = WER_AT + 4 * N
 G2_LATE_AT = G_PLANES_AT + J
-V_WORDS_AT = WER_AT + RAW
 
 
 def tile_list_ckg_bias_kernel(
@@ -80,38 +78,36 @@ def tile_list_ckg_bias_kernel(
         nc.sync.dma_start(list2[:], offs2)
         nc.sync.dma_start(v2_rows[96:P, :], tab2_scales.rearrange("a g t -> g a t").bitcast(I32))
         for w, src in enumerate((wrr_scales, wri_scales)):
-            for a in range(2):
-                nc.scalar.dma_start(
-                    wr_rows[96 + a : P : 2, w, :], src[a].rearrange("(q s) c -> s q c", s=4).bitcast(I32)
-                )
+            nc.scalar.dma_start(wr_rows[96:P, w, :], src.rearrange("a g c -> g a c").bitcast(I32))
         v2_words = held([P, T], I32, "v2_words")
         nc.sync.dma_start(v2_words[:], tab2_words[0].rearrange("p t i -> p (t i)").bitcast(I32))
-        wr_raw = [placed([P, 2, R], I32, "wrr_raw", V_WORDS_AT), held([P, 2, R], I32, "wri_raw")]
+        wr_raw = [held([P, 2, R], I32, f"wr_raw{w}") for w in range(2)]
         for w, src in enumerate((wrr_words, wri_words)):
             nc.sync.dma_start(wr_raw[w][:], src.rearrange("a p r i -> p a (r i)").bitcast(I32))
         we_raw = [placed([P, PACK, R], F32, "wer_raw", WER_AT)]
         nc.sync.dma_start(we_raw[0][:], wer.rearrange("(p i) r -> p i r", i=PACK))
         nc.sync.dma_start(list1[:], offs)
-        nc.gpsimd.dma_start(v_rows[112:P, :], tab_scales[0].bitcast(I32))
+        nc.scalar.dma_start(v_rows[112:P, :], tab_scales[0].bitcast(I32))
 
         wr_rows_t = held([P, 2, PACK, P], U8, "wr_rows_t")
-        nc.gpsimd.tensor_copy(
+        nc.vector.tensor_copy(
             wr_rows_t[:],
             wr_rows[:].rearrange("p w c -> p (w c)").bitcast(U8).rearrange("p (w m t) -> p w t m", w=2, t=PACK),
         )
-        for s in range(4):
+        for q in range(4):
             nc.sync.dma_start(
-                wr_plane[s:P:32, :],
-                wr_rows_t[96 + 8 * s : 96 + 8 * s + 8, :, :, :].rearrange("p w t m -> p (w t m)").bitcast(I32),
+                wr_plane[32 * q : 32 * q + 4, :],
+                wr_rows_t[96 + 8 * q : 96 + 8 * q + 8, :, :, :].rearrange("p w t m -> p (w t m)").bitcast(I32),
             )
         we_raw.append(placed([P, PACK, R], F32, "wei_raw", WEI_AT))
         nc.sync.dma_start(we_raw[1][:], wei.rearrange("(p i) r -> p i r", i=PACK))
-        g2_early = placed([P, 2 * EARLY // 4], I32, "g2_early", G2_EARLY_AT)
+        g2_early = held([P, 2 * EARLY // 4], I32, "g2_early")
         nc.gpsimd.memset(g2_early[:], 0)
-        wr_words = held([P, 2, 2, PACK, P], I32, "wr_words")
+        wr_words = held([P, 2, 2, PACK, P], U32, "wr_words")
         for w in range(2):
-            for a in range(2):
-                nc.gpsimd.tensor_copy(wr_words[:, w, a, :, :], wr_raw[w][:, a, :].rearrange("p (m t) -> p t m", t=PACK))
+            nc.scalar.copy(
+                wr_words[:, w, :, :, :], wr_raw[w][:].bitcast(U32).rearrange("p a (m t) -> p a t m", t=PACK)
+            )
         wr_scale = wr_plane[:].bitcast(U8).rearrange("p (a w t m) -> p a w t m", a=2, w=2, t=PACK)
 
         g2_rows = held([P, J], U8, "g2_rows")
@@ -120,8 +116,6 @@ def tile_list_ckg_bias_kernel(
             nc.sync.dma_start(
                 g2_early[32 * q : 32 * q + 4, :], g2_rows[96 + 8 * q : 96 + 8 * q + 8, 0:EARLY].bitcast(I32)
             )
-        v_words = placed([P, T], I32, "v_words", V_WORDS_AT)
-        nc.sync.dma_start(v_words[:], tab_words[0].rearrange("p t i -> p (t i)").bitcast(I32))
 
         g_words = {}
 
@@ -139,6 +133,8 @@ def tile_list_ckg_bias_kernel(
 
         for h in range(2):
             nc.vector.tensor_copy(g2_pairs[h][:], v2_words[:].bitcast(U32).indirect(entries(list2, h, HALF)))
+        v_words = held([P, T], I32, "v_words", "v2_words")
+        nc.sync.dma_start(v_words[:], tab_words[0].rearrange("p t i -> p (t i)").bitcast(I32))
         part_v2(0)
         g_rows = held([P, J], U8, "g_rows", "g2_pairs0")
         nc.vector.tensor_copy(g_rows[:], v_rows[:].bitcast(U8).indirect(list1[:]))
@@ -155,8 +151,8 @@ def tile_list_ckg_bias_kernel(
             nc.vector.quantize_mx(out=we_words[w][:].bitcast(FP8X4), scales=we_plane[w][:], in_=we_bf[w][:])
         g_planes = placed([P, J // 4], I32, "g_planes", G_PLANES_AT)
         nc.gpsimd.memset(g_planes[:], 0)
-        for s in range(4):
-            nc.sync.dma_start(g_planes[s:P:32, :], g_rows[112 + s : P : 4, :].bitcast(I32))
+        for q in range(4):
+            nc.sync.dma_start(g_planes[32 * q : 32 * q + 4, :], g_rows[112 + 4 * q : 112 + 4 * q + 4, :].bitcast(I32))
         g2_late = placed([P, 2 * (J - EARLY) // 4], I32, "g2_late", G2_LATE_AT)
         nc.gpsimd.memset(g2_late[:], 0)
         for q in range(4):

@@ -28,8 +28,9 @@ LAST = N_TILES - 1
 GROUPS = [4, 4, 4, 1, 1, 1, 1]
 REL_AHEAD = 3
 TERM_BUFS = 6
-WORDS_AFTER = {2: 2, 3: 6}
-SPLIT = {2: 352, 6: 352, 10: 352, 11: 416, 14: 416}
+GATHERS = [(0, 2), (2, 4), (6, 4), (10, 4), (14, 2)]
+WORDS_AFTER = {2: 2, 3: 6, 4: 10}
+SPLIT = {10: 352, 14: 416}
 
 RAW = PACK * R * 4
 SLOT = 3 * WIDTH * 4
@@ -41,7 +42,6 @@ WEI_BF_AT = RELATION_AT + 3 * SLOT - RAW // 4
 WER_AT = RELATION_AT + (REL_AHEAD + 1) * SLOT
 N_WORDS_AT = WER_AT
 G_PLANES_AT = WER_AT + 4 * N
-G2_LATE_AT = G_PLANES_AT + J
 
 
 def tile_list_ckg_bias_kernel(
@@ -103,6 +103,8 @@ def tile_list_ckg_bias_kernel(
         nc.sync.dma_start(we_raw[1][:], wei.rearrange("(p i) r -> p i r", i=PACK))
         g2_early = held([P, 2 * EARLY // 4], I32, "g2_early")
         nc.gpsimd.memset(g2_early[:], 0)
+        g_early = held([P, EARLY // 4], I32, "g_early")
+        nc.gpsimd.memset(g_early[:], 0)
         wr_words = held([P, 2, 2, PACK, P], U32, "wr_words")
         for w in range(2):
             nc.scalar.copy(
@@ -120,8 +122,12 @@ def tile_list_ckg_bias_kernel(
         g_words = {}
 
         def gather_v(c, tag=None):
-            g_words[c] = held([P, CHUNK], U32, f"g_words{c}", tag)
-            nc.vector.tensor_copy(g_words[c][:], v_words[:].bitcast(U32).indirect(entries(list1, c, CHUNK)))
+            at, tiles = GATHERS[c]
+            words = held([P, tiles * TOK], U32, f"g_words{c}", tag)
+            offsets = list1[:, at * TOK // 16 : (at + tiles) * TOK // 16]
+            nc.vector.tensor_copy(words[:], v_words[:].bitcast(U32).indirect(offsets))
+            for u in range(tiles):
+                g_words[at + u] = words[:, u * TOK : (u + 1) * TOK]
 
         g2_pairs = [held([P, HALF], U32, f"g2_pairs{h}") for h in range(2)]
         g2_words = [held([P, 2, 2 * HALF], U8, f"g2_words{h}") for h in range(2)]
@@ -149,16 +155,26 @@ def tile_list_ckg_bias_kernel(
                 we_raw[w][:].rearrange("p i (m t) -> p m t i", t=PACK),
             )
             nc.vector.quantize_mx(out=we_words[w][:].bitcast(FP8X4), scales=we_plane[w][:], in_=we_bf[w][:])
-        g_planes = placed([P, J // 4], I32, "g_planes", G_PLANES_AT)
-        nc.gpsimd.memset(g_planes[:], 0)
         for q in range(4):
-            nc.sync.dma_start(g_planes[32 * q : 32 * q + 4, :], g_rows[112 + 4 * q : 112 + 4 * q + 4, :].bitcast(I32))
-        g2_late = placed([P, 2 * (J - EARLY) // 4], I32, "g2_late", G2_LATE_AT)
+            nc.sync.dma_start(
+                g_early[32 * q : 32 * q + 4, :], g_rows[112 + 4 * q : 112 + 4 * q + 4, 0:EARLY].bitcast(I32)
+            )
+        g2_late = held([P, 2 * (J - EARLY) // 4], I32, "g2_late", "wr_raw1")
         nc.gpsimd.memset(g2_late[:], 0)
         for q in range(4):
             nc.sync.dma_start(
                 g2_late[32 * q : 32 * q + 4, :], g2_rows[96 + 8 * q : 96 + 8 * q + 8, EARLY:J].bitcast(I32)
             )
+        g_late = placed([P, (J - EARLY) // 4], I32, "g_late", G_PLANES_AT)
+        nc.gpsimd.memset(g_late[:], 0)
+        for q in range(4):
+            nc.sync.dma_start(
+                g_late[32 * q : 32 * q + 4, :], g_rows[112 + 4 * q : 112 + 4 * q + 4, EARLY:J].bitcast(I32)
+            )
+
+        def g_scale(i):
+            plane, at = (g_early, i * TOK) if i * TOK < EARLY else (g_late, i * TOK - EARLY)
+            return plane[:].bitcast(U8)[:, at : at + TOK]
 
         def g2_scale(a, i):
             plane, width, at = (g2_early, EARLY, i * TOK) if i * TOK < EARLY else (g2_late, J - EARLY, i * TOK - EARLY)
@@ -174,11 +190,9 @@ def tile_list_ckg_bias_kernel(
             relation[i] = shared.tile(
                 [P, 3, TOK, PACK], F32, name="relation", bufs=REL_AHEAD + 1, align_bytes=64, offset=RELATION_AT
             )
-            for w in range(2):
-                if i == 1:
-                    bank = psum.tile([P, PACK, TOK], F32, name="score", bufs=2)
-                elif i == 2:
-                    bank = psum.tile([P, PACK, TOK], F32, name=f"ent0{w}")
+            for w in (1, 0):
+                if i in (1, 2):
+                    bank = psum.tile([P, PACK, TOK], F32, name=f"ent{i % 2}{w}")
                 else:
                     bank = psum.tile([P, PACK, TOK], F32, name=f"rel{w}")
                 for t in range(PACK):
@@ -193,13 +207,11 @@ def tile_list_ckg_bias_kernel(
                             stop=(a == 1),
                         )
                 nc.scalar.copy(relation[i][:, 1 + w, :, :], bank[:].rearrange("p t n -> p n t"))
-            nc.scalar.mul(relation[i][:, 0, :, :], bank[:].rearrange("p t n -> p n t"), -1.0)
+            nc.scalar.mul(relation[i][:, 0, :, :], relation[i][:, 2, :, :], -1.0)
 
         terms = {}
 
         def products(i):
-            c, u = divmod(i, CHUNK // TOK)
-            tok = slice(u * TOK, (u + 1) * TOK)
             ent = {}
             for w in (0, 1) if i == 0 else (1, 0):
                 if i == 0:
@@ -211,8 +223,8 @@ def tile_list_ckg_bias_kernel(
                         out=bank[:, t, :],
                         lhsT=we_words[w][:, t * P : (t + 1) * P].bitcast(FP8X4),
                         lhsT_scale=we_plane[w][:, t * P : (t + 1) * P],
-                        rhs=g_words[c][:, tok].bitcast(FP8X4),
-                        rhs_scale=g_planes[:].bitcast(U8)[:, i * TOK : (i + 1) * TOK],
+                        rhs=g_words[i].bitcast(FP8X4),
+                        rhs_scale=g_scale(i),
                         start=True,
                         stop=True,
                     )

@@ -90,7 +90,7 @@ def tile_list_ckg_bias_kernel(
         nc.scalar.dma_start(v_rows[112:P, :], tab_scales[0].bitcast(I32))
 
         wr_rows_t = held([P, 2, PACK, P], U8, "wr_rows_t")
-        nc.vector.tensor_copy(
+        nc.gpsimd.tensor_copy(
             wr_rows_t[:],
             wr_rows[:].rearrange("p w c -> p (w c)").bitcast(U8).rearrange("p (w m t) -> p w t m", w=2, t=PACK),
         )
@@ -234,9 +234,8 @@ def tile_list_ckg_bias_kernel(
             else:
                 first = ring.tile([P, 2, TOK, PACK], F32, name="first", bufs=TERM_BUFS)
             second = ring.tile([P, 2, TOK, PACK], F32, name="second", bufs=TERM_BUFS)
-            for lo, hi in [(0, 1), (1, 2)] if i == 0 else [(0, 2)]:
-                nc.vector.tensor_tensor(first[:, lo:hi], ent[0][:, lo:hi], relation[i][:, 1 + lo : 1 + hi, :, :], MULT)
-                nc.vector.tensor_tensor(second[:, lo:hi], ent[1][:, lo:hi], relation[i][:, lo:hi, :, :], MULT)
+            nc.vector.tensor_tensor(first[:], ent[0], relation[i][:, 1:3, :, :], MULT)
+            nc.vector.tensor_tensor(second[:], ent[1], relation[i][:, 0:2, :, :], MULT)
             terms[i] = (first, second)
 
         starts = [sum(GROUPS[:g]) for g in range(len(GROUPS))]
@@ -323,19 +322,19 @@ def tile_list_ckg_bias_kernel(
             nc.sync.dma_start(bias[:], b.rearrange("(q p) -> p q", p=P))
 
         def score_last(g):
-            banks = [psum.tile([P, CHUNK], F32, name=f"rel{pair}") for pair in range(2)]
-            for pair, bank in enumerate(banks):
-                for u in range(2):
-                    one_pass(g, 2 * pair + u, 0, bank[:, u * TOK : (u + 1) * TOK], u == 0, False)
-            for pair, bank in enumerate(banks):
+            banks = [psum.tile([P, CHUNK], F32, name=name) for name in ("rel0", "rel1", "ent00", "ent01")]
+            for q, bank in enumerate(banks):
+                one_pass(g, q, 0, bank[:, 0:TOK], True, False)
+            for pair in range(2):
                 staged = ring.tile([P, CHUNK], F32, name="staged", bufs=4)
-                for u in range(2):
-                    one_pass(g, 2 * pair + u, 1, bank[:, u * TOK : (u + 1) * TOK], False, u == 1)
-                nc.vector.tensor_tensor(
-                    staged[:, 0 : 2 * TOK].rearrange("p (q j) -> p q j", q=2),
-                    bank[:, 0 : 2 * TOK].rearrange("p (q j) -> p q j", q=2),
-                    bias[:, 2 * pair : 2 * pair + 2].unsqueeze(2).to_broadcast([P, 2, TOK]),
-                    ADD,
+                by_vector, by_scalar = 2 * pair, 2 * pair + 1
+                for q in (by_vector, by_scalar):
+                    one_pass(g, q, 1, banks[q][:, 0:TOK], False, True)
+                nc.vector.tensor_scalar_add(
+                    staged[:, 0:TOK], banks[by_vector][:, 0:TOK], bias[:, by_vector : by_vector + 1]
+                )
+                nc.scalar.activation(
+                    staged[:, TOK : 2 * TOK], banks[by_scalar][:, 0:TOK], IDENTITY, bias=bias[:, by_scalar : by_scalar + 1]
                 )
                 nc.sync.dma_start(
                     out[2 * pair * P : 2 * (pair + 1) * P, LAST * TOK : J].rearrange("(q p) j -> p q j", p=P),
@@ -355,9 +354,9 @@ def tile_list_ckg_bias_kernel(
                 if done + 1 - starts[g] == GROUPS[g]:
                     quantise(g)
                     pending.extend([(g, None)] if GROUPS[g] == 1 else [(g, q) for q in range(4)])
-            if i in (0, LAST):
+            if i == LAST:
                 for w in range(2):
-                    add(nc.gpsimd if i == 0 else nc.vector, i, slice(w, w + 1), slice(0, WIDTH))
+                    add(nc.vector, i, slice(w, w + 1), slice(0, WIDTH))
             else:
                 add(nc.gpsimd, i, both, slice(0, SPLIT.get(i, WIDTH)))
             for c in WORDS_AFTER:

@@ -27,6 +27,7 @@ N_TILES = J // TOK
 LAST = N_TILES - 1
 GROUPS = [4, 4, 4, 1, 1, 1, 1]
 REL_AHEAD = 3
+STAGED_BUFS = 8
 TERM_BUFS = 6
 GATHERS = [(0, 2), (2, 4), (6, 4), (10, 4), (14, 2)]
 WORDS_AFTER = {2: 2, 3: 6, 4: 10}
@@ -42,6 +43,8 @@ WEI_BF_AT = RELATION_AT + 3 * SLOT - RAW // 4
 WER_AT = RELATION_AT + (REL_AHEAD + 1) * SLOT
 N_WORDS_AT = WER_AT
 G_PLANES_AT = WER_AT + 4 * N
+G2_LATE_AT = G_PLANES_AT + J - EARLY
+N_PLANE_AT = G2_LATE_AT + 2 * (J - EARLY)
 
 
 def tile_list_ckg_bias_kernel(
@@ -159,7 +162,7 @@ def tile_list_ckg_bias_kernel(
             nc.sync.dma_start(
                 g_early[32 * q : 32 * q + 4, :], g_rows[112 + 4 * q : 112 + 4 * q + 4, 0:EARLY].bitcast(I32)
             )
-        g2_late = held([P, 2 * (J - EARLY) // 4], I32, "g2_late", "wr_raw1")
+        g2_late = placed([P, 2 * (J - EARLY) // 4], I32, "g2_late", G2_LATE_AT)
         nc.gpsimd.memset(g2_late[:], 0)
         for q in range(4):
             nc.sync.dma_start(
@@ -290,14 +293,14 @@ def tile_list_ckg_bias_kernel(
 
         def score_wide(g, q):
             bank = psum.tile([P, CHUNK], F32, name="score", bufs=2)
-            staged = ring.tile([P, CHUNK], F32, name="staged", bufs=4)
+            staged = ring.tile([P, CHUNK], F32, name="staged", bufs=STAGED_BUFS)
             score(g, q, bank[:])
             nc.scalar.activation(staged[:], bank[:], IDENTITY, bias=bias[:, q : q + 1])
             nc.sync.dma_start(out[q * P : (q + 1) * P, starts[g] * TOK : starts[g] * TOK + CHUNK], staged[:])
 
         def score_narrow(g):
             bank = psum.tile([P, CHUNK], F32, name="score", bufs=2)
-            staged = ring.tile([P, CHUNK], F32, name="staged", bufs=4)
+            staged = ring.tile([P, CHUNK], F32, name="staged", bufs=STAGED_BUFS)
             for q in range(4):
                 score(g, q, bank[:, q * TOK : (q + 1) * TOK])
             for q in range(4):
@@ -312,7 +315,7 @@ def tile_list_ckg_bias_kernel(
         n_words = placed([P, 2, N // 2], I32, "n_words", N_WORDS_AT)
         for w, src in enumerate((nr_words, ni_words)):
             nc.sync.dma_start(n_words[:, w, :], src[0].bitcast(I32))
-        n_plane = held([P, 2, N // 4], I32, "n_plane", "we_bf0")
+        n_plane = placed([P, 2, N // 4], I32, "n_plane", N_PLANE_AT)
         nc.gpsimd.memset(n_plane[:], 0)
         for w, src in enumerate((nr_scales, ni_scales)):
             for q in range(4):
@@ -326,7 +329,7 @@ def tile_list_ckg_bias_kernel(
             for q, bank in enumerate(banks):
                 one_pass(g, q, 0, bank[:, 0:TOK], True, False)
             for pair in range(2):
-                staged = ring.tile([P, CHUNK], F32, name="staged", bufs=4)
+                staged = ring.tile([P, CHUNK], F32, name="staged", bufs=STAGED_BUFS)
                 by_vector, by_scalar = 2 * pair, 2 * pair + 1
                 for q in (by_vector, by_scalar):
                     one_pass(g, q, 1, banks[q][:, 0:TOK], False, True)

@@ -81,7 +81,10 @@ def tile_list_ckg_bias_kernel(
         nc.sync.dma_start(list2[:], offs2)
         nc.sync.dma_start(v2_rows[96:P, :], tab2_scales.rearrange("a g t -> g a t").bitcast(I32))
         for w, src in enumerate((wrr_scales, wri_scales)):
-            nc.scalar.dma_start(wr_rows[96:P, w, :], src.rearrange("a g c -> g a c").bitcast(I32))
+            for a in range(2):
+                nc.scalar.dma_start(
+                    wr_rows[96 + a : P : 2, w, :], src[a].rearrange("(q s) c -> s q c", s=4).bitcast(I32)
+                )
         v2_words = held([P, T], I32, "v2_words")
         nc.sync.dma_start(v2_words[:], tab2_words[0].rearrange("p t i -> p (t i)").bitcast(I32))
         wr_raw = [held([P, 2, R], I32, f"wr_raw{w}") for w in range(2)]
@@ -90,17 +93,17 @@ def tile_list_ckg_bias_kernel(
         we_raw = [placed([P, PACK, R], F32, "wer_raw", WER_AT)]
         nc.sync.dma_start(we_raw[0][:], wer.rearrange("(p i) r -> p i r", i=PACK))
         nc.sync.dma_start(list1[:], offs)
-        nc.scalar.dma_start(v_rows[112:P, :], tab_scales[0].bitcast(I32))
+        nc.scalar.dma_start(v_rows[32:96:4, :], tab_scales[0].bitcast(I32))
 
         wr_rows_t = held([P, 2, PACK, P], U8, "wr_rows_t")
         nc.gpsimd.tensor_copy(
             wr_rows_t[:],
             wr_rows[:].rearrange("p w c -> p (w c)").bitcast(U8).rearrange("p (w m t) -> p w t m", w=2, t=PACK),
         )
-        for q in range(4):
+        for s in range(4):
             nc.sync.dma_start(
-                wr_plane[32 * q : 32 * q + 4, :],
-                wr_rows_t[96 + 8 * q : 96 + 8 * q + 8, :, :, :].rearrange("p w t m -> p (w t m)").bitcast(I32),
+                wr_plane[s:P:32, :],
+                wr_rows_t[96 + 8 * s : 96 + 8 * s + 8, :, :, :].rearrange("p w t m -> p (w t m)").bitcast(I32),
             )
         we_raw.append(placed([P, PACK, R], F32, "wei_raw", WEI_AT))
         nc.sync.dma_start(we_raw[1][:], wei.rearrange("(p i) r -> p i r", i=PACK))
@@ -160,7 +163,7 @@ def tile_list_ckg_bias_kernel(
             nc.vector.quantize_mx(out=we_words[w][:].bitcast(FP8X4), scales=we_plane[w][:], in_=we_bf[w][:])
         for q in range(4):
             nc.sync.dma_start(
-                g_early[32 * q : 32 * q + 4, :], g_rows[112 + 4 * q : 112 + 4 * q + 4, 0:EARLY].bitcast(I32)
+                g_early[32 * q : 32 * q + 4, :], g_rows[32 + 16 * q : 48 + 16 * q : 4, 0:EARLY].bitcast(I32)
             )
         g2_late = placed([P, 2 * (J - EARLY) // 4], I32, "g2_late", G2_LATE_AT)
         nc.gpsimd.memset(g2_late[:], 0)
@@ -172,7 +175,7 @@ def tile_list_ckg_bias_kernel(
         nc.gpsimd.memset(g_late[:], 0)
         for q in range(4):
             nc.sync.dma_start(
-                g_late[32 * q : 32 * q + 4, :], g_rows[112 + 4 * q : 112 + 4 * q + 4, EARLY:J].bitcast(I32)
+                g_late[32 * q : 32 * q + 4, :], g_rows[32 + 16 * q : 48 + 16 * q : 4, EARLY:J].bitcast(I32)
             )
 
         def g_scale(i):

@@ -26,12 +26,13 @@ HALF = J // 2
 N_TILES = J // TOK
 LAST = N_TILES - 1
 GROUPS = [4, 4, 4, 1, 1, 1, 1]
+QUANTISED_AFTER = {5: [0], 9: [1], 13: [2, 3], 15: [4, 5]}
 REL_AHEAD = 3
 STAGED_BUFS = 8
 TERM_BUFS = 6
 GATHERS = [(0, 2), (2, 4), (6, 4), (10, 4), (14, 2)]
 WORDS_AFTER = {2: 2, 3: 6, 4: 10}
-SPLIT = {10: 352, 14: 416}
+SPLIT = {10: 352, 14: 352}
 
 RAW = PACK * R * 4
 SLOT = 3 * WIDTH * 4
@@ -41,8 +42,7 @@ WR_ROWS_AT = WEI_AT
 RELATION_AT = WEI_AT
 WEI_BF_AT = RELATION_AT + 3 * SLOT - RAW // 4
 WER_AT = RELATION_AT + (REL_AHEAD + 1) * SLOT
-N_WORDS_AT = WER_AT
-G_PLANES_AT = WER_AT + 4 * N
+G_PLANES_AT = WER_AT
 G2_LATE_AT = G_PLANES_AT + J - EARLY
 N_PLANE_AT = G2_LATE_AT + 2 * (J - EARLY)
 
@@ -161,10 +161,8 @@ def tile_list_ckg_bias_kernel(
                 we_raw[w][:].rearrange("p i (m t) -> p m t i", t=PACK),
             )
             nc.vector.quantize_mx(out=we_words[w][:].bitcast(FP8X4), scales=we_plane[w][:], in_=we_bf[w][:])
-        for q in range(4):
-            nc.sync.dma_start(
-                g_early[32 * q : 32 * q + 4, :], g_rows[32 + 16 * q : 48 + 16 * q : 4, 0:EARLY].bitcast(I32)
-            )
+        for s in range(4):
+            nc.sync.dma_start(g_early[s:P:32, :], g_rows[32 + 4 * s : 96 : 16, 0:EARLY].bitcast(I32))
         g2_late = placed([P, 2 * (J - EARLY) // 4], I32, "g2_late", G2_LATE_AT)
         nc.gpsimd.memset(g2_late[:], 0)
         for q in range(4):
@@ -173,10 +171,8 @@ def tile_list_ckg_bias_kernel(
             )
         g_late = placed([P, (J - EARLY) // 4], I32, "g_late", G_PLANES_AT)
         nc.gpsimd.memset(g_late[:], 0)
-        for q in range(4):
-            nc.sync.dma_start(
-                g_late[32 * q : 32 * q + 4, :], g_rows[32 + 16 * q : 48 + 16 * q : 4, EARLY:J].bitcast(I32)
-            )
+        for s in range(4):
+            nc.sync.dma_start(g_late[s:P:32, :], g_rows[32 + 4 * s : 96 : 16, EARLY:J].bitcast(I32))
 
         def g_scale(i):
             plane, at = (g_early, i * TOK) if i * TOK < EARLY else (g_late, i * TOK - EARLY)
@@ -306,16 +302,18 @@ def tile_list_ckg_bias_kernel(
             staged = ring.tile([P, CHUNK], F32, name="staged", bufs=STAGED_BUFS)
             for q in range(4):
                 score(g, q, bank[:, q * TOK : (q + 1) * TOK])
-            for q in range(4):
-                nc.scalar.activation(
-                    staged[:, q * TOK : (q + 1) * TOK], bank[:, q * TOK : (q + 1) * TOK], IDENTITY, bias=bias[:, q : q + 1]
+            for pair in range(2):
+                for q in (2 * pair, 2 * pair + 1):
+                    span = slice(q * TOK, (q + 1) * TOK)
+                    nc.scalar.activation(staged[:, span], bank[:, span], IDENTITY, bias=bias[:, q : q + 1])
+                nc.sync.dma_start(
+                    out[2 * pair * P : 2 * (pair + 1) * P, starts[g] * TOK : (starts[g] + 1) * TOK].rearrange(
+                        "(q p) j -> p q j", p=P
+                    ),
+                    staged[:, 2 * pair * TOK : 2 * (pair + 1) * TOK].rearrange("p (q j) -> p q j", q=2),
                 )
-            nc.sync.dma_start(
-                out[:, starts[g] * TOK : (starts[g] + 1) * TOK].rearrange("(q p) j -> p q j", p=P),
-                staged[:].rearrange("p (q j) -> p q j", q=4),
-            )
 
-        n_words = placed([P, 2, N // 2], I32, "n_words", N_WORDS_AT)
+        n_words = held([P, 2, N // 2], I32, "n_words", "g2_rows")
         for w, src in enumerate((nr_words, ni_words)):
             nc.sync.dma_start(n_words[:, w, :], src[0].bitcast(I32))
         n_plane = placed([P, 2, N // 4], I32, "n_plane", N_PLANE_AT)
@@ -323,7 +321,7 @@ def tile_list_ckg_bias_kernel(
         for w, src in enumerate((nr_scales, ni_scales)):
             for q in range(4):
                 nc.sync.dma_start(n_plane[32 * q : 32 * q + 4, w, :], src[0, 4 * q : 4 * q + 4, :].bitcast(I32))
-        bias = held([P, N // P], F32, "bias", "g2_rows")
+        bias = held([P, N // P], F32, "bias", "g2_pairs0")
         with nc.allow_non_contiguous_dma(reason="one bias value to a partition"):
             nc.sync.dma_start(bias[:], b.rearrange("(q p) -> p q", p=P))
 
@@ -342,7 +340,7 @@ def tile_list_ckg_bias_kernel(
                 nc.scalar.activation(
                     staged[:, TOK : 2 * TOK], banks[by_scalar][:, 0:TOK], IDENTITY, bias=bias[:, by_scalar : by_scalar + 1]
                 )
-                nc.sync.dma_start(
+                (nc.sync, nc.scalar)[pair].dma_start(
                     out[2 * pair * P : 2 * (pair + 1) * P, LAST * TOK : J].rearrange("(q p) j -> p q j", p=P),
                     staged[:, 0 : 2 * TOK].rearrange("p (q j) -> p q j", q=2),
                 )
@@ -355,11 +353,9 @@ def tile_list_ckg_bias_kernel(
             products(i)
             if i - 1 in SPLIT:
                 add(nc.vector, i - 1, both, slice(SPLIT[i - 1], WIDTH))
-            for done in range(max(i - 2, 0), i - 1 if i < LAST else i):
-                g = group_of[done]
-                if done + 1 - starts[g] == GROUPS[g]:
-                    quantise(g)
-                    pending.extend([(g, None)] if GROUPS[g] == 1 else [(g, q) for q in range(4)])
+            for g in QUANTISED_AFTER.get(i, []):
+                quantise(g)
+                pending.extend([(g, None)] if GROUPS[g] == 1 else [(g, q) for q in range(4)])
             if i == LAST:
                 for w in range(2):
                     add(nc.vector, i, slice(w, w + 1), slice(0, WIDTH))

@@ -1,6 +1,7 @@
 from contextlib import ExitStack
 
 import concourse.mybir as mybir
+from concourse.masks import make_identity
 
 K, L, R, N, T, J = 512, 1024, 512, 512, 4096, 2048
 FLOPS = 2 * J * (2 * K * R + 2 * L * R + 2 * R * N)
@@ -25,14 +26,15 @@ CHUNK = 512
 HALF = J // 2
 N_TILES = J // TOK
 LAST = N_TILES - 1
-GROUPS = [4, 4, 4, 1, 1, 1, 1]
-QUANTISED_AFTER = {5: [0], 9: [1], 13: [2, 3], 15: [4, 5]}
+GROUPS = [4, 4, 2, 2, 1, 1, 1, 1]
+TURNED = LAST - 1
+QUANTISED_AFTER = {5: [0], 9: [1], 11: [2], 13: [3, 4]}
 REL_AHEAD = 3
 STAGED_BUFS = 8
 TERM_BUFS = 6
-GATHERS = [(0, 2), (2, 4), (6, 4), (10, 4), (14, 2)]
-WORDS_AFTER = {2: 2, 3: 6, 4: 10}
-SPLIT = {10: 352, 14: 352}
+GATHERS = [(0, 2), (2, 4), (6, 4), (10, 2), (12, 2), (14, 2)]
+WORDS_AFTER = {2: 2, 3: 6, 4: 8, 5: 10}
+SPLIT = {6: 352}
 
 RAW = PACK * R * 4
 SLOT = 3 * WIDTH * 4
@@ -45,6 +47,7 @@ WER_AT = RELATION_AT + (REL_AHEAD + 1) * SLOT
 G_PLANES_AT = WER_AT
 G2_LATE_AT = G_PLANES_AT + J - EARLY
 N_PLANE_AT = G2_LATE_AT + 2 * (J - EARLY)
+IDENTITY_AT = N_PLANE_AT + 2 * N
 
 
 def tile_list_ckg_bias_kernel(
@@ -182,6 +185,9 @@ def tile_list_ckg_bias_kernel(
             plane, width, at = (g2_early, EARLY, i * TOK) if i * TOK < EARLY else (g2_late, J - EARLY, i * TOK - EARLY)
             return plane[:].bitcast(U8)[:, a * width + at : a * width + at + TOK]
 
+        identity = placed([P, P], F32, "identity", IDENTITY_AT)
+        make_identity(nc, identity[:])
+
         gather_v(0)
         gather_v(1)
 
@@ -197,6 +203,21 @@ def tile_list_ckg_bias_kernel(
                     bank = psum.tile([P, PACK, TOK], F32, name=f"ent{i % 2}{w}")
                 else:
                     bank = psum.tile([P, PACK, TOK], F32, name=f"rel{w}")
+                if i == TURNED:
+                    for a in range(2):
+                        nc.tensor.matmul_mx(
+                            out=bank[:].rearrange("p t n -> p (t n)"),
+                            lhsT=g2_words[h][:, a, 2 * u * TOK : 2 * (u + 1) * TOK].bitcast(FP4X4),
+                            lhsT_scale=g2_scale(a, i),
+                            rhs=wr_words[:, w, a, :, :].rearrange("p t m -> p (t m)").bitcast(FP8X4),
+                            rhs_scale=wr_scale[:, a, w, :, :].rearrange("p t m -> p (t m)"),
+                            start=(a == 0),
+                            stop=(a == 1),
+                        )
+                    nc.scalar.copy(
+                        relation[i][:, 1 + w, :, :].rearrange("p n t -> p (n t)"), bank[:].rearrange("p t n -> p (t n)")
+                    )
+                    continue
                 for t in range(PACK):
                     for a in range(2):
                         nc.tensor.matmul_mx(
@@ -212,6 +233,7 @@ def tile_list_ckg_bias_kernel(
             nc.scalar.mul(relation[i][:, 0, :, :], relation[i][:, 2, :, :], -1.0)
 
         terms = {}
+        entity = {}
 
         def products(i):
             ent = {}
@@ -220,6 +242,19 @@ def tile_list_ckg_bias_kernel(
                     bank = psum.tile([P, PACK, TOK], F32, name=f"rel{w}")
                 else:
                     bank = psum.tile([P, PACK, TOK], F32, name=f"ent{i % 2}{(w + i // 2) % 2}")
+                if i == TURNED:
+                    nc.tensor.matmul_mx(
+                        out=bank[:].rearrange("p t n -> p (t n)"),
+                        lhsT=g_words[i].bitcast(FP8X4),
+                        lhsT_scale=g_scale(i),
+                        rhs=we_words[w][:].bitcast(FP8X4),
+                        rhs_scale=we_plane[w][:],
+                        start=True,
+                        stop=True,
+                    )
+                    flat = bank[:].rearrange("p t (x y) -> p (t x) y", y=PACK)
+                    ent[w] = flat.unsqueeze(1).to_broadcast([P, 2, TOK, PACK])
+                    continue
                 for t in range(PACK):
                     nc.tensor.matmul_mx(
                         out=bank[:, t, :],
@@ -236,9 +271,13 @@ def tile_list_ckg_bias_kernel(
             else:
                 first = ring.tile([P, 2, TOK, PACK], F32, name="first", bufs=TERM_BUFS)
             second = ring.tile([P, 2, TOK, PACK], F32, name="second", bufs=TERM_BUFS)
-            nc.vector.tensor_tensor(first[:], ent[0], relation[i][:, 1:3, :, :], MULT)
-            nc.vector.tensor_tensor(second[:], ent[1], relation[i][:, 0:2, :, :], MULT)
             terms[i] = (first, second)
+            entity[i] = ent
+
+        def multiply(i, lo, hi):
+            first, second = terms[i]
+            nc.vector.tensor_tensor(first[:, lo:hi], entity[i][0][:, lo:hi], relation[i][:, 1 + lo : 1 + hi, :, :], MULT)
+            nc.vector.tensor_tensor(second[:, lo:hi], entity[i][1][:, lo:hi], relation[i][:, lo:hi, :, :], MULT)
 
         starts = [sum(GROUPS[:g]) for g in range(len(GROUPS))]
         group_of = [g for g, n in enumerate(GROUPS) for u in range(n)]
@@ -256,6 +295,27 @@ def tile_list_ckg_bias_kernel(
                 second[:].rearrange("p w n t -> p w (n t)")[:, parts, span],
                 ADD,
             )
+
+        def add_turned(i):
+            g = group_of[i]
+            h_bf[g] = ring.tile([P, 2, GROUPS[g], WIDTH], BF16, name="h_bf", align_bytes=64)
+            banks = [psum.tile([P, PACK, TOK], F32, name=f"rel{part}") for part in range(2)]
+            for k, term in enumerate(terms[i]):
+                for part in range(2):
+                    columns = term[:, part, :, :].rearrange("p n t -> p (n t)")
+                    for t in range(PACK):
+                        nc.tensor.matmul(
+                            banks[part][:, t, :],
+                            lhsT=columns[:, t * P : (t + 1) * P],
+                            rhs=identity[:],
+                            is_transpose=True,
+                            start=(k == 0 and t == 0),
+                            stop=(k == 1 and t == PACK - 1),
+                        )
+            for part in range(2):
+                nc.scalar.copy(
+                    h_bf[g][:, part, 0, :].rearrange("p (n t) -> p n t", t=PACK), banks[part][:].rearrange("p t n -> p n t")
+                )
 
         def quantise(g):
             width = GROUPS[g] * TOK
@@ -297,15 +357,35 @@ def tile_list_ckg_bias_kernel(
             nc.scalar.activation(staged[:], bank[:], IDENTITY, bias=bias[:, q : q + 1])
             nc.sync.dma_start(out[q * P : (q + 1) * P, starts[g] * TOK : starts[g] * TOK + CHUNK], staged[:])
 
-        def score_narrow(g):
+        def score_pair(g, pair):
             bank = psum.tile([P, CHUNK], F32, name="score", bufs=2)
             staged = ring.tile([P, CHUNK], F32, name="staged", bufs=STAGED_BUFS)
-            for q in range(4):
-                score(g, q, bank[:, q * TOK : (q + 1) * TOK])
+            for u in range(2):
+                score(g, 2 * pair + u, bank[:, u * 2 * TOK : (u + 1) * 2 * TOK])
+            for u in range(2):
+                span = slice(u * 2 * TOK, (u + 1) * 2 * TOK)
+                nc.scalar.activation(staged[:, span], bank[:, span], IDENTITY, bias=bias[:, 2 * pair + u : 2 * pair + u + 1])
+            nc.sync.dma_start(
+                out[2 * pair * P : 2 * (pair + 1) * P, starts[g] * TOK : (starts[g] + 2) * TOK].rearrange(
+                    "(q p) j -> p q j", p=P
+                ),
+                staged[:].rearrange("p (q j) -> p q j", q=2),
+            )
+
+        def score_narrow(g):
+            staged = ring.tile([P, CHUNK], F32, name="staged", bufs=STAGED_BUFS)
             for pair in range(2):
-                for q in (2 * pair, 2 * pair + 1):
-                    span = slice(q * TOK, (q + 1) * TOK)
-                    nc.scalar.activation(staged[:, span], bank[:, span], IDENTITY, bias=bias[:, q : q + 1])
+                if starts[g] == LAST - 1:
+                    bank = psum.tile([P, CHUNK], F32, name=f"ent1{pair}")
+                else:
+                    bank = psum.tile([P, CHUNK], F32, name="score", bufs=2)
+                for u in range(2):
+                    score(g, 2 * pair + u, bank[:, u * TOK : (u + 1) * TOK])
+                for u in range(2):
+                    q = 2 * pair + u
+                    nc.scalar.activation(
+                        staged[:, q * TOK : (q + 1) * TOK], bank[:, u * TOK : (u + 1) * TOK], IDENTITY, bias=bias[:, q : q + 1]
+                    )
                 nc.sync.dma_start(
                     out[2 * pair * P : 2 * (pair + 1) * P, starts[g] * TOK : (starts[g] + 1) * TOK].rearrange(
                         "(q p) j -> p q j", p=P
@@ -349,29 +429,42 @@ def tile_list_ckg_bias_kernel(
             project_relation(i)
         both = slice(0, 2)
         pending = []
-        for i in range(N_TILES):
+        for i in range(LAST):
             products(i)
+            for lo, hi in [(0, 1), (1, 2)] if i == 0 else [(0, 2)]:
+                multiply(i, lo, hi)
             if i - 1 in SPLIT:
                 add(nc.vector, i - 1, both, slice(SPLIT[i - 1], WIDTH))
             for g in QUANTISED_AFTER.get(i, []):
                 quantise(g)
-                pending.extend([(g, None)] if GROUPS[g] == 1 else [(g, q) for q in range(4)])
-            if i == LAST:
-                for w in range(2):
-                    add(nc.vector, i, slice(w, w + 1), slice(0, WIDTH))
+                pending.extend([(g, q) for q in range(GROUPS[g])])
+            if i == TURNED:
+                add_turned(i)
             else:
-                add(nc.gpsimd, i, both, slice(0, SPLIT.get(i, WIDTH)))
+                for parts in [slice(0, 1), slice(1, 2)] if i == 0 else [both]:
+                    add(nc.gpsimd, i, parts, slice(0, SPLIT.get(i, WIDTH)))
             for c in WORDS_AFTER:
                 if WORDS_AFTER[c] == i - 2:
                     gather_v(c, f"first{i - 2}")
             if i + REL_AHEAD < N_TILES:
                 project_relation(i + REL_AHEAD)
-            take = len(pending) if i >= N_TILES - 3 else min(1, len(pending))
+            take = len(pending) if i == TURNED else min(2 if i >= TURNED - 3 else 1, len(pending))
             for g, q in pending[:take]:
-                if q is None:
-                    score_narrow(g)
-                else:
+                if GROUPS[g] == 4:
                     score_wide(g, q)
+                elif GROUPS[g] == 2:
+                    score_pair(g, q)
+                else:
+                    score_narrow(g)
             pending = pending[take:]
-        quantise(len(GROUPS) - 1)
-        score_last(len(GROUPS) - 1)
+        products(LAST)
+        multiply(LAST, 0, 1)
+        quantise(group_of[TURNED - 1])
+        add(nc.gpsimd, LAST, slice(0, 1), slice(0, WIDTH))
+        multiply(LAST, 1, 2)
+        score_narrow(group_of[TURNED - 1])
+        quantise(group_of[TURNED])
+        add(nc.vector, LAST, slice(1, 2), slice(0, WIDTH))
+        score_narrow(group_of[TURNED])
+        quantise(group_of[LAST])
+        score_last(group_of[LAST])

@@ -429,8 +429,9 @@ def tile_list_ckg_bias_kernel(
             project_relation(i)
         both = slice(0, 2)
         pending = []
+        products(0)
+        products(1)
         for i in range(LAST):
-            products(i)
             for lo, hi in [(0, 1), (1, 2)] if i == 0 else [(0, 2)]:
                 multiply(i, lo, hi)
             if i - 1 in SPLIT:
@@ -446,6 +447,8 @@ def tile_list_ckg_bias_kernel(
             for c in WORDS_AFTER:
                 if WORDS_AFTER[c] == i - 2:
                     gather_v(c, f"first{i - 2}")
+            if i + 2 < N_TILES:
+                products(i + 2)
             if i + REL_AHEAD < N_TILES:
                 project_relation(i + REL_AHEAD)
             take = len(pending) if i == TURNED else min(2 if i >= TURNED - 3 else 1, len(pending))
@@ -457,7 +460,6 @@ def tile_list_ckg_bias_kernel(
                 else:
                     score_narrow(g)
             pending = pending[take:]
-        products(LAST)
         multiply(LAST, 0, 1)
         quantise(group_of[TURNED - 1])
         add(nc.gpsimd, LAST, slice(0, 1), slice(0, WIDTH))

@@ -27,13 +27,14 @@ HALF = J // 2
 N_TILES = J // TOK
 LAST = N_TILES - 1
 GROUPS = [4, 4, 2, 2, 1, 1, 1, 1]
-TURNED = LAST - 1
+TURNED = (2, LAST - 1)
 QUANTISED_AFTER = {5: [0], 9: [1], 11: [2], 13: [3, 4]}
+UNSIGNED = 4
 REL_AHEAD = 3
 STAGED_BUFS = 8
 TERM_BUFS = 6
 GATHERS = [(0, 2), (2, 4), (6, 4), (10, 2), (12, 2), (14, 2)]
-WORDS_AFTER = {2: 2, 3: 6, 4: 8, 5: 10}
+WORDS_AFTER = {2: 1, 3: 6, 4: 8, 5: 10}
 SPLIT = {6: 352}
 
 RAW = PACK * R * 4
@@ -117,7 +118,8 @@ def tile_list_ckg_bias_kernel(
         wr_words = held([P, 2, 2, PACK, P], U32, "wr_words")
         for w in range(2):
             nc.scalar.copy(
-                wr_words[:, w, :, :, :], wr_raw[w][:].bitcast(U32).rearrange("p a (m t) -> p a t m", t=PACK)
+                wr_words[:, w, :, :, :].rearrange("p a t (x y) -> p a x t y", y=PACK),
+                wr_raw[w][:].bitcast(U32).rearrange("p a (x y t) -> p a x t y", y=PACK, t=PACK),
             )
         wr_scale = wr_plane[:].bitcast(U8).rearrange("p (a w t m) -> p a w t m", a=2, w=2, t=PACK)
 
@@ -132,7 +134,10 @@ def tile_list_ckg_bias_kernel(
 
         def gather_v(c, tag=None):
             at, tiles = GATHERS[c]
-            words = held([P, tiles * TOK], U32, f"g_words{c}", tag)
+            if c == 0:
+                words = placed([P, tiles * TOK], U32, "g_words0", RELATION_AT + REL_AHEAD * SLOT + RAW // 4)
+            else:
+                words = held([P, tiles * TOK], U32, f"g_words{c}", tag)
             offsets = list1[:, at * TOK // 16 : (at + tiles) * TOK // 16]
             nc.vector.tensor_copy(words[:], v_words[:].bitcast(U32).indirect(offsets))
             for u in range(tiles):
@@ -191,19 +196,23 @@ def tile_list_ckg_bias_kernel(
         gather_v(0)
         gather_v(1)
 
+        taken = []
+
+        def score_bank(shape):
+            taken.append(shape)
+            return psum.tile(shape, F32, name=f"score{len(taken) % 2}")
+
         relation = {}
 
         def project_relation(i):
             h, u = divmod(i, HALF // TOK)
-            relation[i] = shared.tile(
-                [P, 3, TOK, PACK], F32, name="relation", bufs=REL_AHEAD + 1, align_bytes=64, offset=RELATION_AT
-            )
+            relation[i] = placed([P, 3, TOK, PACK], F32, f"relation{i}", RELATION_AT + i % (REL_AHEAD + 1) * SLOT)
             for w in (1, 0):
                 if i in (1, 2):
                     bank = psum.tile([P, PACK, TOK], F32, name=f"ent{i % 2}{w}")
                 else:
                     bank = psum.tile([P, PACK, TOK], F32, name=f"rel{w}")
-                if i == TURNED:
+                if i in TURNED:
                     for a in range(2):
                         nc.tensor.matmul_mx(
                             out=bank[:].rearrange("p t n -> p (t n)"),
@@ -230,19 +239,20 @@ def tile_list_ckg_bias_kernel(
                             stop=(a == 1),
                         )
                 nc.scalar.copy(relation[i][:, 1 + w, :, :], bank[:].rearrange("p t n -> p n t"))
-            nc.scalar.mul(relation[i][:, 0, :, :], relation[i][:, 2, :, :], -1.0)
+            if i >= UNSIGNED:
+                nc.scalar.mul(relation[i][:, 0, :, :], relation[i][:, 2, :, :], -1.0)
 
         terms = {}
         entity = {}
 
         def products(i):
             ent = {}
-            for w in (0, 1) if i == 0 else (1, 0):
+            for w in (0, 1) if i < 2 else (1, 0):
                 if i == 0:
-                    bank = psum.tile([P, PACK, TOK], F32, name=f"rel{w}")
+                    bank = psum.tile([P, PACK, TOK], F32, name=f"score{w}")
                 else:
                     bank = psum.tile([P, PACK, TOK], F32, name=f"ent{i % 2}{(w + i // 2) % 2}")
-                if i == TURNED:
+                if i in TURNED:
                     nc.tensor.matmul_mx(
                         out=bank[:].rearrange("p t n -> p (t n)"),
                         lhsT=g_words[i].bitcast(FP8X4),
@@ -265,7 +275,12 @@ def tile_list_ckg_bias_kernel(
                         start=True,
                         stop=True,
                     )
-                ent[w] = bank[:].rearrange("p t n -> p n t").unsqueeze(1).to_broadcast([P, 2, TOK, PACK])
+                ent[w] = bank[:].rearrange("p t n -> p n t")
+                if i == 0 and w == 0:
+                    aer = held([P, TOK, PACK], F32, "aer")
+                    nc.scalar.copy(aer[:], ent[w])
+                    ent[w] = aer[:]
+                ent[w] = ent[w].unsqueeze(1).to_broadcast([P, 2, TOK, PACK])
             if i in WORDS_AFTER.values():
                 first = held([P, 2, TOK, PACK], F32, f"first{i}")
             else:
@@ -276,89 +291,105 @@ def tile_list_ckg_bias_kernel(
 
         def multiply(i, lo, hi):
             first, second = terms[i]
-            nc.vector.tensor_tensor(first[:, lo:hi], entity[i][0][:, lo:hi], relation[i][:, 1 + lo : 1 + hi, :, :], MULT)
-            nc.vector.tensor_tensor(second[:, lo:hi], entity[i][1][:, lo:hi], relation[i][:, lo:hi, :, :], MULT)
+            (nc.gpsimd if i == 0 else nc.vector).tensor_tensor(first[:, lo:hi], entity[i][0][:, lo:hi], relation[i][:, 1 + lo : 1 + hi, :, :], MULT)
+            if i >= UNSIGNED:
+                nc.vector.tensor_tensor(second[:, lo:hi], entity[i][1][:, lo:hi], relation[i][:, lo:hi, :, :], MULT)
+            else:
+                nc.vector.tensor_tensor(second[:, 1], entity[i][1][:, 0], relation[i][:, 1, :, :], MULT)
+                nc.vector.scalar_tensor_tensor(second[:, 0], entity[i][1][:, 0], -1.0, relation[i][:, 2, :, :], MULT, MULT)
 
         starts = [sum(GROUPS[:g]) for g in range(len(GROUPS))]
         group_of = [g for g, n in enumerate(GROUPS) for u in range(n)]
         h_bf = {}
         h_mx = {}
 
-        def add(engine, i, parts, span):
+        def sums(i):
             g = group_of[i]
-            first, second = terms[i]
             if g not in h_bf:
-                h_bf[g] = ring.tile([P, 2, GROUPS[g], WIDTH], BF16, name="h_bf", align_bytes=64)
+                n = min(GROUPS[g], 2)
+                h_bf[g] = [
+                    ring.tile([P, 2, n, WIDTH], BF16, name="h_bf", bufs=6, align_bytes=64) for half in range(GROUPS[g] // n)
+                ]
+            u, half = divmod(i - starts[g], len(h_bf[g]))
+            return h_bf[g][half][:, :, u, :]
+
+        def add(engine, i, parts, span):
+            first, second = terms[i]
             engine.tensor_tensor(
-                h_bf[g][:, parts, i - starts[g], span],
+                sums(i)[:, parts, span],
                 first[:].rearrange("p w n t -> p w (n t)")[:, parts, span],
                 second[:].rearrange("p w n t -> p w (n t)")[:, parts, span],
                 ADD,
             )
 
-        def add_turned(i):
-            g = group_of[i]
-            h_bf[g] = ring.tile([P, 2, GROUPS[g], WIDTH], BF16, name="h_bf", align_bytes=64)
-            banks = [psum.tile([P, PACK, TOK], F32, name=f"rel{part}") for part in range(2)]
+        def add_turned(i, part, name):
+            bank = psum.tile([P, PACK, TOK], F32, name=name)
             for k, term in enumerate(terms[i]):
-                for part in range(2):
-                    columns = term[:, part, :, :].rearrange("p n t -> p (n t)")
-                    for t in range(PACK):
-                        nc.tensor.matmul(
-                            banks[part][:, t, :],
-                            lhsT=columns[:, t * P : (t + 1) * P],
-                            rhs=identity[:],
-                            is_transpose=True,
-                            start=(k == 0 and t == 0),
-                            stop=(k == 1 and t == PACK - 1),
-                        )
-            for part in range(2):
-                nc.scalar.copy(
-                    h_bf[g][:, part, 0, :].rearrange("p (n t) -> p n t", t=PACK), banks[part][:].rearrange("p t n -> p n t")
-                )
+                columns = term[:, part, :, :].rearrange("p n t -> p (n t)")
+                for t in range(PACK):
+                    nc.tensor.matmul(
+                        bank[:, t, :],
+                        lhsT=columns[:, t * P : (t + 1) * P],
+                        rhs=identity[:],
+                        is_transpose=True,
+                        start=(k == 0 and t == 0),
+                        stop=(k == 1 and t == PACK - 1),
+                    )
+            nc.scalar.copy(sums(i)[:, part, :].rearrange("p (n t) -> p n t", t=PACK), bank[:].rearrange("p t n -> p n t"))
 
         def quantise(g):
             width = GROUPS[g] * TOK
             words = ring.tile([P, 2 * width], U32, name="h_words", align_bytes=64)
             plane = ring.tile([P, 2 * width], U8, name="h_plane", align_bytes=64)
             if starts[g] < LAST:
-                nc.vector.quantize_mx(
-                    out=words[:].bitcast(FP8X4), scales=plane[:], in_=h_bf[g][:].rearrange("p w u x -> p (w u x)")
-                )
+                for half, tile in enumerate(h_bf[g]):
+                    span = slice(half * CHUNK, half * CHUNK + 2 * width // len(h_bf[g]))
+                    nc.vector.quantize_mx(
+                        out=words[:, span].bitcast(FP8X4),
+                        scales=plane[:, span],
+                        in_=tile[:].rearrange("p w u x -> p (w u x)"),
+                    )
             else:
                 for w in range(2):
                     span = slice(w * width, (w + 1) * width)
                     nc.vector.quantize_mx(
-                        out=words[:, span].bitcast(FP8X4), scales=plane[:, span], in_=h_bf[g][:, w, 0, :]
+                        out=words[:, span].bitcast(FP8X4), scales=plane[:, span], in_=h_bf[g][0][:, w, 0, :]
                     )
             h_mx[g] = (words, plane)
 
-        def score(g, q, bank):
+        def score(g, q, bank, half=0):
             for w in range(2):
-                one_pass(g, q, w, bank, w == 0, w == 1)
+                one_pass(g, q, w, bank, w == 0, w == 1, half)
 
-        def one_pass(g, q, w, bank, start, stop):
-            width = GROUPS[g] * TOK
+        def one_pass(g, q, w, bank, start, stop, half=0):
+            width = min(GROUPS[g], 2) * TOK
+            span = slice((2 * half + w) * width, (2 * half + w + 1) * width)
             words, plane = h_mx[g]
             nc.tensor.matmul_mx(
                 out=bank,
                 lhsT=n_words[:, w, q * P // 2 : (q + 1) * P // 2].bitcast(FP4X4),
                 lhsT_scale=n_plane[:, w, :].bitcast(U8)[:, q * P : (q + 1) * P],
-                rhs=words[:, w * width : (w + 1) * width].bitcast(FP8X4),
-                rhs_scale=plane[:, w * width : (w + 1) * width],
+                rhs=words[:, span].bitcast(FP8X4),
+                rhs_scale=plane[:, span],
                 start=start,
                 stop=stop,
             )
 
         def score_wide(g, q):
-            bank = psum.tile([P, CHUNK], F32, name="score", bufs=2)
+            bank = score_bank([P, CHUNK])
             staged = ring.tile([P, CHUNK], F32, name="staged", bufs=STAGED_BUFS)
-            score(g, q, bank[:])
-            nc.scalar.activation(staged[:], bank[:], IDENTITY, bias=bias[:, q : q + 1])
+            for half in range(2):
+                score(g, q, bank[:, half * 2 * TOK : (half + 1) * 2 * TOK], half)
+            nc.scalar.activation(
+                staged[:].rearrange("p (u h j) -> p u h j", u=2, h=2),
+                bank[:].rearrange("p (h u j) -> p u h j", u=2, h=2),
+                IDENTITY,
+                bias=bias[:, q : q + 1],
+            )
             nc.sync.dma_start(out[q * P : (q + 1) * P, starts[g] * TOK : starts[g] * TOK + CHUNK], staged[:])
 
         def score_pair(g, pair):
-            bank = psum.tile([P, CHUNK], F32, name="score", bufs=2)
+            bank = score_bank([P, CHUNK])
             staged = ring.tile([P, CHUNK], F32, name="staged", bufs=STAGED_BUFS)
             for u in range(2):
                 score(g, 2 * pair + u, bank[:, u * 2 * TOK : (u + 1) * 2 * TOK])
@@ -378,7 +409,7 @@ def tile_list_ckg_bias_kernel(
                 if starts[g] == LAST - 1:
                     bank = psum.tile([P, CHUNK], F32, name=f"ent1{pair}")
                 else:
-                    bank = psum.tile([P, CHUNK], F32, name="score", bufs=2)
+                    bank = score_bank([P, CHUNK])
                 for u in range(2):
                     score(g, 2 * pair + u, bank[:, u * TOK : (u + 1) * TOK])
                 for u in range(2):
@@ -425,33 +456,36 @@ def tile_list_ckg_bias_kernel(
                     staged[:, 0 : 2 * TOK].rearrange("p (q j) -> p q j", q=2),
                 )
 
-        for i in range(REL_AHEAD):
+        project_relation(0)
+        products(0)
+        for i in range(1, REL_AHEAD + 1):
             project_relation(i)
         both = slice(0, 2)
         pending = []
-        products(0)
         products(1)
         for i in range(LAST):
-            for lo, hi in [(0, 1), (1, 2)] if i == 0 else [(0, 2)]:
+            for lo, hi in [(0, 1), (1, 2)] if i == LAST - 1 else [(0, 2)]:
                 multiply(i, lo, hi)
             if i - 1 in SPLIT:
                 add(nc.vector, i - 1, both, slice(SPLIT[i - 1], WIDTH))
             for g in QUANTISED_AFTER.get(i, []):
                 quantise(g)
                 pending.extend([(g, q) for q in range(GROUPS[g])])
-            if i == TURNED:
-                add_turned(i)
-            else:
-                for parts in [slice(0, 1), slice(1, 2)] if i == 0 else [both]:
-                    add(nc.gpsimd, i, parts, slice(0, SPLIT.get(i, WIDTH)))
+            if i == LAST - 1:
+                for part in range(2):
+                    add_turned(i, part, f"rel{part}")
+            if i not in TURNED:
+                add(nc.gpsimd, i, both, slice(0, SPLIT.get(i, WIDTH)))
             for c in WORDS_AFTER:
-                if WORDS_AFTER[c] == i - 2:
-                    gather_v(c, f"first{i - 2}")
+                if WORDS_AFTER[c] == i - (3 if c == 2 else 2):
+                    gather_v(c, f"first{WORDS_AFTER[c]}")
             if i + 2 < N_TILES:
                 products(i + 2)
-            if i + REL_AHEAD < N_TILES:
+            if i - TURNED[0] in (0, 1):
+                add_turned(TURNED[0], i - TURNED[0], f"score{i - TURNED[0]}")
+            if REL_AHEAD < i + REL_AHEAD < N_TILES:
                 project_relation(i + REL_AHEAD)
-            take = len(pending) if i == TURNED else min(2 if i >= TURNED - 3 else 1, len(pending))
+            take = len(pending) if i == LAST - 1 else min(2 if i >= LAST - 4 else 1, len(pending))
             for g, q in pending[:take]:
                 if GROUPS[g] == 4:
                     score_wide(g, q)
@@ -461,12 +495,12 @@ def tile_list_ckg_bias_kernel(
                     score_narrow(g)
             pending = pending[take:]
         multiply(LAST, 0, 1)
-        quantise(group_of[TURNED - 1])
+        quantise(group_of[LAST - 2])
         add(nc.gpsimd, LAST, slice(0, 1), slice(0, WIDTH))
         multiply(LAST, 1, 2)
-        score_narrow(group_of[TURNED - 1])
-        quantise(group_of[TURNED])
+        score_narrow(group_of[LAST - 2])
+        quantise(group_of[LAST - 1])
         add(nc.vector, LAST, slice(1, 2), slice(0, WIDTH))
-        score_narrow(group_of[TURNED])
+        score_narrow(group_of[LAST - 1])
         quantise(group_of[LAST])
         score_last(group_of[LAST])

@@ -35,7 +35,7 @@ STAGED_BUFS = 8
 TERM_BUFS = 6
 GATHERS = [(0, 2), (2, 4), (6, 4), (10, 2), (12, 2), (14, 2)]
 WORDS_AFTER = {2: 1, 3: 6, 4: 8, 5: 10}
-SPLIT = {6: 352}
+LAST_SCALES_AFTER = 7
 
 RAW = PACK * R * 4
 SLOT = 3 * WIDTH * 4
@@ -156,8 +156,8 @@ def tile_list_ckg_bias_kernel(
         v_words = held([P, T], I32, "v_words", "v2_words")
         nc.sync.dma_start(v_words[:], tab_words[0].rearrange("p t i -> p (t i)").bitcast(I32))
         part_v2(0)
-        g_rows = held([P, J], U8, "g_rows", "g2_pairs0")
-        nc.vector.tensor_copy(g_rows[:], v_rows[:].bitcast(U8).indirect(list1[:]))
+        g_rows = held([P, J - EARLY], U8, "g_rows", "g2_pairs0")
+        nc.vector.tensor_copy(g_rows[:], v_rows[:].bitcast(U8).indirect(list1[:, 0 : (J - EARLY) // 16]))
         part_v2(1)
 
         we_bf = [held([P, PACK * R], BF16, "we_bf0"), placed([P, PACK * R], BF16, "we_bf1", WEI_BF_AT)]
@@ -180,7 +180,7 @@ def tile_list_ckg_bias_kernel(
         g_late = placed([P, (J - EARLY) // 4], I32, "g_late", G_PLANES_AT)
         nc.gpsimd.memset(g_late[:], 0)
         for s in range(4):
-            nc.sync.dma_start(g_late[s:P:32, :], g_rows[32 + 4 * s : 96 : 16, EARLY:J].bitcast(I32))
+            nc.sync.dma_start(g_late[s:P:32, 0 : (J - 2 * EARLY) // 4], g_rows[32 + 4 * s : 96 : 16, EARLY:].bitcast(I32))
 
         def g_scale(i):
             plane, at = (g_early, i * TOK) if i * TOK < EARLY else (g_late, i * TOK - EARLY)
@@ -281,7 +281,7 @@ def tile_list_ckg_bias_kernel(
                     nc.scalar.copy(aer[:], ent[w])
                     ent[w] = aer[:]
                 ent[w] = ent[w].unsqueeze(1).to_broadcast([P, 2, TOK, PACK])
-            if i in WORDS_AFTER.values():
+            if i in WORDS_AFTER.values() or i == LAST_SCALES_AFTER - 2:
                 first = held([P, 2, TOK, PACK], F32, f"first{i}")
             else:
                 first = ring.tile([P, 2, TOK, PACK], F32, name="first", bufs=TERM_BUFS)
@@ -466,8 +466,6 @@ def tile_list_ckg_bias_kernel(
         for i in range(LAST):
             for lo, hi in [(0, 1), (1, 2)] if i == LAST - 1 else [(0, 2)]:
                 multiply(i, lo, hi)
-            if i - 1 in SPLIT:
-                add(nc.vector, i - 1, both, slice(SPLIT[i - 1], WIDTH))
             for g in QUANTISED_AFTER.get(i, []):
                 quantise(g)
                 pending.extend([(g, q) for q in range(GROUPS[g])])
@@ -475,10 +473,17 @@ def tile_list_ckg_bias_kernel(
                 for part in range(2):
                     add_turned(i, part, f"rel{part}")
             if i not in TURNED:
-                add(nc.gpsimd, i, both, slice(0, SPLIT.get(i, WIDTH)))
+                add(nc.gpsimd, i, both, slice(0, WIDTH))
             for c in WORDS_AFTER:
                 if WORDS_AFTER[c] == i - (3 if c == 2 else 2):
                     gather_v(c, f"first{WORDS_AFTER[c]}")
+            if i == LAST_SCALES_AFTER:
+                g_last = held([P, EARLY], U8, "g_last", f"first{i - 2}")
+                nc.vector.tensor_copy(g_last[:], v_rows[:].bitcast(U8).indirect(list1[:, (J - EARLY) // 16 :]))
+                for s in range(4):
+                    nc.sync.dma_start(
+                        g_late[s:P:32, (J - 2 * EARLY) // 4 :], g_last[32 + 4 * s : 96 : 16, :].bitcast(I32)
+                    )
             if i + 2 < N_TILES:
                 products(i + 2)
             if i - TURNED[0] in (0, 1):

from contextlib import ExitStack

import concourse.mybir as mybir
from concourse.masks import make_identity

K, L, R, N, T, J = 512, 1024, 512, 512, 4096, 2048
FLOPS = 2 * J * (2 * K * R + 2 * L * R + 2 * R * N)

F32 = mybir.dt.float32
BF16 = mybir.dt.bfloat16
I32 = mybir.dt.int32
U32 = mybir.dt.uint32
U16 = mybir.dt.uint16
U8 = mybir.dt.uint8
FP8X4 = mybir.dt.float8_e4m3fn_x4
FP4X4 = mybir.dt.float4_e2m1fn_x4
MULT = mybir.AluOpType.mult
ADD = mybir.AluOpType.add
IDENTITY = mybir.ActivationFunctionType.Identity

P = 128
PACK = 4
TOK = 128
WIDTH = TOK * PACK
CHUNK = 512
HALF = J // 2
N_TILES = J // TOK
LAST = N_TILES - 1
GROUPS = [4, 4, 2, 2, 1, 1, 1, 1]
TURNED = (2, LAST - 1)
QUANTISED_AFTER = {5: [0], 9: [1], 11: [2], 13: [3, 4]}
UNSIGNED = 4
REL_AHEAD = 3
STAGED_BUFS = 8
TERM_BUFS = 6
GATHERS = [(0, 2), (2, 4), (6, 4), (10, 2), (12, 2), (14, 2)]
WORDS_AFTER = {2: 1, 3: 6, 4: 8, 5: 10}
LAST_SCALES_AFTER = 7

RAW = PACK * R * 4
SLOT = 3 * WIDTH * 4
EARLY = 512
WEI_AT = 0
WR_ROWS_AT = WEI_AT
RELATION_AT = WEI_AT
WEI_BF_AT = RELATION_AT + 3 * SLOT - RAW // 4
WER_AT = RELATION_AT + (REL_AHEAD + 1) * SLOT
G_PLANES_AT = WER_AT
G2_LATE_AT = G_PLANES_AT + J - EARLY
N_PLANE_AT = G2_LATE_AT + 2 * (J - EARLY)
IDENTITY_AT = N_PLANE_AT + 2 * N


def tile_list_ckg_bias_kernel(
    tc, tab_words, tab_scales, tab2_words, tab2_scales, wer, wei, wrr_words, wrr_scales, wri_words, wri_scales,
    nr_words, nr_scales, ni_words, ni_scales, b, offs, offs2, out,
):
    nc = tc.nc
    with ExitStack() as ctx:
        keep = ctx.enter_context(tc.tile_pool(name="keep", bufs=1))
        shared = ctx.enter_context(tc.tile_pool(name="shared", bufs=1))
        ring = ctx.enter_context(tc.tile_pool(name="ring", bufs=3))
        psum = ctx.enter_context(tc.psum_pool(name="psum", bufs=1))

        def held(shape, dtype, name, tag=None):
            return keep.tile(shape, dtype, name=name, tag=tag or name, align_bytes=64)

        def placed(shape, dtype, name, offset):
            return shared.tile(shape, dtype, name=name, align_bytes=64, offset=offset)

        def entries(lst, c, n):
            return lst[:, c * (n // 16) : (c + 1) * (n // 16)]

        list1 = keep.tile([P, J // 16], U16, name="list1")
        list2 = keep.tile([P, J // 16], U16, name="list2")
        v2_rows = held([P, T // 4], I32, "v2_rows")
        v_rows = held([P, T // 4], I32, "v_rows")
        wr_rows = placed([P, 2, R // 4], I32, "wr_rows", WR_ROWS_AT)
        wr_plane = held([P, 4 * R // 4], I32, "wr_plane")
        nc.gpsimd.memset(v_rows[:], 0)
        nc.vector.memset(v2_rows[0:96, :], 0)
        nc.vector.memset(wr_rows[0:96, :, :], 0)
        nc.vector.memset(wr_plane[:], 0)

        nc.sync.dma_start(list2[:], offs2)
        nc.sync.dma_start(v2_rows[96:P, :], tab2_scales.rearrange("a g t -> g a t").bitcast(I32))
        for w, src in enumerate((wrr_scales, wri_scales)):
            for a in range(2):
                nc.scalar.dma_start(
                    wr_rows[96 + a : P : 2, w, :], src[a].rearrange("(q s) c -> s q c", s=4).bitcast(I32)
                )
        v2_words = held([P, T], I32, "v2_words")
        nc.sync.dma_start(v2_words[:], tab2_words[0].rearrange("p t i -> p (t i)").bitcast(I32))
        wr_raw = [held([P, 2, R], I32, f"wr_raw{w}") for w in range(2)]
        for w, src in enumerate((wrr_words, wri_words)):
            nc.sync.dma_start(wr_raw[w][:], src.rearrange("a p r i -> p a (r i)").bitcast(I32))
        we_raw = [placed([P, PACK, R], F32, "wer_raw", WER_AT)]
        nc.sync.dma_start(we_raw[0][:], wer.rearrange("(p i) r -> p i r", i=PACK))
        nc.sync.dma_start(list1[:], offs)
        nc.scalar.dma_start(v_rows[32:96:4, :], tab_scales[0].bitcast(I32))

        wr_rows_t = held([P, 2, PACK, P], U8, "wr_rows_t")
        nc.gpsimd.tensor_copy(
            wr_rows_t[:],
            wr_rows[:].rearrange("p w c -> p (w c)").bitcast(U8).rearrange("p (w m t) -> p w t m", w=2, t=PACK),
        )
        for s in range(4):
            nc.sync.dma_start(
                wr_plane[s:P:32, :],
                wr_rows_t[96 + 8 * s : 96 + 8 * s + 8, :, :, :].rearrange("p w t m -> p (w t m)").bitcast(I32),
            )
        we_raw.append(placed([P, PACK, R], F32, "wei_raw", WEI_AT))
        nc.sync.dma_start(we_raw[1][:], wei.rearrange("(p i) r -> p i r", i=PACK))
        g2_early = held([P, 2 * EARLY // 4], I32, "g2_early")
        nc.gpsimd.memset(g2_early[:], 0)
        g_early = held([P, EARLY // 4], I32, "g_early")
        nc.gpsimd.memset(g_early[:], 0)
        wr_words = held([P, 2, 2, PACK, P], U32, "wr_words")
        for w in range(2):
            nc.scalar.copy(
                wr_words[:, w, :, :, :].rearrange("p a t (x y) -> p a x t y", y=PACK),
                wr_raw[w][:].bitcast(U32).rearrange("p a (x y t) -> p a x t y", y=PACK, t=PACK),
            )
        wr_scale = wr_plane[:].bitcast(U8).rearrange("p (a w t m) -> p a w t m", a=2, w=2, t=PACK)

        g2_rows = held([P, J], U8, "g2_rows")
        nc.vector.tensor_copy(g2_rows[:], v2_rows[:].bitcast(U8).indirect(list2[:]))
        for q in range(4):
            nc.sync.dma_start(
                g2_early[32 * q : 32 * q + 4, :], g2_rows[96 + 8 * q : 96 + 8 * q + 8, 0:EARLY].bitcast(I32)
            )

        g_words = {}

        def gather_v(c, tag=None):
            at, tiles = GATHERS[c]
            if c == 0:
                words = placed([P, tiles * TOK], U32, "g_words0", RELATION_AT + REL_AHEAD * SLOT + RAW // 4)
            else:
                words = held([P, tiles * TOK], U32, f"g_words{c}", tag)
            offsets = list1[:, at * TOK // 16 : (at + tiles) * TOK // 16]
            nc.vector.tensor_copy(words[:], v_words[:].bitcast(U32).indirect(offsets))
            for u in range(tiles):
                g_words[at + u] = words[:, u * TOK : (u + 1) * TOK]

        g2_pairs = [held([P, HALF], U32, f"g2_pairs{h}") for h in range(2)]
        g2_words = [held([P, 2, 2 * HALF], U8, f"g2_words{h}") for h in range(2)]

        def part_v2(h):
            nc.vector.tensor_copy(
                g2_words[h][:].bitcast(U16), g2_pairs[h][:].bitcast(U16).rearrange("p (n d) -> p d n", d=2)
            )

        for h in range(2):
            nc.vector.tensor_copy(g2_pairs[h][:], v2_words[:].bitcast(U32).indirect(entries(list2, h, HALF)))
        v_words = held([P, T], I32, "v_words", "v2_words")
        nc.sync.dma_start(v_words[:], tab_words[0].rearrange("p t i -> p (t i)").bitcast(I32))
        part_v2(0)
        g_rows = held([P, J - EARLY], U8, "g_rows", "g2_pairs0")
        nc.vector.tensor_copy(g_rows[:], v_rows[:].bitcast(U8).indirect(list1[:, 0 : (J - EARLY) // 16]))
        part_v2(1)

        we_bf = [held([P, PACK * R], BF16, "we_bf0"), placed([P, PACK * R], BF16, "we_bf1", WEI_BF_AT)]
        we_words = [held([P, R], U32, f"we_words{w}") for w in range(2)]
        we_plane = [held([P, R], U8, f"we_plane{w}") for w in range(2)]
        for w in range(2):
            nc.scalar.copy(
                we_bf[w][:].rearrange("p (t m i) -> p m t i", t=PACK, i=PACK),
                we_raw[w][:].rearrange("p i (m t) -> p m t i", t=PACK),
            )
            nc.vector.quantize_mx(out=we_words[w][:].bitcast(FP8X4), scales=we_plane[w][:], in_=we_bf[w][:])
        for s in range(4):
            nc.sync.dma_start(g_early[s:P:32, :], g_rows[32 + 4 * s : 96 : 16, 0:EARLY].bitcast(I32))
        g2_late = placed([P, 2 * (J - EARLY) // 4], I32, "g2_late", G2_LATE_AT)
        nc.gpsimd.memset(g2_late[:], 0)
        for q in range(4):
            nc.sync.dma_start(
                g2_late[32 * q : 32 * q + 4, :], g2_rows[96 + 8 * q : 96 + 8 * q + 8, EARLY:J].bitcast(I32)
            )
        g_late = placed([P, (J - EARLY) // 4], I32, "g_late", G_PLANES_AT)
        nc.gpsimd.memset(g_late[:], 0)
        for s in range(4):
            nc.sync.dma_start(g_late[s:P:32, 0 : (J - 2 * EARLY) // 4], g_rows[32 + 4 * s : 96 : 16, EARLY:].bitcast(I32))

        def g_scale(i):
            plane, at = (g_early, i * TOK) if i * TOK < EARLY else (g_late, i * TOK - EARLY)
            return plane[:].bitcast(U8)[:, at : at + TOK]

        def g2_scale(a, i):
            plane, width, at = (g2_early, EARLY, i * TOK) if i * TOK < EARLY else (g2_late, J - EARLY, i * TOK - EARLY)
            return plane[:].bitcast(U8)[:, a * width + at : a * width + at + TOK]

        identity = placed([P, P], F32, "identity", IDENTITY_AT)
        make_identity(nc, identity[:])

        gather_v(0)
        gather_v(1)

        taken = []

        def score_bank(shape):
            taken.append(shape)
            return psum.tile(shape, F32, name=f"score{len(taken) % 2}")

        relation = {}

        def project_relation(i):
            h, u = divmod(i, HALF // TOK)
            relation[i] = placed([P, 3, TOK, PACK], F32, f"relation{i}", RELATION_AT + i % (REL_AHEAD + 1) * SLOT)
            for w in (1, 0):
                if i in (1, 2):
                    bank = psum.tile([P, PACK, TOK], F32, name=f"ent{i % 2}{w}")
                else:
                    bank = psum.tile([P, PACK, TOK], F32, name=f"rel{w}")
                if i in TURNED:
                    for a in range(2):
                        nc.tensor.matmul_mx(
                            out=bank[:].rearrange("p t n -> p (t n)"),
                            lhsT=g2_words[h][:, a, 2 * u * TOK : 2 * (u + 1) * TOK].bitcast(FP4X4),
                            lhsT_scale=g2_scale(a, i),
                            rhs=wr_words[:, w, a, :, :].rearrange("p t m -> p (t m)").bitcast(FP8X4),
                            rhs_scale=wr_scale[:, a, w, :, :].rearrange("p t m -> p (t m)"),
                            start=(a == 0),
                            stop=(a == 1),
                        )
                    nc.scalar.copy(
                        relation[i][:, 1 + w, :, :].rearrange("p n t -> p (n t)"), bank[:].rearrange("p t n -> p (t n)")
                    )
                    continue
                for t in range(PACK):
                    for a in range(2):
                        nc.tensor.matmul_mx(
                            out=bank[:, t, :],
                            lhsT=wr_words[:, w, a, t, :].bitcast(FP8X4),
                            lhsT_scale=wr_scale[:, a, w, t, :],
                            rhs=g2_words[h][:, a, 2 * u * TOK : 2 * (u + 1) * TOK].bitcast(FP4X4),
                            rhs_scale=g2_scale(a, i),
                            start=(a == 0),
                            stop=(a == 1),
                        )
                nc.scalar.copy(relation[i][:, 1 + w, :, :], bank[:].rearrange("p t n -> p n t"))
            if i >= UNSIGNED:
                nc.scalar.mul(relation[i][:, 0, :, :], relation[i][:, 2, :, :], -1.0)

        terms = {}
        entity = {}

        def products(i):
            ent = {}
            for w in (0, 1) if i < 2 else (1, 0):
                if i == 0:
                    bank = psum.tile([P, PACK, TOK], F32, name=f"score{w}")
                else:
                    bank = psum.tile([P, PACK, TOK], F32, name=f"ent{i % 2}{(w + i // 2) % 2}")
                if i in TURNED:
                    nc.tensor.matmul_mx(
                        out=bank[:].rearrange("p t n -> p (t n)"),
                        lhsT=g_words[i].bitcast(FP8X4),
                        lhsT_scale=g_scale(i),
                        rhs=we_words[w][:].bitcast(FP8X4),
                        rhs_scale=we_plane[w][:],
                        start=True,
                        stop=True,
                    )
                    flat = bank[:].rearrange("p t (x y) -> p (t x) y", y=PACK)
                    ent[w] = flat.unsqueeze(1).to_broadcast([P, 2, TOK, PACK])
                    continue
                for t in range(PACK):
                    nc.tensor.matmul_mx(
                        out=bank[:, t, :],
                        lhsT=we_words[w][:, t * P : (t + 1) * P].bitcast(FP8X4),
                        lhsT_scale=we_plane[w][:, t * P : (t + 1) * P],
                        rhs=g_words[i].bitcast(FP8X4),
                        rhs_scale=g_scale(i),
                        start=True,
                        stop=True,
                    )
                ent[w] = bank[:].rearrange("p t n -> p n t")
                if i == 0 and w == 0:
                    aer = held([P, TOK, PACK], F32, "aer")
                    nc.scalar.copy(aer[:], ent[w])
                    ent[w] = aer[:]
                ent[w] = ent[w].unsqueeze(1).to_broadcast([P, 2, TOK, PACK])
            if i in WORDS_AFTER.values() or i == LAST_SCALES_AFTER - 2:
                first = held([P, 2, TOK, PACK], F32, f"first{i}")
            else:
                first = ring.tile([P, 2, TOK, PACK], F32, name="first", bufs=TERM_BUFS)
            second = ring.tile([P, 2, TOK, PACK], F32, name="second", bufs=TERM_BUFS)
            terms[i] = (first, second)
            entity[i] = ent

        def multiply(i, lo, hi):
            first, second = terms[i]
            (nc.gpsimd if i == 0 else nc.vector).tensor_tensor(first[:, lo:hi], entity[i][0][:, lo:hi], relation[i][:, 1 + lo : 1 + hi, :, :], MULT)
            if i >= UNSIGNED:
                nc.vector.tensor_tensor(second[:, lo:hi], entity[i][1][:, lo:hi], relation[i][:, lo:hi, :, :], MULT)
            else:
                nc.vector.tensor_tensor(second[:, 1], entity[i][1][:, 0], relation[i][:, 1, :, :], MULT)
                nc.vector.scalar_tensor_tensor(second[:, 0], entity[i][1][:, 0], -1.0, relation[i][:, 2, :, :], MULT, MULT)

        starts = [sum(GROUPS[:g]) for g in range(len(GROUPS))]
        group_of = [g for g, n in enumerate(GROUPS) for u in range(n)]
        h_bf = {}
        h_mx = {}

        def sums(i):
            g = group_of[i]
            if g not in h_bf:
                n = min(GROUPS[g], 2)
                h_bf[g] = [
                    ring.tile([P, 2, n, WIDTH], BF16, name="h_bf", bufs=6, align_bytes=64) for half in range(GROUPS[g] // n)
                ]
            u, half = divmod(i - starts[g], len(h_bf[g]))
            return h_bf[g][half][:, :, u, :]

        def add(engine, i, parts, span):
            first, second = terms[i]
            engine.tensor_tensor(
                sums(i)[:, parts, span],
                first[:].rearrange("p w n t -> p w (n t)")[:, parts, span],
                second[:].rearrange("p w n t -> p w (n t)")[:, parts, span],
                ADD,
            )

        def add_turned(i, part, name):
            bank = psum.tile([P, PACK, TOK], F32, name=name)
            for k, term in enumerate(terms[i]):
                columns = term[:, part, :, :].rearrange("p n t -> p (n t)")
                for t in range(PACK):
                    nc.tensor.matmul(
                        bank[:, t, :],
                        lhsT=columns[:, t * P : (t + 1) * P],
                        rhs=identity[:],
                        is_transpose=True,
                        start=(k == 0 and t == 0),
                        stop=(k == 1 and t == PACK - 1),
                    )
            nc.scalar.copy(sums(i)[:, part, :].rearrange("p (n t) -> p n t", t=PACK), bank[:].rearrange("p t n -> p n t"))

        def quantise(g):
            width = GROUPS[g] * TOK
            words = ring.tile([P, 2 * width], U32, name="h_words", align_bytes=64)
            plane = ring.tile([P, 2 * width], U8, name="h_plane", align_bytes=64)
            if starts[g] < LAST:
                for half, tile in enumerate(h_bf[g]):
                    span = slice(half * CHUNK, half * CHUNK + 2 * width // len(h_bf[g]))
                    nc.vector.quantize_mx(
                        out=words[:, span].bitcast(FP8X4),
                        scales=plane[:, span],
                        in_=tile[:].rearrange("p w u x -> p (w u x)"),
                    )
            else:
                for w in range(2):
                    span = slice(w * width, (w + 1) * width)
                    nc.vector.quantize_mx(
                        out=words[:, span].bitcast(FP8X4), scales=plane[:, span], in_=h_bf[g][0][:, w, 0, :]
                    )
            h_mx[g] = (words, plane)

        def score(g, q, bank, half=0):
            for w in range(2):
                one_pass(g, q, w, bank, w == 0, w == 1, half)

        def one_pass(g, q, w, bank, start, stop, half=0):
            width = min(GROUPS[g], 2) * TOK
            span = slice((2 * half + w) * width, (2 * half + w + 1) * width)
            words, plane = h_mx[g]
            nc.tensor.matmul_mx(
                out=bank,
                lhsT=n_words[:, w, q * P // 2 : (q + 1) * P // 2].bitcast(FP4X4),
                lhsT_scale=n_plane[:, w, :].bitcast(U8)[:, q * P : (q + 1) * P],
                rhs=words[:, span].bitcast(FP8X4),
                rhs_scale=plane[:, span],
                start=start,
                stop=stop,
            )

        def score_wide(g, q):
            bank = score_bank([P, CHUNK])
            staged = ring.tile([P, CHUNK], F32, name="staged", bufs=STAGED_BUFS)
            for half in range(2):
                score(g, q, bank[:, half * 2 * TOK : (half + 1) * 2 * TOK], half)
            nc.scalar.activation(
                staged[:].rearrange("p (u h j) -> p u h j", u=2, h=2),
                bank[:].rearrange("p (h u j) -> p u h j", u=2, h=2),
                IDENTITY,
                bias=bias[:, q : q + 1],
            )
            nc.sync.dma_start(out[q * P : (q + 1) * P, starts[g] * TOK : starts[g] * TOK + CHUNK], staged[:])

        def score_pair(g, pair):
            bank = score_bank([P, CHUNK])
            staged = ring.tile([P, CHUNK], F32, name="staged", bufs=STAGED_BUFS)
            for u in range(2):
                score(g, 2 * pair + u, bank[:, u * 2 * TOK : (u + 1) * 2 * TOK])
            for u in range(2):
                span = slice(u * 2 * TOK, (u + 1) * 2 * TOK)
                nc.scalar.activation(staged[:, span], bank[:, span], IDENTITY, bias=bias[:, 2 * pair + u : 2 * pair + u + 1])
            nc.sync.dma_start(
                out[2 * pair * P : 2 * (pair + 1) * P, starts[g] * TOK : (starts[g] + 2) * TOK].rearrange(
                    "(q p) j -> p q j", p=P
                ),
                staged[:].rearrange("p (q j) -> p q j", q=2),
            )

        def score_narrow(g):
            staged = ring.tile([P, CHUNK], F32, name="staged", bufs=STAGED_BUFS)
            for pair in range(2):
                if starts[g] == LAST - 1:
                    bank = psum.tile([P, CHUNK], F32, name=f"ent1{pair}")
                else:
                    bank = score_bank([P, CHUNK])
                for u in range(2):
                    score(g, 2 * pair + u, bank[:, u * TOK : (u + 1) * TOK])
                for u in range(2):
                    q = 2 * pair + u
                    nc.scalar.activation(
                        staged[:, q * TOK : (q + 1) * TOK], bank[:, u * TOK : (u + 1) * TOK], IDENTITY, bias=bias[:, q : q + 1]
                    )
                nc.sync.dma_start(
                    out[2 * pair * P : 2 * (pair + 1) * P, starts[g] * TOK : (starts[g] + 1) * TOK].rearrange(
                        "(q p) j -> p q j", p=P
                    ),
                    staged[:, 2 * pair * TOK : 2 * (pair + 1) * TOK].rearrange("p (q j) -> p q j", q=2),
                )

        n_words = held([P, 2, N // 2], I32, "n_words", "g2_rows")
        for w, src in enumerate((nr_words, ni_words)):
            nc.sync.dma_start(n_words[:, w, :], src[0].bitcast(I32))
        n_plane = placed([P, 2, N // 4], I32, "n_plane", N_PLANE_AT)
        nc.gpsimd.memset(n_plane[:], 0)
        for w, src in enumerate((nr_scales, ni_scales)):
            for q in range(4):
                nc.sync.dma_start(n_plane[32 * q : 32 * q + 4, w, :], src[0, 4 * q : 4 * q + 4, :].bitcast(I32))
        bias = held([P, N // P], F32, "bias", "g2_pairs0")
        with nc.allow_non_contiguous_dma(reason="one bias value to a partition"):
            nc.sync.dma_start(bias[:], b.rearrange("(q p) -> p q", p=P))

        def score_last(g):
            banks = [psum.tile([P, CHUNK], F32, name=name) for name in ("rel0", "rel1", "ent00", "ent01")]
            for q, bank in enumerate(banks):
                one_pass(g, q, 0, bank[:, 0:TOK], True, False)
            for pair in range(2):
                staged = ring.tile([P, CHUNK], F32, name="staged", bufs=STAGED_BUFS)
                by_vector, by_scalar = 2 * pair, 2 * pair + 1
                for q in (by_vector, by_scalar):
                    one_pass(g, q, 1, banks[q][:, 0:TOK], False, True)
                nc.vector.tensor_scalar_add(
                    staged[:, 0:TOK], banks[by_vector][:, 0:TOK], bias[:, by_vector : by_vector + 1]
                )
                nc.scalar.activation(
                    staged[:, TOK : 2 * TOK], banks[by_scalar][:, 0:TOK], IDENTITY, bias=bias[:, by_scalar : by_scalar + 1]
                )
                (nc.sync, nc.scalar)[pair].dma_start(
                    out[2 * pair * P : 2 * (pair + 1) * P, LAST * TOK : J].rearrange("(q p) j -> p q j", p=P),
                    staged[:, 0 : 2 * TOK].rearrange("p (q j) -> p q j", q=2),
                )

        project_relation(0)
        products(0)
        for i in range(1, REL_AHEAD + 1):
            project_relation(i)
        both = slice(0, 2)
        pending = []
        products(1)
        for i in range(LAST):
            for lo, hi in [(0, 1), (1, 2)] if i == LAST - 1 else [(0, 2)]:
                multiply(i, lo, hi)
            for g in QUANTISED_AFTER.get(i, []):
                quantise(g)
                pending.extend([(g, q) for q in range(GROUPS[g])])
            if i == LAST - 1:
                for part in range(2):
                    add_turned(i, part, f"rel{part}")
            if i not in TURNED:
                add(nc.gpsimd, i, both, slice(0, WIDTH))
            for c in WORDS_AFTER:
                if WORDS_AFTER[c] == i - (3 if c == 2 else 2):
                    gather_v(c, f"first{WORDS_AFTER[c]}")
            if i == LAST_SCALES_AFTER:
                g_last = held([P, EARLY], U8, "g_last", f"first{i - 2}")
                nc.vector.tensor_copy(g_last[:], v_rows[:].bitcast(U8).indirect(list1[:, (J - EARLY) // 16 :]))
                for s in range(4):
                    nc.sync.dma_start(
                        g_late[s:P:32, (J - 2 * EARLY) // 4 :], g_last[32 + 4 * s : 96 : 16, :].bitcast(I32)
                    )
            if i + 2 < N_TILES:
                products(i + 2)
            if i - TURNED[0] in (0, 1):
                add_turned(TURNED[0], i - TURNED[0], f"score{i - TURNED[0]}")
            if REL_AHEAD < i + REL_AHEAD < N_TILES:
                project_relation(i + REL_AHEAD)
            take = len(pending) if i == LAST - 1 else min(2 if i >= LAST - 4 else 1, len(pending))
            for g, q in pending[:take]:
                if GROUPS[g] == 4:
                    score_wide(g, q)
                elif GROUPS[g] == 2:
                    score_pair(g, q)
                else:
                    score_narrow(g)
            pending = pending[take:]
        multiply(LAST, 0, 1)
        quantise(group_of[LAST - 2])
        add(nc.gpsimd, LAST, slice(0, 1), slice(0, WIDTH))
        multiply(LAST, 1, 2)
        score_narrow(group_of[LAST - 2])
        quantise(group_of[LAST - 1])
        add(nc.vector, LAST, slice(1, 2), slice(0, WIDTH))
        score_narrow(group_of[LAST - 1])
        quantise(group_of[LAST])
        score_last(group_of[LAST])
